import numpy as np
import ml_dtypes


def mxq(x, axis, fmt="e4m3"):
    dtype, down = {"e4m3": (ml_dtypes.float8_e4m3fn, 7), "e5m2": (ml_dtypes.float8_e5m2, 14)}[fmt]
    v = np.moveaxis(np.asarray(x, np.float32).astype(ml_dtypes.bfloat16).astype(np.float64), axis, -1)
    blocks = v.reshape(v.shape[:-1] + (-1, 32))
    amax = np.abs(blocks).max(-1, keepdims=True)
    byte = np.maximum(np.where(amax > 0, np.frexp(amax)[1] - 1 + 127, 0) - down, 1)
    scale = np.exp2(byte - 127.0)
    codes = (blocks / scale).astype(np.float32).astype(dtype).astype(np.float64)
    return np.moveaxis((codes * scale).reshape(v.shape), -1, axis)


WIDE = False


def mx_kscale(k):
    if not WIDE:
        return np.ones(k)
    levels = np.array([10, -10, 5, -5, 0])
    if k % 512:
        return np.exp2(np.random.permutation(np.resize(levels, k // 32))).repeat(32)
    a = np.empty((k // 512, 16))
    for p in range(k // 512):
        a[p, :8] = np.random.permutation(np.resize(levels, 8))
        for g in range(8):
            far = levels[np.abs(levels - a[p, g]) >= 10]
            a[p, g + 8] = far[np.random.randint(len(far))]
    return np.exp2(a.ravel()).repeat(32)


def f64(x):
    return np.asarray(x).astype(np.float64)


def striped(idx):
    return np.tile(idx.reshape(-1, 16).T, (8, 1)).astype(np.uint16)


def unstriped(offs):
    return offs[:16].T.reshape(-1).astype(np.int64)


def gelu(v):
    return 0.5 * v * (1.0 + np.tanh(np.sqrt(2.0 / np.pi) * (v + 0.044715 * v**3)))


K, T, E, C, H, N = 512, 1024, 16, 128, 512, 128


def by_expert(wq, xq):
    return np.concatenate([wq[e].T @ xq[:, e * C:(e + 1) * C] for e in range(E)], axis=1)


def setup_inputs():
    n = np.random.standard_normal
    s = mx_kscale(K)[:, None]
    u = mx_kscale(H)
    first = np.random.permutation(np.repeat(np.arange(E), T // E))
    second = (first + 1 + np.random.permutation(np.repeat(np.arange(E - 1), -(-T // (E - 1)))[:T])) % E
    while np.bincount(second, minlength=E).max() != T // E:
        load = np.bincount(second, minlength=E); hi, lo = int(load.argmax()), int(load.argmin())
        t = np.flatnonzero((second == hi) & (first != lo))[0]; second[t] = lo
    slot_token = np.empty(E * C, np.int64); pos = np.empty((2, T), np.int64); fill = np.zeros(E, np.int64)
    place = np.stack([np.random.permutation(C) for _ in range(E)])
    for r, deal in enumerate((first, second)):
        for t in np.random.permutation(T):
            e = deal[t]; j = e * C + place[e, fill[e]]; fill[e] += 1; slot_token[j] = t; pos[r, t] = j
    g = np.random.uniform(0.2, 0.8, T)
    return {
        "xT": (n((K, T)) * s).astype(np.float32),
        "w1": (n((E, K, H)) / np.sqrt(K) / s[None] * u[None, None, :]).astype(np.float32),
        "w2": (n((E, H, N)) / np.sqrt(H) / u[None, :, None]).astype(np.float32),
        "gate": np.stack([np.tile(g, (N, 1)), np.tile(1.0 - g, (N, 1))]).astype(np.float32),
        "offs": striped(slot_token),
        "pos1": striped(pos[0]),
        "pos2": striped(pos[1]),
    }


def reference(xT, w1, w2, gate, offs, pos1, pos2):
    idx = unstriped(offs)
    xq = mxq(f64(xT)[:, idx], 0, "e4m3")
    h = gelu(by_expert(mxq(f64(w1), 1, "e4m3"), xq))
    y = by_expert(mxq(f64(w2), 1, "e4m3"), mxq(h, 0, "e4m3"))
    return f64(gate[0]) * y[:, unstriped(pos1)] + f64(gate[1]) * y[:, unstriped(pos2)]

@@ -1,0 +1,304 @@
+from contextlib import ExitStack
+
+import concourse.mybir as mybir
+
+F32 = mybir.dt.float32
+BF16 = mybir.dt.bfloat16
+U32 = mybir.dt.uint32
+U16 = mybir.dt.uint16
+U8 = mybir.dt.uint8
+FP8X4 = mybir.dt.float8_e4m3fn_x4
+ACT = mybir.ActivationFunctionType
+ALU = mybir.AluOpType
+
+P = 128
+K, T, E, C, H, N = 512, 1024, 16, 128, 512, 128
+S = E * C
+FLOPS = 2 * S * K * H + 2 * S * H * N
+
+CHUNK = 512
+EPC = CHUNK // C
+NCHUNK = S // CHUNK
+RAW_BUFS = 9
+M_VEC = [16,16,16,16,16,16,16,16,32,48,80,80,80,80,80,80]
+M_GPS = [0,0,0,0,0,0,0,0,0,0,0,0,0,0,0,0]
+X_ENG = ["S","V","V","V"]
+W2_ENG = ["S","S","S","S","S","S","S","S","S","S","S","S","S","S","S","S"]
+Y_ENG = ["S","S","S","S","S","S","S","S"]
+G_PLANE = [0,0,0,0,0,0,0,0,0,0,0,0,0,0,0,0]
+HEAD = ["p0","p1","p2","p3"]
+W2_LATE = False
+PE_ADD = [0,0,0,0]
+GATHER_LEAD = 2
+CTS = [256,256,256,256]
+
+
+def tile_routed_moe_kernel(tc, xT, w1, w2, gate, offs, pos1, pos2, out):
+    nc = tc.nc
+    with ExitStack() as ctx:
+        lists = ctx.enter_context(tc.tile_pool(name="lists", bufs=1))
+        held = ctx.enter_context(tc.tile_pool(name="held", bufs=1))
+        raw_pool = ctx.enter_context(tc.tile_pool(name="raw_pool", bufs=RAW_BUFS))
+        g4_pool = ctx.enter_context(tc.tile_pool(name="g4_pool", bufs=2))
+        xg_pool = ctx.enter_context(tc.tile_pool(name="xg_pool", bufs=2))
+        w1g_pool = ctx.enter_context(tc.tile_pool(name="w1g_pool", bufs=4))
+        w1q_pool = ctx.enter_context(tc.tile_pool(name="w1q_pool", bufs=4))
+        w2g_pool = ctx.enter_context(tc.tile_pool(name="w2g_pool", bufs=2))
+        h_pool = ctx.enter_context(tc.tile_pool(name="h_pool", bufs=4))
+        comb = ctx.enter_context(tc.tile_pool(name="comb", bufs=3))
+        ps1_pool = ctx.enter_context(tc.psum_pool(name="ps1_pool", bufs=4))
+        ps2_pool = ctx.enter_context(tc.psum_pool(name="ps2_pool", bufs=3))
+
+        warm = held.tile([P, 1], F32, name="warm")
+        warm2 = held.tile([P, 1], F32, name="warm2")
+        nc.vector.memset(warm[:], 0.0)
+        nc.scalar.activation(out=warm2[:], in_=warm[:], func=ACT.Gelu_apprx_tanh)
+
+        offs_sb = lists.tile([P, S // 16], U16, name="offs_sb")
+        nc.sync.dma_start(offs_sb[:], offs)
+        pos1_sb = lists.tile([P, T // 16], U16, name="pos1_sb")
+        pos2_sb = lists.tile([P, T // 16], U16, name="pos2_sb")
+
+        x_view = xT.rearrange("(p t) n -> p t n", t=4)
+        planes = []
+        for t in range(4):
+            plane = held.tile([P, T], F32, name="plane%d" % t)
+            planes.append(plane)
+
+        y_all = held.tile([P, S], F32, name="y_all")
+
+        raw = {}
+        w1g, w1c, w1s = {}, {}, {}
+        w2g, w2c, w2s = {}, {}, {}
+        g4, xg, xc, xs = {}, {}, {}, {}
+        ps1, ps2 = {}, {}
+        hg, hc, hs = {}, {}, {}
+
+        def copy_on(eng, dst, src):
+            if eng == "V":
+                nc.vector.tensor_copy(out=dst, in_=src)
+            elif eng == "S":
+                nc.scalar.copy(out=dst, in_=src)
+            else:
+                nc.gpsimd.tensor_scalar(out=dst, in0=src, scalar1=1.0, scalar2=0.0, op0=ALU.mult, op1=ALU.add)
+
+        order = []
+        for item in HEAD:
+            order.append((item[0:2], int(item[2:])) if item[0] == "w" else ("plane", int(item[1:])))
+        for e in range(E):
+            if e % EPC == 0 and (e // EPC < NCHUNK - 1 or not W2_LATE):
+                if ("w2", e // EPC) not in order:
+                    if e == 0 and ("w1", 0) not in order:
+                        order.append(("w1", 0))
+                    order.append(("w2", e // EPC))
+            if ("w1", e) not in order:
+                order.append(("w1", e))
+        order.append(("pos", 0))
+        if W2_LATE:
+            order.append(("w2", NCHUNK - 1))
+        order.append(("gate", 0))
+        state = {"next": 0, "live": 0}
+
+        def issue_loads():
+            while state["next"] < len(order) and state["live"] < RAW_BUFS:
+                kind, idx = order[state["next"]]
+                state["next"] += 1
+                if kind == "plane":
+                    nc.sync.dma_start(planes[idx][:], x_view[:, idx, :])
+                    continue
+                if kind == "pos":
+                    nc.sync.dma_start(pos1_sb[:], pos1)
+                    nc.sync.dma_start(pos2_sb[:], pos2)
+                    continue
+                state["live"] += 1
+                if kind == "w1":
+                    tl = raw_pool.tile([P, 4, H], F32, name="raw")
+                    nc.sync.dma_start(tl[:], w1[idx].rearrange("(p j) c -> p j c", j=4))
+                elif kind == "w2":
+                    tl = raw_pool.tile([P, EPC, 4 * N], F32, name="raw")
+                    nc.sync.dma_start(tl[:], w2[idx * EPC : (idx + 1) * EPC].rearrange("e (p j) n -> p e (j n)", j=4))
+                else:
+                    tl = raw_pool.tile([P, 2, T], F32, name="raw")
+                    nc.sync.dma_start(tl[:], gate.rearrange("r n t -> n r t"))
+                raw[(kind, idx)] = tl
+
+        def consumed():
+            state["live"] -= 1
+
+        def gather(q, t):
+            if t == 0:
+                g4[q] = g4_pool.tile([P, 4, CHUNK], F32, name="g4")
+            nc.vector.tensor_copy(
+                g4[q][:, t, :], planes[t][:].indirect(offs_sb[:, q * (CHUNK // 16) : (q + 1) * (CHUNK // 16)])
+            )
+
+        def x_interleave(q):
+            xg[q] = xg_pool.tile([P, CHUNK, 4], BF16, name="xg", align_bytes=64)
+            eng = X_ENG[q]
+            if eng == "G":
+                for a in range(EPC):
+                    sl = slice(a * C, (a + 1) * C)
+                    copy_on("G", xg[q][:, sl, :], g4[q][:, :, sl].rearrange("p t n -> p n t"))
+            else:
+                copy_on(
+                    eng,
+                    xg[q][:].rearrange("p (c i) t -> p c t i", i=4),
+                    g4[q][:].rearrange("p t (c i) -> p c t i", i=4),
+                )
+
+        def x_quantize(q):
+            xc[q] = held.tile([P, CHUNK], U32, name="xc%d" % q, align_bytes=64)
+            xs[q] = held.tile([P, CHUNK], U8, name="xs%d" % q, align_bytes=64)
+            nc.vector.quantize_mx(
+                out=xc[q][:].bitcast(FP8X4), scales=xs[q][:], in_=xg[q][:].rearrange("p n t -> p (n t)")
+            )
+
+        def w1_interleave(e):
+            w1g[e] = w1g_pool.tile([P, 4 * H], BF16, name="w1g", align_bytes=64)
+            dst = w1g[e][:].rearrange("p (t m j) -> p m j t", t=4, j=4)
+            src = raw[("w1", e)][:].rearrange("p j (m t) -> p m j t", t=4)
+            mv = M_VEC[e]
+            tm = 3 if G_PLANE[e] else 4
+            if G_PLANE[e]:
+                copy_on(
+                    "G",
+                    w1g[e][:, 3 * H : 4 * H].rearrange("p (m j) -> p m j", j=4),
+                    raw[("w1", e)][:].rearrange("p j (m t) -> p t m j", t=4)[:, 3, :, :],
+                )
+            if mv > 0:
+                copy_on("V", dst[:, 0:mv, :, 0:tm], src[:, 0:mv, :, 0:tm])
+            if mv < P:
+                copy_on("S", dst[:, mv:P, :, 0:tm], src[:, mv:P, :, 0:tm])
+            consumed()
+
+        def w1_quantize(e):
+            w1c[e] = w1q_pool.tile([P, H], U32, name="w1c", align_bytes=64)
+            w1s[e] = w1q_pool.tile([P, H], U8, name="w1s", align_bytes=64)
+            nc.vector.quantize_mx(out=w1c[e][:].bitcast(FP8X4), scales=w1s[e][:], in_=w1g[e][:])
+
+        def w2_interleave(e):
+            q, a = e // EPC, e % EPC
+            if a == 0:
+                w2g[q] = w2g_pool.tile([P, EPC, N, 4], BF16, name="w2g", align_bytes=64)
+            eng = W2_ENG[e]
+            if eng == "G":
+                copy_on("G", w2g[q][:, a, :, :], raw[("w2", q)][:, a, :].rearrange("p (j n) -> p n j", j=4))
+            else:
+                copy_on(
+                    eng,
+                    w2g[q][:, a, :, :].rearrange("p (c i) j -> p c j i", i=4),
+                    raw[("w2", q)][:, a, :].rearrange("p (j c i) -> p c j i", j=4, i=4),
+                )
+            if a == EPC - 1:
+                consumed()
+
+        def w2_quantize(q):
+            w2c[q] = held.tile([P, EPC * N], U32, name="w2c%d" % q, align_bytes=64)
+            w2s[q] = held.tile([P, EPC * N], U8, name="w2s%d" % q, align_bytes=64)
+            nc.vector.quantize_mx(
+                out=w2c[q][:].bitcast(FP8X4), scales=w2s[q][:], in_=w2g[q][:].rearrange("p e n j -> p (e n j)")
+            )
+
+        def layer1(e):
+            q, a = e // EPC, e % EPC
+            ps1[e] = ps1_pool.tile([P, 4, C], F32, name="ps1")
+            for t in range(4):
+                nc.tensor.matmul_mx(
+                    out=ps1[e][:, t, :],
+                    lhsT=w1c[e][:, t * P : (t + 1) * P].bitcast(FP8X4),
+                    lhsT_scale=w1s[e][:, t * P : (t + 1) * P],
+                    rhs=xc[q][:, a * C : (a + 1) * C].bitcast(FP8X4),
+                    rhs_scale=xs[q][:, a * C : (a + 1) * C],
+                    start=True,
+                    stop=True,
+                )
+
+        def gelu(e):
+            k, a = e // 2, e % 2
+            if a == 0:
+                hg[k] = h_pool.tile([P, 2, C, 4], BF16, name="hg", align_bytes=64)
+            nc.scalar.activation(
+                out=hg[k][:, a, :, :], in_=ps1[e][:].rearrange("p t n -> p n t"), func=ACT.Gelu_apprx_tanh
+            )
+
+        def h_quantize(k):
+            hc[k] = h_pool.tile([P, 2 * C], U32, name="hc", align_bytes=64)
+            hs[k] = h_pool.tile([P, 2 * C], U8, name="hs", align_bytes=64)
+            nc.vector.quantize_mx(
+                out=hc[k][:].bitcast(FP8X4), scales=hs[k][:], in_=hg[k][:].rearrange("p a n t -> p (a n t)")
+            )
+
+        def layer2(k):
+            ps2[k] = ps2_pool.tile([P, 2 * C], F32, name="ps2")
+            for b in range(2):
+                e = 2 * k + b
+                q, a = e // EPC, e % EPC
+                nc.tensor.matmul_mx(
+                    out=ps2[k][:, b * C : (b + 1) * C],
+                    lhsT=w2c[q][:, a * N : (a + 1) * N].bitcast(FP8X4),
+                    lhsT_scale=w2s[q][:, a * N : (a + 1) * N],
+                    rhs=hc[k][:, b * C : (b + 1) * C].bitcast(FP8X4),
+                    rhs_scale=hs[k][:, b * C : (b + 1) * C],
+                    start=True,
+                    stop=True,
+                )
+            copy_on(Y_ENG[k], y_all[:, 2 * k * C : (2 * k + 2) * C], ps2[k][:])
+
+        issue_loads()
+        later = [(q, t) for q in range(1, NCHUNK) for t in range(4)]
+        for t in range(4):
+            gather(0, t)
+        x_interleave(0)
+        for g in range(GATHER_LEAD):
+            gather(later[g][0], later[g][1])
+        x_quantize(0)
+
+        LAST = NCHUNK - 1
+        for i in range(E + 5):
+            if 0 <= i - 2 < E:
+                gelu(i - 2)
+            if i < E:
+                w1_interleave(i)
+            for q in range(1, NCHUNK):
+                if i == EPC * q - GATHER_LEAD + 1:
+                    x_quantize(q)
+            if 0 <= i - 1 < E:
+                w1_quantize(i - 1)
+                layer1(i - 1)
+            if i + GATHER_LEAD < len(later):
+                q, t = later[i + GATHER_LEAD]
+                gather(q, t)
+                if t == 3:
+                    x_interleave(q)
+            if i < EPC * (LAST if W2_LATE else NCHUNK) and i % EPC < 2:
+                w2_interleave(EPC * (i // EPC) + 2 * (i % EPC))
+                w2_interleave(EPC * (i // EPC) + 2 * (i % EPC) + 1)
+            if i < EPC * (LAST if W2_LATE else NCHUNK) and i % EPC == 2:
+                w2_quantize(i // EPC)
+            if i == E and W2_LATE:
+                for a in range(EPC):
+                    w2_interleave(EPC * LAST + a)
+                w2_quantize(LAST)
+            if i >= 4 and i % 2 == 0 and (i - 4) // 2 < E // 2:
+                k = (i - 4) // 2
+                h_quantize(k)
+                layer2(k)
+            issue_loads()
+
+        gt = raw[("gate", 0)]
+        prods = {}
+        starts = [sum(CTS[:c]) for c in range(len(CTS))]
+        for c in range(len(CTS) + 1):
+            if c < len(CTS):
+                cols = slice(starts[c], starts[c] + CTS[c])
+                lcols = slice(starts[c] // 16, (starts[c] + CTS[c]) // 16)
+                pa = comb.tile([P, CTS[c]], F32, name="pa")
+                nc.vector.tensor_tensor(pa[:], y_all[:].indirect(pos1_sb[:, lcols]), gt[:, 0, cols], ALU.mult)
+                pb = comb.tile([P, CTS[c]], F32, name="pb")
+                nc.vector.tensor_tensor(pb[:], y_all[:].indirect(pos2_sb[:, lcols]), gt[:, 1, cols], ALU.mult)
+                prods[c] = (pa, pb)
+            if c >= 1:
+                pa, pb = prods[c - 1]
+                res = comb.tile([P, CTS[c - 1]], F32, name="res")
+                nc.vector.tensor_tensor(res[:], pa[:], pb[:], ALU.add)
+                nc.sync.dma_start(out[:, starts[c - 1] : starts[c - 1] + CTS[c - 1]], res[:])

@@ -20,11 +20,11 @@ CHUNK = 512
 EPC = CHUNK // C
 NCHUNK = S // CHUNK
 RAW_BUFS = 9
-M_VEC = [16,16,16,16,16,16,16,16,32,48,80,80,80,80,80,80]
+M_VEC = [0,0,0,0,0,0,0,0,0,0,0,0,0,0,0,0]
 M_GPS = [0,0,0,0,0,0,0,0,0,0,0,0,0,0,0,0]
-X_ENG = ["S","V","V","V"]
-W2_ENG = ["S","S","S","S","S","S","S","S","S","S","S","S","S","S","S","S"]
-Y_ENG = ["S","S","S","S","S","S","S","S"]
+X_ENG = ["V","V","V","V"]
+W2_ENG = ["V","V","V","V","V","V","V","V","V","V","V","V","V","V","V","V"]
+Y_ENG = ["V","V","V","V","V","V","V","V"]
 G_PLANE = [0,0,0,0,0,0,0,0,0,0,0,0,0,0,0,0]
 HEAD = ["p0","p1","p2","p3"]
 W2_LATE = False
@@ -139,6 +139,8 @@ def tile_routed_moe_kernel(tc, xT, w1, w2, gate, offs, pos1, pos2, out):
                 for a in range(EPC):
                     sl = slice(a * C, (a + 1) * C)
                     copy_on("G", xg[q][:, sl, :], g4[q][:, :, sl].rearrange("p t n -> p n t"))
+            elif eng == "V":
+                copy_on("V", xg[q][:], g4[q][:].rearrange("p t n -> p n t"))
             else:
                 copy_on(
                     eng,
@@ -181,7 +183,10 @@ def tile_routed_moe_kernel(tc, xT, w1, w2, gate, offs, pos1, pos2, out):
             if a == 0:
                 w2g[q] = w2g_pool.tile([P, EPC, N, 4], BF16, name="w2g", align_bytes=64)
             eng = W2_ENG[e]
-            if eng == "G":
+            if eng == "V":
+                if a == 0:
+                    copy_on("V", w2g[q][:], raw[("w2", q)][:].rearrange("p e (j n) -> p e n j", j=4))
+            elif eng == "G":
                 copy_on("G", w2g[q][:, a, :, :], raw[("w2", q)][:, a, :].rearrange("p (j n) -> p n j", j=4))
             else:
                 copy_on(

@@ -16,21 +16,18 @@ K, T, E, C, H, N = 512, 1024, 16, 128, 512, 128
 S = E * C
 FLOPS = 2 * S * K * H + 2 * S * H * N
 
-CHUNK = 512
-EPC = CHUNK // C
-NCHUNK = S // CHUNK
-RAW_BUFS = 9
-M_VEC = [0,0,0,0,0,0,0,0,0,0,0,0,0,0,0,0]
-M_GPS = [0,0,0,0,0,0,0,0,0,0,0,0,0,0,0,0]
-X_ENG = ["V","V","V","V"]
-W2_ENG = ["V","V","V","V","V","V","V","V","V","V","V","V","V","V","V","V"]
-Y_ENG = ["V","V","V","V","V","V","V","V"]
+CH = 256
+EPCH = CH // C
+NCH = S // CH
+WG = 4
+M_VEC = [56,56,56,56,56,56,56,56,88,88,88,88,88,88,88,88]
 G_PLANE = [0,0,0,0,0,0,0,0,0,0,0,0,0,0,0,0]
-HEAD = ["p0","p1","p2","p3"]
-W2_LATE = False
-PE_ADD = [0,0,0,0]
-GATHER_LEAD = 2
+X_ENG = "S"
+W2_ENG = "S"
+Y_ENG = "S"
 CTS = [256,256,256,256]
+LC, QL, GL, HL, XLEAD, W2LEAD = 2, 1, 2, 4, 4, 0
+RAW_BUFS = 9
 
 
 def tile_routed_moe_kernel(tc, xT, w1, w2, gate, offs, pos1, pos2, out):
@@ -40,8 +37,9 @@ def tile_routed_moe_kernel(tc, xT, w1, w2, gate, offs, pos1, pos2, out):
         held = ctx.enter_context(tc.tile_pool(name="held", bufs=1))
         raw_pool = ctx.enter_context(tc.tile_pool(name="raw_pool", bufs=RAW_BUFS))
         g4_pool = ctx.enter_context(tc.tile_pool(name="g4_pool", bufs=2))
-        xg_pool = ctx.enter_context(tc.tile_pool(name="xg_pool", bufs=2))
-        w1g_pool = ctx.enter_context(tc.tile_pool(name="w1g_pool", bufs=4))
+        xg_pool = ctx.enter_context(tc.tile_pool(name="xg_pool", bufs=1))
+        xc_pool = ctx.enter_context(tc.tile_pool(name="xc_pool", bufs=2))
+        w1g_pool = ctx.enter_context(tc.tile_pool(name="w1g_pool", bufs=6))
         w1q_pool = ctx.enter_context(tc.tile_pool(name="w1q_pool", bufs=4))
         w2g_pool = ctx.enter_context(tc.tile_pool(name="w2g_pool", bufs=2))
         h_pool = ctx.enter_context(tc.tile_pool(name="h_pool", bufs=4))
@@ -63,6 +61,7 @@ def tile_routed_moe_kernel(tc, xT, w1, w2, gate, offs, pos1, pos2, out):
         planes = []
         for t in range(4):
             plane = held.tile([P, T], F32, name="plane%d" % t)
+            nc.sync.dma_start(plane[:], x_view[:, t, :])
             planes.append(plane)
 
         y_all = held.tile([P, S], F32, name="y_all")
@@ -83,19 +82,17 @@ def tile_routed_moe_kernel(tc, xT, w1, w2, gate, offs, pos1, pos2, out):
                 nc.gpsimd.tensor_scalar(out=dst, in0=src, scalar1=1.0, scalar2=0.0, op0=ALU.mult, op1=ALU.add)
 
         order = []
-        for item in HEAD:
-            order.append((item[0:2], int(item[2:])) if item[0] == "w" else ("plane", int(item[1:])))
         for e in range(E):
-            if e % EPC == 0 and (e // EPC < NCHUNK - 1 or not W2_LATE):
-                if ("w2", e // EPC) not in order:
-                    if e == 0 and ("w1", 0) not in order:
-                        order.append(("w1", 0))
-                    order.append(("w2", e // EPC))
-            if ("w1", e) not in order:
-                order.append(("w1", e))
+            if e == 0:
+                order.append(("w1", 0))
+                order.append(("w2", 0))
+                continue
+            if (e + W2LEAD) % WG == 0 and (e + W2LEAD) // WG < E // WG and not (False and (e + W2LEAD) // WG == E // WG - 1):
+                order.append(("w2", (e + W2LEAD) // WG))
+            order.append(("w1", e))
         order.append(("pos", 0))
-        if W2_LATE:
-            order.append(("w2", NCHUNK - 1))
+        if False:
+            order.append(("w2", E // WG - 1))
         order.append(("gate", 0))
         state = {"next": 0, "live": 0}
 
@@ -103,9 +100,6 @@ def tile_routed_moe_kernel(tc, xT, w1, w2, gate, offs, pos1, pos2, out):
             while state["next"] < len(order) and state["live"] < RAW_BUFS:
                 kind, idx = order[state["next"]]
                 state["next"] += 1
-                if kind == "plane":
-                    nc.sync.dma_start(planes[idx][:], x_view[:, idx, :])
-                    continue
                 if kind == "pos":
                     nc.sync.dma_start(pos1_sb[:], pos1)
                     nc.sync.dma_start(pos2_sb[:], pos2)
@@ -115,8 +109,8 @@ def tile_routed_moe_kernel(tc, xT, w1, w2, gate, offs, pos1, pos2, out):
                     tl = raw_pool.tile([P, 4, H], F32, name="raw")
                     nc.sync.dma_start(tl[:], w1[idx].rearrange("(p j) c -> p j c", j=4))
                 elif kind == "w2":
-                    tl = raw_pool.tile([P, EPC, 4 * N], F32, name="raw")
-                    nc.sync.dma_start(tl[:], w2[idx * EPC : (idx + 1) * EPC].rearrange("e (p j) n -> p e (j n)", j=4))
+                    tl = raw_pool.tile([P, WG, 4 * N], F32, name="raw")
+                    nc.sync.dma_start(tl[:], w2[idx * WG : (idx + 1) * WG].rearrange("e (p j) n -> p e (j n)", j=4))
                 else:
                     tl = raw_pool.tile([P, 2, T], F32, name="raw")
                     nc.sync.dma_start(tl[:], gate.rearrange("r n t -> n r t"))
@@ -125,34 +119,29 @@ def tile_routed_moe_kernel(tc, xT, w1, w2, gate, offs, pos1, pos2, out):
         def consumed():
             state["live"] -= 1
 
-        def gather(q, t):
-            if t == 0:
-                g4[q] = g4_pool.tile([P, 4, CHUNK], F32, name="g4")
-            nc.vector.tensor_copy(
-                g4[q][:, t, :], planes[t][:].indirect(offs_sb[:, q * (CHUNK // 16) : (q + 1) * (CHUNK // 16)])
-            )
-
-        def x_interleave(q):
-            xg[q] = xg_pool.tile([P, CHUNK, 4], BF16, name="xg", align_bytes=64)
-            eng = X_ENG[q]
-            if eng == "G":
-                for a in range(EPC):
-                    sl = slice(a * C, (a + 1) * C)
-                    copy_on("G", xg[q][:, sl, :], g4[q][:, :, sl].rearrange("p t n -> p n t"))
-            elif eng == "V":
-                copy_on("V", xg[q][:], g4[q][:].rearrange("p t n -> p n t"))
-            else:
-                copy_on(
-                    eng,
-                    xg[q][:].rearrange("p (c i) t -> p c t i", i=4),
-                    g4[q][:].rearrange("p t (c i) -> p c t i", i=4),
+        def gathers(c):
+            g4[c] = g4_pool.tile([P, 4, CH], F32, name="g4")
+            for t in range(4):
+                nc.vector.tensor_copy(
+                    g4[c][:, t, :], planes[t][:].indirect(offs_sb[:, c * (CH // 16) : (c + 1) * (CH // 16)])
                 )
 
-        def x_quantize(q):
-            xc[q] = held.tile([P, CHUNK], U32, name="xc%d" % q, align_bytes=64)
-            xs[q] = held.tile([P, CHUNK], U8, name="xs%d" % q, align_bytes=64)
+        def x_interleave(c):
+            xg[c] = xg_pool.tile([P, CH, 4], BF16, name="xg", align_bytes=64)
+            if X_ENG == "G" or False:
+                copy_on(X_ENG, xg[c][:], g4[c][:].rearrange("p t n -> p n t"))
+            else:
+                copy_on(
+                    X_ENG,
+                    xg[c][:].rearrange("p (c i) t -> p c t i", i=4),
+                    g4[c][:].rearrange("p t (c i) -> p c t i", i=4),
+                )
+
+        def x_quantize(c):
+            xc[c] = xc_pool.tile([P, CH], U32, name="xc", align_bytes=64)
+            xs[c] = xc_pool.tile([P, CH], U8, name="xs", align_bytes=64)
             nc.vector.quantize_mx(
-                out=xc[q][:].bitcast(FP8X4), scales=xs[q][:], in_=xg[q][:].rearrange("p n t -> p (n t)")
+                out=xc[c][:].bitcast(FP8X4), scales=xs[c][:], in_=xg[c][:].rearrange("p n t -> p (n t)")
             )
 
         def w1_interleave(e):
@@ -167,10 +156,10 @@ def tile_routed_moe_kernel(tc, xT, w1, w2, gate, offs, pos1, pos2, out):
                     w1g[e][:, 3 * H : 4 * H].rearrange("p (m j) -> p m j", j=4),
                     raw[("w1", e)][:].rearrange("p j (m t) -> p t m j", t=4)[:, 3, :, :],
                 )
-            if mv > 0:
-                copy_on("V", dst[:, 0:mv, :, 0:tm], src[:, 0:mv, :, 0:tm])
             if mv < P:
                 copy_on("S", dst[:, mv:P, :, 0:tm], src[:, mv:P, :, 0:tm])
+            if mv > 0:
+                copy_on("V", dst[:, 0:mv, :, 0:tm], src[:, 0:mv, :, 0:tm])
             consumed()
 
         def w1_quantize(e):
@@ -178,42 +167,37 @@ def tile_routed_moe_kernel(tc, xT, w1, w2, gate, offs, pos1, pos2, out):
             w1s[e] = w1q_pool.tile([P, H], U8, name="w1s", align_bytes=64)
             nc.vector.quantize_mx(out=w1c[e][:].bitcast(FP8X4), scales=w1s[e][:], in_=w1g[e][:])
 
-        def w2_interleave(e):
-            q, a = e // EPC, e % EPC
+        def w2_interleave(q, a):
             if a == 0:
-                w2g[q] = w2g_pool.tile([P, EPC, N, 4], BF16, name="w2g", align_bytes=64)
-            eng = W2_ENG[e]
-            if eng == "V":
-                if a == 0:
-                    copy_on("V", w2g[q][:], raw[("w2", q)][:].rearrange("p e (j n) -> p e n j", j=4))
-            elif eng == "G":
+                w2g[q] = w2g_pool.tile([P, WG, N, 4], BF16, name="w2g", align_bytes=64)
+            if W2_ENG == "G":
                 copy_on("G", w2g[q][:, a, :, :], raw[("w2", q)][:, a, :].rearrange("p (j n) -> p n j", j=4))
             else:
                 copy_on(
-                    eng,
+                    W2_ENG,
                     w2g[q][:, a, :, :].rearrange("p (c i) j -> p c j i", i=4),
                     raw[("w2", q)][:, a, :].rearrange("p (j c i) -> p c j i", j=4, i=4),
                 )
-            if a == EPC - 1:
+            if a == WG - 1:
                 consumed()
 
         def w2_quantize(q):
-            w2c[q] = held.tile([P, EPC * N], U32, name="w2c%d" % q, align_bytes=64)
-            w2s[q] = held.tile([P, EPC * N], U8, name="w2s%d" % q, align_bytes=64)
+            w2c[q] = held.tile([P, WG * N], U32, name="w2c%d" % q, align_bytes=64)
+            w2s[q] = held.tile([P, WG * N], U8, name="w2s%d" % q, align_bytes=64)
             nc.vector.quantize_mx(
                 out=w2c[q][:].bitcast(FP8X4), scales=w2s[q][:], in_=w2g[q][:].rearrange("p e n j -> p (e n j)")
             )
 
         def layer1(e):
-            q, a = e // EPC, e % EPC
+            c, a = e // EPCH, e % EPCH
             ps1[e] = ps1_pool.tile([P, 4, C], F32, name="ps1")
             for t in range(4):
                 nc.tensor.matmul_mx(
                     out=ps1[e][:, t, :],
                     lhsT=w1c[e][:, t * P : (t + 1) * P].bitcast(FP8X4),
                     lhsT_scale=w1s[e][:, t * P : (t + 1) * P],
-                    rhs=xc[q][:, a * C : (a + 1) * C].bitcast(FP8X4),
-                    rhs_scale=xs[q][:, a * C : (a + 1) * C],
+                    rhs=xc[c][:, a * C : (a + 1) * C].bitcast(FP8X4),
+                    rhs_scale=xs[c][:, a * C : (a + 1) * C],
                     start=True,
                     stop=True,
                 )
@@ -237,7 +221,7 @@ def tile_routed_moe_kernel(tc, xT, w1, w2, gate, offs, pos1, pos2, out):
             ps2[k] = ps2_pool.tile([P, 2 * C], F32, name="ps2")
             for b in range(2):
                 e = 2 * k + b
-                q, a = e // EPC, e % EPC
+                q, a = e // WG, e % WG
                 nc.tensor.matmul_mx(
                     out=ps2[k][:, b * C : (b + 1) * C],
                     lhsT=w2c[q][:, a * N : (a + 1) * N].bitcast(FP8X4),
@@ -247,48 +231,46 @@ def tile_routed_moe_kernel(tc, xT, w1, w2, gate, offs, pos1, pos2, out):
                     start=True,
                     stop=True,
                 )
-            copy_on(Y_ENG[k], y_all[:, 2 * k * C : (2 * k + 2) * C], ps2[k][:])
+            copy_on(Y_ENG[k % len(Y_ENG)], y_all[:, 2 * k * C : (2 * k + 2) * C], ps2[k][:])
 
         issue_loads()
-        later = [(q, t) for q in range(1, NCHUNK) for t in range(4)]
-        for t in range(4):
-            gather(0, t)
-        x_interleave(0)
-        for g in range(GATHER_LEAD):
-            gather(later[g][0], later[g][1])
-        x_quantize(0)
-
-        LAST = NCHUNK - 1
-        for i in range(E + 5):
-            if 0 <= i - 2 < E:
-                gelu(i - 2)
-            if i < E:
-                w1_interleave(i)
-            for q in range(1, NCHUNK):
-                if i == EPC * q - GATHER_LEAD + 1:
-                    x_quantize(q)
-            if 0 <= i - 1 < E:
-                w1_quantize(i - 1)
-                layer1(i - 1)
-            if i + GATHER_LEAD < len(later):
-                q, t = later[i + GATHER_LEAD]
-                gather(q, t)
-                if t == 3:
-                    x_interleave(q)
-            if i < EPC * (LAST if W2_LATE else NCHUNK) and i % EPC < 2:
-                w2_interleave(EPC * (i // EPC) + 2 * (i % EPC))
-                w2_interleave(EPC * (i // EPC) + 2 * (i % EPC) + 1)
-            if i < EPC * (LAST if W2_LATE else NCHUNK) and i % EPC == 2:
-                w2_quantize(i // EPC)
-            if i == E and W2_LATE:
-                for a in range(EPC):
-                    w2_interleave(EPC * LAST + a)
-                w2_quantize(LAST)
-            if i >= 4 and i % 2 == 0 and (i - 4) // 2 < E // 2:
-                k = (i - 4) // 2
-                h_quantize(k)
-                layer2(k)
-            issue_loads()
+        t0 = -XLEAD - 1
+        for i in range(t0, E + HL + 2):
+            for c in range(NCH):
+                if i == max(EPCH * c - XLEAD, t0 + c) + 2:
+                    x_quantize(c)
+            if 0 <= i - GL < E:
+                gelu(i - GL)
+            if 0 <= i + LC < E and i >= 0 or (i == 0 and False):
+                w1_interleave(i + LC)
+            if i == 0:
+                for e in range(LC):
+                    w1_interleave(e)
+            if 0 <= i - QL < E:
+                w1_quantize(i - QL)
+                layer1(i - QL)
+            for c in range(NCH):
+                if i == max(EPCH * c - XLEAD, t0 + c) + 1:
+                    x_interleave(c)
+            for c in range(NCH):
+                if i == max(EPCH * c - XLEAD, t0 + c):
+                    gathers(c)
+            j = i + W2LEAD
+            if 0 <= j < E and i >= 0 and not (False and j // WG == E // WG - 1):
+                if j % WG < 2:
+                    w2_interleave(j // WG, 2 * (j % WG))
+                    w2_interleave(j // WG, 2 * (j % WG) + 1)
+                if j % WG == 2:
+                    w2_quantize(j // WG)
+            if i == E and False:
+                for a in range(WG):
+                    w2_interleave(E // WG - 1, a)
+                w2_quantize(E // WG - 1)
+            if i >= HL and (i - HL) % 2 == 0 and (i - HL) // 2 < E // 2:
+                h_quantize((i - HL) // 2)
+                layer2((i - HL) // 2)
+            if i >= 0:
+                issue_loads()
 
         gt = raw[("gate", 0)]
         prods = {}

@@ -8,26 +8,50 @@ U32 = mybir.dt.uint32
 U16 = mybir.dt.uint16
 U8 = mybir.dt.uint8
 FP8X4 = mybir.dt.float8_e4m3fn_x4
-ACT = mybir.ActivationFunctionType
-ALU = mybir.AluOpType
+GELU = mybir.ActivationFunctionType.Gelu_apprx_tanh
+MULT = mybir.AluOpType.mult
+ADD = mybir.AluOpType.add
 
 P = 128
+PACK = 4
 K, T, E, C, H, N = 512, 1024, 16, 128, 512, 128
-S = E * C
-FLOPS = 2 * S * K * H + 2 * S * H * N
+SLOTS = E * C
+FLOPS = 2 * SLOTS * K * H + 2 * SLOTS * H * N
 
-CH = 256
-EPCH = CH // C
-NCH = S // CH
-WG = 4
-M_VEC = [56,56,56,56,56,56,56,56,88,88,88,88,88,88,88,88]
-G_PLANE = [0,0,0,0,0,0,0,0,0,0,0,0,0,0,0,0]
-X_ENG = "S"
-W2_ENG = "S"
-Y_ENG = "S"
-CTS = [256,256,256,256]
-LC, QL, GL, HL, XLEAD, W2LEAD = 2, 1, 2, 4, 4, 0
-RAW_BUFS = 9
+CHUNK = 256
+CHUNK_EXPERTS = CHUNK // C
+CHUNKS = SLOTS // CHUNK
+W2_GROUP = 4
+PAIR = 2
+
+COPY_AHEAD = 3
+QUANT_LAG = 1
+GELU_LAG = 2
+SECOND_LAG = 4
+X_AHEAD = 6
+FIRST_TICK = -X_AHEAD - 1
+LAST_TICK = E - PAIR + SECOND_LAG
+
+EARLY_GROUPS, LATE_GROUPS, LATE_FROM = 40, 80, 8
+
+GATHERED_BUFS, TOKEN_BF16_BUFS, TOKEN_CODE_BUFS = 2, 1, 2
+LOAD_BUFS = 9
+W1_BF16_BUFS = COPY_AHEAD + 4
+W1_CODE_BUFS = 4
+W2_BF16_BUFS = 2
+HIDDEN_BUFS = 4
+COMBINE_BUFS = 3
+FIRST_BANKS, SECOND_BANKS = 4, 3
+
+COMBINE_TOKENS = [512,256,256]
+
+
+def vector_groups(e):
+    return EARLY_GROUPS if e < LATE_FROM else LATE_GROUPS
+
+
+def gather_tick(c):
+    return max(CHUNK_EXPERTS * c - X_AHEAD, FIRST_TICK + c)
 
 
 def tile_routed_moe_kernel(tc, xT, w1, w2, gate, offs, pos1, pos2, out):
@@ -35,257 +59,229 @@ def tile_routed_moe_kernel(tc, xT, w1, w2, gate, offs, pos1, pos2, out):
     with ExitStack() as ctx:
         lists = ctx.enter_context(tc.tile_pool(name="lists", bufs=1))
         held = ctx.enter_context(tc.tile_pool(name="held", bufs=1))
-        raw_pool = ctx.enter_context(tc.tile_pool(name="raw_pool", bufs=RAW_BUFS))
-        g4_pool = ctx.enter_context(tc.tile_pool(name="g4_pool", bufs=2))
-        xg_pool = ctx.enter_context(tc.tile_pool(name="xg_pool", bufs=1))
-        xc_pool = ctx.enter_context(tc.tile_pool(name="xc_pool", bufs=2))
-        w1g_pool = ctx.enter_context(tc.tile_pool(name="w1g_pool", bufs=6))
-        w1q_pool = ctx.enter_context(tc.tile_pool(name="w1q_pool", bufs=4))
-        w2g_pool = ctx.enter_context(tc.tile_pool(name="w2g_pool", bufs=2))
-        h_pool = ctx.enter_context(tc.tile_pool(name="h_pool", bufs=4))
-        comb = ctx.enter_context(tc.tile_pool(name="comb", bufs=3))
-        ps1_pool = ctx.enter_context(tc.psum_pool(name="ps1_pool", bufs=4))
-        ps2_pool = ctx.enter_context(tc.psum_pool(name="ps2_pool", bufs=3))
+        load_pool = ctx.enter_context(tc.tile_pool(name="load_pool", bufs=LOAD_BUFS))
+        gathered_pool = ctx.enter_context(tc.tile_pool(name="gathered_pool", bufs=GATHERED_BUFS))
+        token_bf16_pool = ctx.enter_context(tc.tile_pool(name="token_bf16_pool", bufs=TOKEN_BF16_BUFS))
+        token_code_pool = ctx.enter_context(tc.tile_pool(name="token_code_pool", bufs=TOKEN_CODE_BUFS))
+        w1_bf16_pool = ctx.enter_context(tc.tile_pool(name="w1_bf16_pool", bufs=W1_BF16_BUFS))
+        w1_code_pool = ctx.enter_context(tc.tile_pool(name="w1_code_pool", bufs=W1_CODE_BUFS))
+        w2_bf16_pool = ctx.enter_context(tc.tile_pool(name="w2_bf16_pool", bufs=W2_BF16_BUFS))
+        hidden_pool = ctx.enter_context(tc.tile_pool(name="hidden_pool", bufs=HIDDEN_BUFS))
+        combine_pool = ctx.enter_context(tc.tile_pool(name="combine_pool", bufs=COMBINE_BUFS))
+        first_psum = ctx.enter_context(tc.psum_pool(name="first_psum", bufs=FIRST_BANKS))
+        second_psum = ctx.enter_context(tc.psum_pool(name="second_psum", bufs=SECOND_BANKS))
 
-        warm = held.tile([P, 1], F32, name="warm")
-        warm2 = held.tile([P, 1], F32, name="warm2")
-        nc.vector.memset(warm[:], 0.0)
-        nc.scalar.activation(out=warm2[:], in_=warm[:], func=ACT.Gelu_apprx_tanh)
+        zero = held.tile([P, 1], F32, name="zero")
+        unused = held.tile([P, 1], F32, name="unused")
+        nc.vector.memset(zero[:], 0.0)
+        nc.scalar.activation(out=unused[:], in_=zero[:], func=GELU)
 
-        offs_sb = lists.tile([P, S // 16], U16, name="offs_sb")
+        offs_sb = lists.tile([P, SLOTS // 16], U16, name="offs_sb")
         nc.sync.dma_start(offs_sb[:], offs)
         pos1_sb = lists.tile([P, T // 16], U16, name="pos1_sb")
         pos2_sb = lists.tile([P, T // 16], U16, name="pos2_sb")
 
-        x_view = xT.rearrange("(p t) n -> p t n", t=4)
+        rows_of_plane = xT.rearrange("(p j) n -> p j n", j=PACK)
         planes = []
-        for t in range(4):
-            plane = held.tile([P, T], F32, name="plane%d" % t)
-            nc.sync.dma_start(plane[:], x_view[:, t, :])
+        for j in range(PACK):
+            plane = held.tile([P, T], F32, name="plane%d" % j)
+            nc.sync.dma_start(plane[:], rows_of_plane[:, j, :])
             planes.append(plane)
 
-        y_all = held.tile([P, S], F32, name="y_all")
+        y_all = held.tile([P, SLOTS], F32, name="y_all")
 
-        raw = {}
-        w1g, w1c, w1s = {}, {}, {}
-        w2g, w2c, w2s = {}, {}, {}
-        g4, xg, xc, xs = {}, {}, {}, {}
-        ps1, ps2 = {}, {}
-        hg, hc, hs = {}, {}, {}
-
-        def copy_on(eng, dst, src):
-            if eng == "V":
-                nc.vector.tensor_copy(out=dst, in_=src)
-            elif eng == "S":
-                nc.scalar.copy(out=dst, in_=src)
-            else:
-                nc.gpsimd.tensor_scalar(out=dst, in0=src, scalar1=1.0, scalar2=0.0, op0=ALU.mult, op1=ALU.add)
-
-        order = []
+        stream = []
         for e in range(E):
             if e == 0:
-                order.append(("w1", 0))
-                order.append(("w2", 0))
-                continue
-            if (e + W2LEAD) % WG == 0 and (e + W2LEAD) // WG < E // WG and not (False and (e + W2LEAD) // WG == E // WG - 1):
-                order.append(("w2", (e + W2LEAD) // WG))
-            order.append(("w1", e))
-        order.append(("pos", 0))
-        if False:
-            order.append(("w2", E // WG - 1))
-        order.append(("gate", 0))
-        state = {"next": 0, "live": 0}
+                stream.append(("w1", 0))
+            if e % W2_GROUP == 0:
+                stream.append(("w2", e // W2_GROUP))
+            if e > 0:
+                stream.append(("w1", e))
+        stream.append(("lists", 0))
+        stream.append(("gate", 0))
+        loaded = {}
+        ring = {"next": 0, "in_use": 0}
 
-        def issue_loads():
-            while state["next"] < len(order) and state["live"] < RAW_BUFS:
-                kind, idx = order[state["next"]]
-                state["next"] += 1
-                if kind == "pos":
+        def load_while_the_ring_has_room():
+            while ring["next"] < len(stream) and ring["in_use"] < LOAD_BUFS:
+                what, index = stream[ring["next"]]
+                ring["next"] += 1
+                if what == "lists":
                     nc.sync.dma_start(pos1_sb[:], pos1)
                     nc.sync.dma_start(pos2_sb[:], pos2)
                     continue
-                state["live"] += 1
-                if kind == "w1":
-                    tl = raw_pool.tile([P, 4, H], F32, name="raw")
-                    nc.sync.dma_start(tl[:], w1[idx].rearrange("(p j) c -> p j c", j=4))
-                elif kind == "w2":
-                    tl = raw_pool.tile([P, WG, 4 * N], F32, name="raw")
-                    nc.sync.dma_start(tl[:], w2[idx * WG : (idx + 1) * WG].rearrange("e (p j) n -> p e (j n)", j=4))
+                ring["in_use"] += 1
+                if what == "w1":
+                    tile = load_pool.tile([P, PACK, H], F32, name="load")
+                    nc.sync.dma_start(tile[:], w1[index].rearrange("(p j) i -> p j i", j=PACK))
+                elif what == "w2":
+                    tile = load_pool.tile([P, W2_GROUP, PACK * N], F32, name="load")
+                    group = w2[index * W2_GROUP : (index + 1) * W2_GROUP]
+                    nc.sync.dma_start(tile[:], group.rearrange("e (p j) n -> p e (j n)", j=PACK))
                 else:
-                    tl = raw_pool.tile([P, 2, T], F32, name="raw")
-                    nc.sync.dma_start(tl[:], gate.rearrange("r n t -> n r t"))
-                raw[(kind, idx)] = tl
+                    tile = load_pool.tile([P, 2, T], F32, name="load")
+                    nc.sync.dma_start(tile[:], gate.rearrange("r n t -> n r t"))
+                loaded[(what, index)] = tile
 
-        def consumed():
-            state["live"] -= 1
+        gathered, token_bf16, token_codes, token_scales = {}, {}, {}, {}
+        w1_bf16, w1_codes, w1_scales = {}, {}, {}
+        w2_bf16, w2_codes, w2_scales = {}, {}, {}
+        first_sums, hidden_bf16, hidden_codes, hidden_scales = {}, {}, {}, {}
 
-        def gathers(c):
-            g4[c] = g4_pool.tile([P, 4, CH], F32, name="g4")
-            for t in range(4):
-                nc.vector.tensor_copy(
-                    g4[c][:, t, :], planes[t][:].indirect(offs_sb[:, c * (CH // 16) : (c + 1) * (CH // 16)])
-                )
+        def gather_tokens(c):
+            gathered[c] = gathered_pool.tile([P, PACK, CHUNK], F32, name="gathered")
+            entries = offs_sb[:, c * (CHUNK // 16) : (c + 1) * (CHUNK // 16)]
+            for j in range(PACK):
+                nc.vector.tensor_copy(gathered[c][:, j, :], planes[j][:].indirect(entries))
 
-        def x_interleave(c):
-            xg[c] = xg_pool.tile([P, CH, 4], BF16, name="xg", align_bytes=64)
-            if X_ENG == "G" or False:
-                copy_on(X_ENG, xg[c][:], g4[c][:].rearrange("p t n -> p n t"))
-            else:
-                copy_on(
-                    X_ENG,
-                    xg[c][:].rearrange("p (c i) t -> p c t i", i=4),
-                    g4[c][:].rearrange("p t (c i) -> p c t i", i=4),
-                )
-
-        def x_quantize(c):
-            xc[c] = xc_pool.tile([P, CH], U32, name="xc", align_bytes=64)
-            xs[c] = xc_pool.tile([P, CH], U8, name="xs", align_bytes=64)
-            nc.vector.quantize_mx(
-                out=xc[c][:].bitcast(FP8X4), scales=xs[c][:], in_=xg[c][:].rearrange("p n t -> p (n t)")
+        def interleave_tokens(c):
+            token_bf16[c] = token_bf16_pool.tile([P, CHUNK, PACK], BF16, name="token_bf16", align_bytes=64)
+            nc.scalar.copy(
+                out=token_bf16[c][:].rearrange("p (s i) j -> p s j i", i=4),
+                in_=gathered[c][:].rearrange("p j (s i) -> p s j i", i=4),
             )
 
-        def w1_interleave(e):
-            w1g[e] = w1g_pool.tile([P, 4 * H], BF16, name="w1g", align_bytes=64)
-            dst = w1g[e][:].rearrange("p (t m j) -> p m j t", t=4, j=4)
-            src = raw[("w1", e)][:].rearrange("p j (m t) -> p m j t", t=4)
-            mv = M_VEC[e]
-            tm = 3 if G_PLANE[e] else 4
-            if G_PLANE[e]:
-                copy_on(
-                    "G",
-                    w1g[e][:, 3 * H : 4 * H].rearrange("p (m j) -> p m j", j=4),
-                    raw[("w1", e)][:].rearrange("p j (m t) -> p t m j", t=4)[:, 3, :, :],
-                )
-            if mv < P:
-                copy_on("S", dst[:, mv:P, :, 0:tm], src[:, mv:P, :, 0:tm])
-            if mv > 0:
-                copy_on("V", dst[:, 0:mv, :, 0:tm], src[:, 0:mv, :, 0:tm])
-            consumed()
+        def quantize_tokens(c):
+            token_codes[c] = token_code_pool.tile([P, CHUNK], U32, name="token_codes", align_bytes=64)
+            token_scales[c] = token_code_pool.tile([P, CHUNK], U8, name="token_scales", align_bytes=64)
+            nc.vector.quantize_mx(
+                out=token_codes[c][:].bitcast(FP8X4),
+                scales=token_scales[c][:],
+                in_=token_bf16[c][:].rearrange("p s j -> p (s j)"),
+            )
 
-        def w1_quantize(e):
-            w1c[e] = w1q_pool.tile([P, H], U32, name="w1c", align_bytes=64)
-            w1s[e] = w1q_pool.tile([P, H], U8, name="w1s", align_bytes=64)
-            nc.vector.quantize_mx(out=w1c[e][:].bitcast(FP8X4), scales=w1s[e][:], in_=w1g[e][:])
+        def interleave_w1(e):
+            w1_bf16[e] = w1_bf16_pool.tile([P, PACK * H], BF16, name="w1_bf16", align_bytes=64)
+            dst = w1_bf16[e][:].rearrange("p (t m j) -> p m j t", t=4, j=PACK)
+            src = loaded[("w1", e)][:].rearrange("p j (m t) -> p m j t", t=4)
+            split = vector_groups(e)
+            nc.scalar.copy(out=dst[:, split:P, :, :], in_=src[:, split:P, :, :])
+            nc.vector.tensor_copy(out=dst[:, 0:split, :, :], in_=src[:, 0:split, :, :])
+            ring["in_use"] -= 1
 
-        def w2_interleave(q, a):
+        def quantize_w1(e):
+            w1_codes[e] = w1_code_pool.tile([P, H], U32, name="w1_codes", align_bytes=64)
+            w1_scales[e] = w1_code_pool.tile([P, H], U8, name="w1_scales", align_bytes=64)
+            nc.vector.quantize_mx(out=w1_codes[e][:].bitcast(FP8X4), scales=w1_scales[e][:], in_=w1_bf16[e][:])
+
+        def interleave_w2(e):
+            q, a = e // W2_GROUP, e % W2_GROUP
             if a == 0:
-                w2g[q] = w2g_pool.tile([P, WG, N, 4], BF16, name="w2g", align_bytes=64)
-            if W2_ENG == "G":
-                copy_on("G", w2g[q][:, a, :, :], raw[("w2", q)][:, a, :].rearrange("p (j n) -> p n j", j=4))
-            else:
-                copy_on(
-                    W2_ENG,
-                    w2g[q][:, a, :, :].rearrange("p (c i) j -> p c j i", i=4),
-                    raw[("w2", q)][:, a, :].rearrange("p (j c i) -> p c j i", j=4, i=4),
-                )
-            if a == WG - 1:
-                consumed()
+                w2_bf16[q] = w2_bf16_pool.tile([P, W2_GROUP, N, PACK], BF16, name="w2_bf16", align_bytes=64)
+            nc.scalar.copy(
+                out=w2_bf16[q][:, a, :, :].rearrange("p (n i) j -> p n j i", i=4),
+                in_=loaded[("w2", q)][:, a, :].rearrange("p (j n i) -> p n j i", j=PACK, i=4),
+            )
+            if a == W2_GROUP - 1:
+                ring["in_use"] -= 1
 
-        def w2_quantize(q):
-            w2c[q] = held.tile([P, WG * N], U32, name="w2c%d" % q, align_bytes=64)
-            w2s[q] = held.tile([P, WG * N], U8, name="w2s%d" % q, align_bytes=64)
+        def quantize_w2(q):
+            w2_codes[q] = held.tile([P, W2_GROUP * N], U32, name="w2_codes%d" % q, align_bytes=64)
+            w2_scales[q] = held.tile([P, W2_GROUP * N], U8, name="w2_scales%d" % q, align_bytes=64)
             nc.vector.quantize_mx(
-                out=w2c[q][:].bitcast(FP8X4), scales=w2s[q][:], in_=w2g[q][:].rearrange("p e n j -> p (e n j)")
+                out=w2_codes[q][:].bitcast(FP8X4),
+                scales=w2_scales[q][:],
+                in_=w2_bf16[q][:].rearrange("p a n j -> p (a n j)"),
             )
 
-        def layer1(e):
-            c, a = e // EPCH, e % EPCH
-            ps1[e] = ps1_pool.tile([P, 4, C], F32, name="ps1")
+        def first_layer(e):
+            c, a = e // CHUNK_EXPERTS, e % CHUNK_EXPERTS
+            first_sums[e] = first_psum.tile([P, 4, C], F32, name="first_sums")
             for t in range(4):
                 nc.tensor.matmul_mx(
-                    out=ps1[e][:, t, :],
-                    lhsT=w1c[e][:, t * P : (t + 1) * P].bitcast(FP8X4),
-                    lhsT_scale=w1s[e][:, t * P : (t + 1) * P],
-                    rhs=xc[c][:, a * C : (a + 1) * C].bitcast(FP8X4),
-                    rhs_scale=xs[c][:, a * C : (a + 1) * C],
+                    out=first_sums[e][:, t, :],
+                    lhsT=w1_codes[e][:, t * P : (t + 1) * P].bitcast(FP8X4),
+                    lhsT_scale=w1_scales[e][:, t * P : (t + 1) * P],
+                    rhs=token_codes[c][:, a * C : (a + 1) * C].bitcast(FP8X4),
+                    rhs_scale=token_scales[c][:, a * C : (a + 1) * C],
                     start=True,
                     stop=True,
                 )
 
         def gelu(e):
-            k, a = e // 2, e % 2
-            if a == 0:
-                hg[k] = h_pool.tile([P, 2, C, 4], BF16, name="hg", align_bytes=64)
+            k, b = e // PAIR, e % PAIR
+            if b == 0:
+                hidden_bf16[k] = hidden_pool.tile([P, PAIR, C, PACK], BF16, name="hidden_bf16", align_bytes=64)
             nc.scalar.activation(
-                out=hg[k][:, a, :, :], in_=ps1[e][:].rearrange("p t n -> p n t"), func=ACT.Gelu_apprx_tanh
+                out=hidden_bf16[k][:, b, :, :], in_=first_sums[e][:].rearrange("p t s -> p s t"), func=GELU
             )
 
-        def h_quantize(k):
-            hc[k] = h_pool.tile([P, 2 * C], U32, name="hc", align_bytes=64)
-            hs[k] = h_pool.tile([P, 2 * C], U8, name="hs", align_bytes=64)
+        def second_layer(k):
+            hidden_codes[k] = hidden_pool.tile([P, PAIR * C], U32, name="hidden_codes", align_bytes=64)
+            hidden_scales[k] = hidden_pool.tile([P, PAIR * C], U8, name="hidden_scales", align_bytes=64)
             nc.vector.quantize_mx(
-                out=hc[k][:].bitcast(FP8X4), scales=hs[k][:], in_=hg[k][:].rearrange("p a n t -> p (a n t)")
+                out=hidden_codes[k][:].bitcast(FP8X4),
+                scales=hidden_scales[k][:],
+                in_=hidden_bf16[k][:].rearrange("p b s t -> p (b s t)"),
             )
-
-        def layer2(k):
-            ps2[k] = ps2_pool.tile([P, 2 * C], F32, name="ps2")
-            for b in range(2):
-                e = 2 * k + b
-                q, a = e // WG, e % WG
+            second_sums = second_psum.tile([P, PAIR * C], F32, name="second_sums")
+            for b in range(PAIR):
+                e = PAIR * k + b
+                q, a = e // W2_GROUP, e % W2_GROUP
                 nc.tensor.matmul_mx(
-                    out=ps2[k][:, b * C : (b + 1) * C],
-                    lhsT=w2c[q][:, a * N : (a + 1) * N].bitcast(FP8X4),
-                    lhsT_scale=w2s[q][:, a * N : (a + 1) * N],
-                    rhs=hc[k][:, b * C : (b + 1) * C].bitcast(FP8X4),
-                    rhs_scale=hs[k][:, b * C : (b + 1) * C],
+                    out=second_sums[:, b * C : (b + 1) * C],
+                    lhsT=w2_codes[q][:, a * N : (a + 1) * N].bitcast(FP8X4),
+                    lhsT_scale=w2_scales[q][:, a * N : (a + 1) * N],
+                    rhs=hidden_codes[k][:, b * C : (b + 1) * C].bitcast(FP8X4),
+                    rhs_scale=hidden_scales[k][:, b * C : (b + 1) * C],
                     start=True,
                     stop=True,
                 )
-            copy_on(Y_ENG[k % len(Y_ENG)], y_all[:, 2 * k * C : (2 * k + 2) * C], ps2[k][:])
+            y_slots = y_all[:, PAIR * k * C : PAIR * (k + 1) * C]
+            if k == E // PAIR - 1:
+                nc.vector.tensor_copy(out=y_slots, in_=second_sums[:])
+            else:
+                nc.scalar.copy(out=y_slots, in_=second_sums[:])
 
-        issue_loads()
-        t0 = -XLEAD - 1
-        for i in range(t0, E + HL + 2):
-            for c in range(NCH):
-                if i == max(EPCH * c - XLEAD, t0 + c) + 2:
-                    x_quantize(c)
-            if 0 <= i - GL < E:
-                gelu(i - GL)
-            if 0 <= i + LC < E and i >= 0 or (i == 0 and False):
-                w1_interleave(i + LC)
-            if i == 0:
-                for e in range(LC):
-                    w1_interleave(e)
-            if 0 <= i - QL < E:
-                w1_quantize(i - QL)
-                layer1(i - QL)
-            for c in range(NCH):
-                if i == max(EPCH * c - XLEAD, t0 + c) + 1:
-                    x_interleave(c)
-            for c in range(NCH):
-                if i == max(EPCH * c - XLEAD, t0 + c):
-                    gathers(c)
-            j = i + W2LEAD
-            if 0 <= j < E and i >= 0 and not (False and j // WG == E // WG - 1):
-                if j % WG < 2:
-                    w2_interleave(j // WG, 2 * (j % WG))
-                    w2_interleave(j // WG, 2 * (j % WG) + 1)
-                if j % WG == 2:
-                    w2_quantize(j // WG)
-            if i == E and False:
-                for a in range(WG):
-                    w2_interleave(E // WG - 1, a)
-                w2_quantize(E // WG - 1)
-            if i >= HL and (i - HL) % 2 == 0 and (i - HL) // 2 < E // 2:
-                h_quantize((i - HL) // 2)
-                layer2((i - HL) // 2)
-            if i >= 0:
-                issue_loads()
+        load_while_the_ring_has_room()
+        for tick in range(FIRST_TICK, LAST_TICK + 1):
+            for c in range(CHUNKS):
+                if tick == gather_tick(c) + 2:
+                    quantize_tokens(c)
+            if 0 <= tick - GELU_LAG < E:
+                gelu(tick - GELU_LAG)
+            if 0 <= tick < E - COPY_AHEAD:
+                interleave_w1(tick + COPY_AHEAD)
+            if tick == 0:
+                for e in range(COPY_AHEAD):
+                    interleave_w1(e)
+            if 0 <= tick - QUANT_LAG < E:
+                quantize_w1(tick - QUANT_LAG)
+                first_layer(tick - QUANT_LAG)
+            for c in range(CHUNKS):
+                if tick == gather_tick(c) + 1:
+                    interleave_tokens(c)
+            for c in range(CHUNKS):
+                if tick == gather_tick(c):
+                    gather_tokens(c)
+            if 0 <= tick < E:
+                q, step = tick // W2_GROUP, tick % W2_GROUP
+                if step < 2:
+                    interleave_w2(W2_GROUP * q + 2 * step)
+                    interleave_w2(W2_GROUP * q + 2 * step + 1)
+                if step == 2:
+                    quantize_w2(q)
+            if tick >= SECOND_LAG and (tick - SECOND_LAG) % PAIR == 0:
+                second_layer((tick - SECOND_LAG) // PAIR)
+            if tick >= 0:
+                load_while_the_ring_has_room()
 
-        gt = raw[("gate", 0)]
-        prods = {}
-        starts = [sum(CTS[:c]) for c in range(len(CTS))]
-        for c in range(len(CTS) + 1):
-            if c < len(CTS):
-                cols = slice(starts[c], starts[c] + CTS[c])
-                lcols = slice(starts[c] // 16, (starts[c] + CTS[c]) // 16)
-                pa = comb.tile([P, CTS[c]], F32, name="pa")
-                nc.vector.tensor_tensor(pa[:], y_all[:].indirect(pos1_sb[:, lcols]), gt[:, 0, cols], ALU.mult)
-                pb = comb.tile([P, CTS[c]], F32, name="pb")
-                nc.vector.tensor_tensor(pb[:], y_all[:].indirect(pos2_sb[:, lcols]), gt[:, 1, cols], ALU.mult)
-                prods[c] = (pa, pb)
-            if c >= 1:
-                pa, pb = prods[c - 1]
-                res = comb.tile([P, CTS[c - 1]], F32, name="res")
-                nc.vector.tensor_tensor(res[:], pa[:], pb[:], ALU.add)
-                nc.sync.dma_start(out[:, starts[c - 1] : starts[c - 1] + CTS[c - 1]], res[:])
+        gate_sb = loaded[("gate", 0)]
+        products = []
+        first_token = 0
+        for step in range(len(COMBINE_TOKENS) + 1):
+            if step < len(COMBINE_TOKENS):
+                tokens = slice(first_token, first_token + COMBINE_TOKENS[step])
+                entries = slice(tokens.start // 16, tokens.stop // 16)
+                first_token = tokens.stop
+                one = combine_pool.tile([P, COMBINE_TOKENS[step]], F32, name="one")
+                nc.vector.tensor_tensor(one[:], y_all[:].indirect(pos1_sb[:, entries]), gate_sb[:, 0, tokens], MULT)
+                two = combine_pool.tile([P, COMBINE_TOKENS[step]], F32, name="two")
+                nc.vector.tensor_tensor(two[:], y_all[:].indirect(pos2_sb[:, entries]), gate_sb[:, 1, tokens], MULT)
+                products.append((one, two, tokens))
+            if step >= 1:
+                one, two, tokens = products[step - 1]
+                total = combine_pool.tile([P, tokens.stop - tokens.start], F32, name="total")
+                nc.vector.tensor_tensor(total[:], one[:], two[:], ADD)
+                nc.sync.dma_start(out[:, tokens], total[:])

@@ -9,6 +9,7 @@ U16 = mybir.dt.uint16
 U8 = mybir.dt.uint8
 FP8X4 = mybir.dt.float8_e4m3fn_x4
 GELU = mybir.ActivationFunctionType.Gelu_apprx_tanh
+COPY = mybir.ActivationFunctionType.Copy
 MULT = mybir.AluOpType.mult
 ADD = mybir.AluOpType.add
 
@@ -18,40 +19,37 @@ K, T, E, C, H, N = 512, 1024, 16, 128, 512, 128
 SLOTS = E * C
 FLOPS = 2 * SLOTS * K * H + 2 * SLOTS * H * N
 
-CHUNK = 256
+CHUNK = 128
 CHUNK_EXPERTS = CHUNK // C
 CHUNKS = SLOTS // CHUNK
 W2_GROUP = 4
 PAIR = 2
 
-COPY_AHEAD = 3
-QUANT_LAG = 1
-GELU_LAG = 2
-SECOND_LAG = 4
-X_AHEAD = 6
-FIRST_TICK = -X_AHEAD - 1
+COPY_LEAD = 0
+GELU_LAG = 1
+SECOND_LAG = 5
+X_AHEAD = 4
+QT_AHEAD = 0
+W2_COPY_AHEAD = 1
+W2_QUANT_LAG = 2
+FIRST_TICK = -6
 LAST_TICK = E - PAIR + SECOND_LAG
+HEAD_LOADS = 0
 
-EARLY_GROUPS, LATE_GROUPS, LATE_FROM = 40, 80, 8
+W2_ON_SCALAR = 0
 
-GATHERED_BUFS, TOKEN_BF16_BUFS, TOKEN_CODE_BUFS = 2, 1, 2
+TOKEN_BF16_BUFS = 2
+TOKEN_CODE_BUFS = 2
 LOAD_BUFS = 9
-W1_BF16_BUFS = COPY_AHEAD + 4
+W1_BF16_BUFS = 4
 W1_CODE_BUFS = 4
 W2_BF16_BUFS = 2
+W2_CODE_BUFS = 1
 HIDDEN_BUFS = 4
 COMBINE_BUFS = 3
 FIRST_BANKS, SECOND_BANKS = 4, 3
 
 COMBINE_TOKENS = [512,256,256]
-
-
-def vector_groups(e):
-    return EARLY_GROUPS if e < LATE_FROM else LATE_GROUPS
-
-
-def gather_tick(c):
-    return max(CHUNK_EXPERTS * c - X_AHEAD, FIRST_TICK + c)
 
 
 def tile_routed_moe_kernel(tc, xT, w1, w2, gate, offs, pos1, pos2, out):
@@ -60,12 +58,12 @@ def tile_routed_moe_kernel(tc, xT, w1, w2, gate, offs, pos1, pos2, out):
         lists = ctx.enter_context(tc.tile_pool(name="lists", bufs=1))
         held = ctx.enter_context(tc.tile_pool(name="held", bufs=1))
         load_pool = ctx.enter_context(tc.tile_pool(name="load_pool", bufs=LOAD_BUFS))
-        gathered_pool = ctx.enter_context(tc.tile_pool(name="gathered_pool", bufs=GATHERED_BUFS))
         token_bf16_pool = ctx.enter_context(tc.tile_pool(name="token_bf16_pool", bufs=TOKEN_BF16_BUFS))
         token_code_pool = ctx.enter_context(tc.tile_pool(name="token_code_pool", bufs=TOKEN_CODE_BUFS))
         w1_bf16_pool = ctx.enter_context(tc.tile_pool(name="w1_bf16_pool", bufs=W1_BF16_BUFS))
         w1_code_pool = ctx.enter_context(tc.tile_pool(name="w1_code_pool", bufs=W1_CODE_BUFS))
         w2_bf16_pool = ctx.enter_context(tc.tile_pool(name="w2_bf16_pool", bufs=W2_BF16_BUFS))
+        w2_code_pool = ctx.enter_context(tc.tile_pool(name="w2_code_pool", bufs=W2_CODE_BUFS))
         hidden_pool = ctx.enter_context(tc.tile_pool(name="hidden_pool", bufs=HIDDEN_BUFS))
         combine_pool = ctx.enter_context(tc.tile_pool(name="combine_pool", bufs=COMBINE_BUFS))
         first_psum = ctx.enter_context(tc.psum_pool(name="first_psum", bufs=FIRST_BANKS))
@@ -83,10 +81,17 @@ def tile_routed_moe_kernel(tc, xT, w1, w2, gate, offs, pos1, pos2, out):
 
         rows_of_plane = xT.rearrange("(p j) n -> p j n", j=PACK)
         planes = []
-        for j in range(PACK):
-            plane = held.tile([P, T], F32, name="plane%d" % j)
-            nc.sync.dma_start(plane[:], rows_of_plane[:, j, :])
-            planes.append(plane)
+        planes_bf16 = []
+
+        def load_planes():
+            for j in range(PACK):
+                plane = held.tile([P, T], F32, name="plane%d" % j)
+                nc.sync.dma_start(plane[:], rows_of_plane[:, j, :])
+                planes.append(plane)
+            for j in range(PACK):
+                plane_bf16 = held.tile([P, T], BF16, name="plane_bf16_%d" % j)
+                nc.vector.tensor_copy(out=plane_bf16[:], in_=planes[j][:])
+                planes_bf16.append(plane_bf16)
 
         y_all = held.tile([P, SLOTS], F32, name="y_all")
 
@@ -105,6 +110,8 @@ def tile_routed_moe_kernel(tc, xT, w1, w2, gate, offs, pos1, pos2, out):
 
         def load_while_the_ring_has_room():
             while ring["next"] < len(stream) and ring["in_use"] < LOAD_BUFS:
+                if ring["next"] == HEAD_LOADS:
+                    load_planes()
                 what, index = stream[ring["next"]]
                 ring["next"] += 1
                 if what == "lists":
@@ -124,23 +131,20 @@ def tile_routed_moe_kernel(tc, xT, w1, w2, gate, offs, pos1, pos2, out):
                     nc.sync.dma_start(tile[:], gate.rearrange("r n t -> n r t"))
                 loaded[(what, index)] = tile
 
-        gathered, token_bf16, token_codes, token_scales = {}, {}, {}, {}
+        token_bf16, token_codes, token_scales = {}, {}, {}
         w1_bf16, w1_codes, w1_scales = {}, {}, {}
         w2_bf16, w2_codes, w2_scales = {}, {}, {}
         first_sums, hidden_bf16, hidden_codes, hidden_scales = {}, {}, {}, {}
 
         def gather_tokens(c):
-            gathered[c] = gathered_pool.tile([P, PACK, CHUNK], F32, name="gathered")
-            entries = offs_sb[:, c * (CHUNK // 16) : (c + 1) * (CHUNK // 16)]
-            for j in range(PACK):
-                nc.vector.tensor_copy(gathered[c][:, j, :], planes[j][:].indirect(entries))
-
-        def interleave_tokens(c):
             token_bf16[c] = token_bf16_pool.tile([P, CHUNK, PACK], BF16, name="token_bf16", align_bytes=64)
-            nc.scalar.copy(
-                out=token_bf16[c][:].rearrange("p (s i) j -> p s j i", i=4),
-                in_=gathered[c][:].rearrange("p j (s i) -> p s j i", i=4),
-            )
+            for a in range(CHUNK_EXPERTS):
+                e = c * CHUNK_EXPERTS + a
+                entries = offs_sb[:, e * (C // 16) : (e + 1) * (C // 16)]
+                for j in range(PACK):
+                    nc.scalar.activation(
+                        out=token_bf16[c][:, a * C : (a + 1) * C, j], in_=planes_bf16[j][:].indirect(entries), func=COPY
+                    )
 
         def quantize_tokens(c):
             token_codes[c] = token_code_pool.tile([P, CHUNK], U32, name="token_codes", align_bytes=64)
@@ -155,9 +159,7 @@ def tile_routed_moe_kernel(tc, xT, w1, w2, gate, offs, pos1, pos2, out):
             w1_bf16[e] = w1_bf16_pool.tile([P, PACK * H], BF16, name="w1_bf16", align_bytes=64)
             dst = w1_bf16[e][:].rearrange("p (t m j) -> p m j t", t=4, j=PACK)
             src = loaded[("w1", e)][:].rearrange("p j (m t) -> p m j t", t=4)
-            split = vector_groups(e)
-            nc.scalar.copy(out=dst[:, split:P, :, :], in_=src[:, split:P, :, :])
-            nc.vector.tensor_copy(out=dst[:, 0:split, :, :], in_=src[:, 0:split, :, :])
+            nc.vector.tensor_copy(out=dst, in_=src)
             ring["in_use"] -= 1
 
         def quantize_w1(e):
@@ -165,20 +167,25 @@ def tile_routed_moe_kernel(tc, xT, w1, w2, gate, offs, pos1, pos2, out):
             w1_scales[e] = w1_code_pool.tile([P, H], U8, name="w1_scales", align_bytes=64)
             nc.vector.quantize_mx(out=w1_codes[e][:].bitcast(FP8X4), scales=w1_scales[e][:], in_=w1_bf16[e][:])
 
-        def interleave_w2(e):
-            q, a = e // W2_GROUP, e % W2_GROUP
-            if a == 0:
+        def interleave_w2(q, step):
+            if step == 0:
                 w2_bf16[q] = w2_bf16_pool.tile([P, W2_GROUP, N, PACK], BF16, name="w2_bf16", align_bytes=64)
-            nc.scalar.copy(
-                out=w2_bf16[q][:, a, :, :].rearrange("p (n i) j -> p n j i", i=4),
-                in_=loaded[("w2", q)][:, a, :].rearrange("p (j n i) -> p n j i", j=PACK, i=4),
-            )
-            if a == W2_GROUP - 1:
+                for a in range(W2_ON_SCALAR):
+                    nc.scalar.copy(
+                        out=w2_bf16[q][:, a, :, :].rearrange("p (n i) j -> p n j i", i=4),
+                        in_=loaded[("w2", q)][:, a, :].rearrange("p (j n i) -> p n j i", j=PACK, i=4),
+                    )
+            else:
+                if W2_ON_SCALAR < W2_GROUP:
+                    nc.vector.tensor_copy(
+                        out=w2_bf16[q][:, W2_ON_SCALAR:W2_GROUP, :, :].rearrange("p a (n i) j -> p a n j i", i=4),
+                        in_=loaded[("w2", q)][:, W2_ON_SCALAR:W2_GROUP, :].rearrange("p a (j n i) -> p a n j i", j=PACK, i=4),
+                    )
                 ring["in_use"] -= 1
 
         def quantize_w2(q):
-            w2_codes[q] = held.tile([P, W2_GROUP * N], U32, name="w2_codes%d" % q, align_bytes=64)
-            w2_scales[q] = held.tile([P, W2_GROUP * N], U8, name="w2_scales%d" % q, align_bytes=64)
+            w2_codes[q] = w2_code_pool.tile([P, W2_GROUP * N], U32, name="w2_codes", align_bytes=64)
+            w2_scales[q] = w2_code_pool.tile([P, W2_GROUP * N], U8, name="w2_scales", align_bytes=64)
             nc.vector.quantize_mx(
                 out=w2_codes[q][:].bitcast(FP8X4),
                 scales=w2_scales[q][:],
@@ -236,36 +243,29 @@ def tile_routed_moe_kernel(tc, xT, w1, w2, gate, offs, pos1, pos2, out):
 
         load_while_the_ring_has_room()
         for tick in range(FIRST_TICK, LAST_TICK + 1):
-            for c in range(CHUNKS):
-                if tick == gather_tick(c) + 2:
-                    quantize_tokens(c)
-            if 0 <= tick - GELU_LAG < E:
-                gelu(tick - GELU_LAG)
-            if 0 <= tick < E - COPY_AHEAD:
-                interleave_w1(tick + COPY_AHEAD)
-            if tick == 0:
-                for e in range(COPY_AHEAD):
-                    interleave_w1(e)
-            if 0 <= tick - QUANT_LAG < E:
-                quantize_w1(tick - QUANT_LAG)
-                first_layer(tick - QUANT_LAG)
-            for c in range(CHUNKS):
-                if tick == gather_tick(c) + 1:
-                    interleave_tokens(c)
-            for c in range(CHUNKS):
-                if tick == gather_tick(c):
-                    gather_tokens(c)
-            if 0 <= tick < E:
-                q, step = tick // W2_GROUP, tick % W2_GROUP
-                if step < 2:
-                    interleave_w2(W2_GROUP * q + 2 * step)
-                    interleave_w2(W2_GROUP * q + 2 * step + 1)
-                if step == 2:
-                    quantize_w2(q)
             if tick >= SECOND_LAG and (tick - SECOND_LAG) % PAIR == 0:
                 second_layer((tick - SECOND_LAG) // PAIR)
-            if tick >= 0:
-                load_while_the_ring_has_room()
+            if 0 <= tick - GELU_LAG < E:
+                gelu(tick - GELU_LAG)
+            if 0 <= tick + COPY_LEAD < E:
+                interleave_w1(tick + COPY_LEAD)
+            if 0 <= tick < E:
+                quantize_w1(tick)
+            for c in range(CHUNKS):
+                if tick == CHUNK_EXPERTS * c - QT_AHEAD:
+                    quantize_tokens(c)
+            if 0 <= tick < E:
+                first_layer(tick)
+            for q in range(E // W2_GROUP):
+                for step in range(2):
+                    if tick == W2_GROUP * q - W2_COPY_AHEAD + step:
+                        interleave_w2(q, step)
+                if tick == W2_GROUP * q + W2_QUANT_LAG:
+                    quantize_w2(q)
+            for c in range(CHUNKS):
+                if tick == max(CHUNK_EXPERTS * c - X_AHEAD, FIRST_TICK):
+                    gather_tokens(c)
+            load_while_the_ring_has_room()
 
         gate_sb = loaded[("gate", 0)]
         products = []

@@ -19,35 +19,29 @@ K, T, E, C, H, N = 512, 1024, 16, 128, 512, 128
 SLOTS = E * C
 FLOPS = 2 * SLOTS * K * H + 2 * SLOTS * H * N
 
-CHUNK = 128
-CHUNK_EXPERTS = CHUNK // C
-CHUNKS = SLOTS // CHUNK
 W2_GROUP = 4
 PAIR = 2
 
-COPY_LEAD = 0
-GELU_LAG = 1
-SECOND_LAG = 5
-X_AHEAD = 4
-QT_AHEAD = 0
+GATHER_AHEAD = 4
+TOKEN_AHEAD = 1
+COPY_AHEAD = 1
+GELU_LAG = 0
+SECOND_LAG = 3
 W2_COPY_AHEAD = 1
-W2_QUANT_LAG = 2
-FIRST_TICK = -6
+W2_QUANT_LAG = 1
+FIRST_TICK = -GATHER_AHEAD
 LAST_TICK = E - PAIR + SECOND_LAG
-HEAD_LOADS = 0
 
-W2_ON_SCALAR = 0
-
-TOKEN_BF16_BUFS = 2
-TOKEN_CODE_BUFS = 2
 LOAD_BUFS = 9
-W1_BF16_BUFS = 4
+BY_SCALAR_BUFS = 8
+BY_COPY_BUFS = 4
 W1_CODE_BUFS = 4
-W2_BF16_BUFS = 2
-W2_CODE_BUFS = 1
-HIDDEN_BUFS = 4
+TOKEN_CODE_BUFS = 4
+HIDDEN_CODE_BUFS = 3
+W2_CODE_BUFS = 2
+SCALE_BUFS = 12
+SUMS_BANKS = 8
 COMBINE_BUFS = 3
-FIRST_BANKS, SECOND_BANKS = 4, 3
 
 COMBINE_TOKENS = [512,256,256]
 
@@ -58,16 +52,15 @@ def tile_routed_moe_kernel(tc, xT, w1, w2, gate, offs, pos1, pos2, out):
         lists = ctx.enter_context(tc.tile_pool(name="lists", bufs=1))
         held = ctx.enter_context(tc.tile_pool(name="held", bufs=1))
         load_pool = ctx.enter_context(tc.tile_pool(name="load_pool", bufs=LOAD_BUFS))
-        token_bf16_pool = ctx.enter_context(tc.tile_pool(name="token_bf16_pool", bufs=TOKEN_BF16_BUFS))
-        token_code_pool = ctx.enter_context(tc.tile_pool(name="token_code_pool", bufs=TOKEN_CODE_BUFS))
-        w1_bf16_pool = ctx.enter_context(tc.tile_pool(name="w1_bf16_pool", bufs=W1_BF16_BUFS))
+        by_scalar_pool = ctx.enter_context(tc.tile_pool(name="by_scalar_pool", bufs=BY_SCALAR_BUFS))
+        by_copy_pool = ctx.enter_context(tc.tile_pool(name="by_copy_pool", bufs=BY_COPY_BUFS))
         w1_code_pool = ctx.enter_context(tc.tile_pool(name="w1_code_pool", bufs=W1_CODE_BUFS))
-        w2_bf16_pool = ctx.enter_context(tc.tile_pool(name="w2_bf16_pool", bufs=W2_BF16_BUFS))
+        token_code_pool = ctx.enter_context(tc.tile_pool(name="token_code_pool", bufs=TOKEN_CODE_BUFS))
+        hidden_code_pool = ctx.enter_context(tc.tile_pool(name="hidden_code_pool", bufs=HIDDEN_CODE_BUFS))
         w2_code_pool = ctx.enter_context(tc.tile_pool(name="w2_code_pool", bufs=W2_CODE_BUFS))
-        hidden_pool = ctx.enter_context(tc.tile_pool(name="hidden_pool", bufs=HIDDEN_BUFS))
+        scale_pool = ctx.enter_context(tc.tile_pool(name="scale_pool", bufs=SCALE_BUFS))
         combine_pool = ctx.enter_context(tc.tile_pool(name="combine_pool", bufs=COMBINE_BUFS))
-        first_psum = ctx.enter_context(tc.psum_pool(name="first_psum", bufs=FIRST_BANKS))
-        second_psum = ctx.enter_context(tc.psum_pool(name="second_psum", bufs=SECOND_BANKS))
+        sums_pool = ctx.enter_context(tc.psum_pool(name="sums_pool", bufs=SUMS_BANKS))
 
         zero = held.tile([P, 1], F32, name="zero")
         unused = held.tile([P, 1], F32, name="unused")
@@ -82,16 +75,14 @@ def tile_routed_moe_kernel(tc, xT, w1, w2, gate, offs, pos1, pos2, out):
         rows_of_plane = xT.rearrange("(p j) n -> p j n", j=PACK)
         planes = []
         planes_bf16 = []
-
-        def load_planes():
-            for j in range(PACK):
-                plane = held.tile([P, T], F32, name="plane%d" % j)
-                nc.sync.dma_start(plane[:], rows_of_plane[:, j, :])
-                planes.append(plane)
-            for j in range(PACK):
-                plane_bf16 = held.tile([P, T], BF16, name="plane_bf16_%d" % j)
-                nc.vector.tensor_copy(out=plane_bf16[:], in_=planes[j][:])
-                planes_bf16.append(plane_bf16)
+        for j in range(PACK):
+            plane = held.tile([P, T], F32, name="plane%d" % j)
+            nc.sync.dma_start(plane[:], rows_of_plane[:, j, :])
+            planes.append(plane)
+        for j in range(PACK):
+            plane_bf16 = held.tile([P, T], BF16, name="plane_bf16_%d" % j)
+            nc.vector.tensor_copy(out=plane_bf16[:], in_=planes[j][:])
+            planes_bf16.append(plane_bf16)
 
         y_all = held.tile([P, SLOTS], F32, name="y_all")
 
@@ -106,86 +97,63 @@ def tile_routed_moe_kernel(tc, xT, w1, w2, gate, offs, pos1, pos2, out):
         stream.append(("lists", 0))
         stream.append(("gate", 0))
         loaded = {}
-        ring = {"next": 0, "in_use": 0}
-
-        def load_while_the_ring_has_room():
-            while ring["next"] < len(stream) and ring["in_use"] < LOAD_BUFS:
-                if ring["next"] == HEAD_LOADS:
-                    load_planes()
-                what, index = stream[ring["next"]]
-                ring["next"] += 1
-                if what == "lists":
-                    nc.sync.dma_start(pos1_sb[:], pos1)
-                    nc.sync.dma_start(pos2_sb[:], pos2)
-                    continue
-                ring["in_use"] += 1
-                if what == "w1":
-                    tile = load_pool.tile([P, PACK, H], F32, name="load")
-                    nc.sync.dma_start(tile[:], w1[index].rearrange("(p j) i -> p j i", j=PACK))
-                elif what == "w2":
-                    tile = load_pool.tile([P, W2_GROUP, PACK * N], F32, name="load")
-                    group = w2[index * W2_GROUP : (index + 1) * W2_GROUP]
-                    nc.sync.dma_start(tile[:], group.rearrange("e (p j) n -> p e (j n)", j=PACK))
-                else:
-                    tile = load_pool.tile([P, 2, T], F32, name="load")
-                    nc.sync.dma_start(tile[:], gate.rearrange("r n t -> n r t"))
-                loaded[(what, index)] = tile
+        for what, index in stream:
+            if what == "lists":
+                nc.sync.dma_start(pos1_sb[:], pos1)
+                nc.sync.dma_start(pos2_sb[:], pos2)
+            elif what == "w1":
+                loaded[(what, index)] = load_pool.tile([P, PACK, H], F32, name="load")
+                nc.sync.dma_start(loaded[(what, index)][:], w1[index].rearrange("(p j) i -> p j i", j=PACK))
+            elif what == "w2":
+                loaded[(what, index)] = load_pool.tile([P, W2_GROUP, PACK * N], F32, name="load")
+                group = w2[index * W2_GROUP : (index + 1) * W2_GROUP]
+                nc.sync.dma_start(loaded[(what, index)][:], group.rearrange("e (p j) n -> p e (j n)", j=PACK))
+            else:
+                loaded[(what, index)] = load_pool.tile([P, 2, T], F32, name="load")
+                nc.sync.dma_start(loaded[(what, index)][:], gate.rearrange("r n t -> n r t"))
 
         token_bf16, token_codes, token_scales = {}, {}, {}
         w1_bf16, w1_codes, w1_scales = {}, {}, {}
         w2_bf16, w2_codes, w2_scales = {}, {}, {}
         first_sums, hidden_bf16, hidden_codes, hidden_scales = {}, {}, {}, {}
 
-        def gather_tokens(c):
-            token_bf16[c] = token_bf16_pool.tile([P, CHUNK, PACK], BF16, name="token_bf16", align_bytes=64)
-            for a in range(CHUNK_EXPERTS):
-                e = c * CHUNK_EXPERTS + a
-                entries = offs_sb[:, e * (C // 16) : (e + 1) * (C // 16)]
-                for j in range(PACK):
-                    nc.scalar.activation(
-                        out=token_bf16[c][:, a * C : (a + 1) * C, j], in_=planes_bf16[j][:].indirect(entries), func=COPY
-                    )
+        def gather_tokens(e):
+            token_bf16[e] = by_scalar_pool.tile([P, C, PACK], BF16, name="by_scalar", align_bytes=64)
+            entries = offs_sb[:, e * (C // 16) : (e + 1) * (C // 16)]
+            for j in range(PACK):
+                nc.scalar.activation(out=token_bf16[e][:, :, j], in_=planes_bf16[j][:].indirect(entries), func=COPY)
 
-        def quantize_tokens(c):
-            token_codes[c] = token_code_pool.tile([P, CHUNK], U32, name="token_codes", align_bytes=64)
-            token_scales[c] = token_code_pool.tile([P, CHUNK], U8, name="token_scales", align_bytes=64)
+        def quantize_tokens(e):
+            token_codes[e] = token_code_pool.tile([P, C], U32, name="token_codes", align_bytes=64)
+            token_scales[e] = scale_pool.tile([P, C], U8, name="scales", align_bytes=64)
             nc.vector.quantize_mx(
-                out=token_codes[c][:].bitcast(FP8X4),
-                scales=token_scales[c][:],
-                in_=token_bf16[c][:].rearrange("p s j -> p (s j)"),
+                out=token_codes[e][:].bitcast(FP8X4),
+                scales=token_scales[e][:],
+                in_=token_bf16[e][:].rearrange("p s j -> p (s j)"),
             )
 
         def interleave_w1(e):
-            w1_bf16[e] = w1_bf16_pool.tile([P, PACK * H], BF16, name="w1_bf16", align_bytes=64)
-            dst = w1_bf16[e][:].rearrange("p (t m j) -> p m j t", t=4, j=PACK)
-            src = loaded[("w1", e)][:].rearrange("p j (m t) -> p m j t", t=4)
-            nc.vector.tensor_copy(out=dst, in_=src)
-            ring["in_use"] -= 1
+            w1_bf16[e] = by_copy_pool.tile([P, PACK * H], BF16, name="by_copy", align_bytes=64)
+            nc.vector.tensor_copy(
+                out=w1_bf16[e][:].rearrange("p (t m j) -> p m j t", t=4, j=PACK),
+                in_=loaded[("w1", e)][:].rearrange("p j (m t) -> p m j t", t=4),
+            )
 
         def quantize_w1(e):
             w1_codes[e] = w1_code_pool.tile([P, H], U32, name="w1_codes", align_bytes=64)
-            w1_scales[e] = w1_code_pool.tile([P, H], U8, name="w1_scales", align_bytes=64)
+            w1_scales[e] = scale_pool.tile([P, H], U8, name="scales", align_bytes=64)
             nc.vector.quantize_mx(out=w1_codes[e][:].bitcast(FP8X4), scales=w1_scales[e][:], in_=w1_bf16[e][:])
 
-        def interleave_w2(q, step):
-            if step == 0:
-                w2_bf16[q] = w2_bf16_pool.tile([P, W2_GROUP, N, PACK], BF16, name="w2_bf16", align_bytes=64)
-                for a in range(W2_ON_SCALAR):
-                    nc.scalar.copy(
-                        out=w2_bf16[q][:, a, :, :].rearrange("p (n i) j -> p n j i", i=4),
-                        in_=loaded[("w2", q)][:, a, :].rearrange("p (j n i) -> p n j i", j=PACK, i=4),
-                    )
-            else:
-                if W2_ON_SCALAR < W2_GROUP:
-                    nc.vector.tensor_copy(
-                        out=w2_bf16[q][:, W2_ON_SCALAR:W2_GROUP, :, :].rearrange("p a (n i) j -> p a n j i", i=4),
-                        in_=loaded[("w2", q)][:, W2_ON_SCALAR:W2_GROUP, :].rearrange("p a (j n i) -> p a n j i", j=PACK, i=4),
-                    )
-                ring["in_use"] -= 1
+        def interleave_w2(q):
+            w2_bf16[q] = by_copy_pool.tile([P, W2_GROUP, N, PACK], BF16, name="by_copy", align_bytes=64)
+            nc.vector.tensor_copy(
+                out=w2_bf16[q][:].rearrange("p a (n i) j -> p a n j i", i=4),
+                in_=loaded[("w2", q)][:].rearrange("p a (j n i) -> p a n j i", j=PACK, i=4),
+            )
 
         def quantize_w2(q):
             w2_codes[q] = w2_code_pool.tile([P, W2_GROUP * N], U32, name="w2_codes", align_bytes=64)
-            w2_scales[q] = w2_code_pool.tile([P, W2_GROUP * N], U8, name="w2_scales", align_bytes=64)
+            w2_scales[q] = scale_pool.tile([P, W2_GROUP * N], U8, name="scales", align_bytes=64)
             nc.vector.quantize_mx(
                 out=w2_codes[q][:].bitcast(FP8X4),
                 scales=w2_scales[q][:],
@@ -193,15 +161,14 @@ def tile_routed_moe_kernel(tc, xT, w1, w2, gate, offs, pos1, pos2, out):
             )
 
         def first_layer(e):
-            c, a = e // CHUNK_EXPERTS, e % CHUNK_EXPERTS
-            first_sums[e] = first_psum.tile([P, 4, C], F32, name="first_sums")
+            first_sums[e] = sums_pool.tile([P, 4, C], F32, name="sums")
             for t in range(4):
                 nc.tensor.matmul_mx(
                     out=first_sums[e][:, t, :],
                     lhsT=w1_codes[e][:, t * P : (t + 1) * P].bitcast(FP8X4),
                     lhsT_scale=w1_scales[e][:, t * P : (t + 1) * P],
-                    rhs=token_codes[c][:, a * C : (a + 1) * C].bitcast(FP8X4),
-                    rhs_scale=token_scales[c][:, a * C : (a + 1) * C],
+                    rhs=token_codes[e][:].bitcast(FP8X4),
+                    rhs_scale=token_scales[e][:],
                     start=True,
                     stop=True,
                 )
@@ -209,20 +176,20 @@ def tile_routed_moe_kernel(tc, xT, w1, w2, gate, offs, pos1, pos2, out):
         def gelu(e):
             k, b = e // PAIR, e % PAIR
             if b == 0:
-                hidden_bf16[k] = hidden_pool.tile([P, PAIR, C, PACK], BF16, name="hidden_bf16", align_bytes=64)
+                hidden_bf16[k] = by_scalar_pool.tile([P, PAIR, C, PACK], BF16, name="by_scalar", align_bytes=64)
             nc.scalar.activation(
                 out=hidden_bf16[k][:, b, :, :], in_=first_sums[e][:].rearrange("p t s -> p s t"), func=GELU
             )
 
         def second_layer(k):
-            hidden_codes[k] = hidden_pool.tile([P, PAIR * C], U32, name="hidden_codes", align_bytes=64)
-            hidden_scales[k] = hidden_pool.tile([P, PAIR * C], U8, name="hidden_scales", align_bytes=64)
+            hidden_codes[k] = hidden_code_pool.tile([P, PAIR * C], U32, name="hidden_codes", align_bytes=64)
+            hidden_scales[k] = scale_pool.tile([P, PAIR * C], U8, name="scales", align_bytes=64)
             nc.vector.quantize_mx(
                 out=hidden_codes[k][:].bitcast(FP8X4),
                 scales=hidden_scales[k][:],
                 in_=hidden_bf16[k][:].rearrange("p b s t -> p (b s t)"),
             )
-            second_sums = second_psum.tile([P, PAIR * C], F32, name="second_sums")
+            second_sums = sums_pool.tile([P, PAIR * C], F32, name="sums")
             for b in range(PAIR):
                 e = PAIR * k + b
                 q, a = e // W2_GROUP, e % W2_GROUP
@@ -241,31 +208,25 @@ def tile_routed_moe_kernel(tc, xT, w1, w2, gate, offs, pos1, pos2, out):
             else:
                 nc.scalar.copy(out=y_slots, in_=second_sums[:])
 
-        load_while_the_ring_has_room()
         for tick in range(FIRST_TICK, LAST_TICK + 1):
             if tick >= SECOND_LAG and (tick - SECOND_LAG) % PAIR == 0:
                 second_layer((tick - SECOND_LAG) // PAIR)
-            if 0 <= tick - GELU_LAG < E:
-                gelu(tick - GELU_LAG)
-            if 0 <= tick + COPY_LEAD < E:
-                interleave_w1(tick + COPY_LEAD)
+            if 0 <= tick + TOKEN_AHEAD < E:
+                quantize_tokens(tick + TOKEN_AHEAD)
             if 0 <= tick < E:
                 quantize_w1(tick)
-            for c in range(CHUNKS):
-                if tick == CHUNK_EXPERTS * c - QT_AHEAD:
-                    quantize_tokens(c)
-            if 0 <= tick < E:
                 first_layer(tick)
+            if 0 <= tick - GELU_LAG < E:
+                gelu(tick - GELU_LAG)
+            if 0 <= tick + GATHER_AHEAD < E:
+                gather_tokens(tick + GATHER_AHEAD)
             for q in range(E // W2_GROUP):
-                for step in range(2):
-                    if tick == W2_GROUP * q - W2_COPY_AHEAD + step:
-                        interleave_w2(q, step)
                 if tick == W2_GROUP * q + W2_QUANT_LAG:
                     quantize_w2(q)
-            for c in range(CHUNKS):
-                if tick == max(CHUNK_EXPERTS * c - X_AHEAD, FIRST_TICK):
-                    gather_tokens(c)
-            load_while_the_ring_has_room()
+                if tick == W2_GROUP * q - W2_COPY_AHEAD:
+                    interleave_w2(q)
+            if 0 <= tick + COPY_AHEAD < E:
+                interleave_w1(tick + COPY_AHEAD)
 
         gate_sb = loaded[("gate", 0)]
         products = []

@@ -27,7 +27,10 @@ TOKEN_AHEAD = 1
 COPY_AHEAD = 1
 GELU_LAG = 0
 SECOND_LAG = 3
-W2_COPY_AHEAD = 1
+W2_ON_SCALAR = 2
+EARLY_GROUPS = 128
+LATE_GROUPS = 128
+LATE_FROM = 12
 W2_QUANT_LAG = 1
 FIRST_TICK = -GATHER_AHEAD
 LAST_TICK = E - PAIR + SECOND_LAG
@@ -134,10 +137,12 @@ def tile_routed_moe_kernel(tc, xT, w1, w2, gate, offs, pos1, pos2, out):
 
         def interleave_w1(e):
             w1_bf16[e] = by_copy_pool.tile([P, PACK * H], BF16, name="by_copy", align_bytes=64)
-            nc.vector.tensor_copy(
-                out=w1_bf16[e][:].rearrange("p (t m j) -> p m j t", t=4, j=PACK),
-                in_=loaded[("w1", e)][:].rearrange("p j (m t) -> p m j t", t=4),
-            )
+            dst = w1_bf16[e][:].rearrange("p (t m j) -> p m j t", t=4, j=PACK)
+            src = loaded[("w1", e)][:].rearrange("p j (m t) -> p m j t", t=4)
+            split = EARLY_GROUPS if e < LATE_FROM else LATE_GROUPS
+            if split < P:
+                nc.scalar.copy(out=dst[:, split:P, :, :], in_=src[:, split:P, :, :])
+            nc.vector.tensor_copy(out=dst[:, 0:split, :, :], in_=src[:, 0:split, :, :])
 
         def quantize_w1(e):
             w1_codes[e] = w1_code_pool.tile([P, H], U32, name="w1_codes", align_bytes=64)
@@ -146,10 +151,16 @@ def tile_routed_moe_kernel(tc, xT, w1, w2, gate, offs, pos1, pos2, out):
 
         def interleave_w2(q):
             w2_bf16[q] = by_copy_pool.tile([P, W2_GROUP, N, PACK], BF16, name="by_copy", align_bytes=64)
-            nc.vector.tensor_copy(
-                out=w2_bf16[q][:].rearrange("p a (n i) j -> p a n j i", i=4),
-                in_=loaded[("w2", q)][:].rearrange("p a (j n i) -> p a n j i", j=PACK, i=4),
-            )
+            for a in range(W2_ON_SCALAR):
+                nc.scalar.copy(
+                    out=w2_bf16[q][:, a, :, :].rearrange("p (n i) j -> p n j i", i=4),
+                    in_=loaded[("w2", q)][:, a, :].rearrange("p (j n i) -> p n j i", j=PACK, i=4),
+                )
+            if W2_ON_SCALAR < W2_GROUP:
+                nc.vector.tensor_copy(
+                    out=w2_bf16[q][:, W2_ON_SCALAR:W2_GROUP, :, :].rearrange("p a (n i) j -> p a n j i", i=4),
+                    in_=loaded[("w2", q)][:, W2_ON_SCALAR:W2_GROUP, :].rearrange("p a (j n i) -> p a n j i", j=PACK, i=4),
+                )
 
         def quantize_w2(q):
             w2_codes[q] = w2_code_pool.tile([P, W2_GROUP * N], U32, name="w2_codes", align_bytes=64)
@@ -209,13 +220,13 @@ def tile_routed_moe_kernel(tc, xT, w1, w2, gate, offs, pos1, pos2, out):
                 nc.scalar.copy(out=y_slots, in_=second_sums[:])
 
         for tick in range(FIRST_TICK, LAST_TICK + 1):
-            if tick >= SECOND_LAG and (tick - SECOND_LAG) % PAIR == 0:
-                second_layer((tick - SECOND_LAG) // PAIR)
             if 0 <= tick + TOKEN_AHEAD < E:
                 quantize_tokens(tick + TOKEN_AHEAD)
             if 0 <= tick < E:
                 quantize_w1(tick)
                 first_layer(tick)
+            if tick >= SECOND_LAG and (tick - SECOND_LAG) % PAIR == 0:
+                second_layer((tick - SECOND_LAG) // PAIR)
             if 0 <= tick - GELU_LAG < E:
                 gelu(tick - GELU_LAG)
             if 0 <= tick + GATHER_AHEAD < E:
@@ -223,9 +234,10 @@ def tile_routed_moe_kernel(tc, xT, w1, w2, gate, offs, pos1, pos2, out):
             for q in range(E // W2_GROUP):
                 if tick == W2_GROUP * q + W2_QUANT_LAG:
                     quantize_w2(q)
-                if tick == W2_GROUP * q - W2_COPY_AHEAD:
-                    interleave_w2(q)
             if 0 <= tick + COPY_AHEAD < E:
+                before = stream[stream.index(("w1", tick + COPY_AHEAD)) - 1]
+                if before[0] == "w2":
+                    interleave_w2(before[1])
                 interleave_w1(tick + COPY_AHEAD)
 
         gate_sb = loaded[("gate", 0)]

@@ -20,29 +20,27 @@ SLOTS = E * C
 FLOPS = 2 * SLOTS * K * H + 2 * SLOTS * H * N
 
 W2_GROUP = 4
-PAIR = 2
 
 GATHER_AHEAD = 4
 TOKEN_AHEAD = 1
-COPY_AHEAD = 1
 GELU_LAG = 0
-SECOND_LAG = 3
+SECOND_LAG = 2
 W2_ON_SCALAR = 2
 EARLY_GROUPS = 128
 LATE_GROUPS = 128
 LATE_FROM = 12
 W2_QUANT_LAG = 1
 FIRST_TICK = -GATHER_AHEAD
-LAST_TICK = E - PAIR + SECOND_LAG
+LAST_TICK = E - 1 + SECOND_LAG
 
 LOAD_BUFS = 9
-BY_SCALAR_BUFS = 8
-BY_COPY_BUFS = 4
+BY_SCALAR_BUFS = 12
+BY_VECTOR_BUFS = 16
+LAST_GROUPS_FROM = 3
 W1_CODE_BUFS = 4
 TOKEN_CODE_BUFS = 4
-HIDDEN_CODE_BUFS = 3
+HIDDEN_CODE_BUFS = 6
 W2_CODE_BUFS = 2
-SCALE_BUFS = 12
 SUMS_BANKS = 8
 COMBINE_BUFS = 3
 
@@ -56,12 +54,11 @@ def tile_routed_moe_kernel(tc, xT, w1, w2, gate, offs, pos1, pos2, out):
         held = ctx.enter_context(tc.tile_pool(name="held", bufs=1))
         load_pool = ctx.enter_context(tc.tile_pool(name="load_pool", bufs=LOAD_BUFS))
         by_scalar_pool = ctx.enter_context(tc.tile_pool(name="by_scalar_pool", bufs=BY_SCALAR_BUFS))
-        by_copy_pool = ctx.enter_context(tc.tile_pool(name="by_copy_pool", bufs=BY_COPY_BUFS))
+        by_vector_pool = ctx.enter_context(tc.tile_pool(name="by_vector_pool", bufs=BY_VECTOR_BUFS))
         w1_code_pool = ctx.enter_context(tc.tile_pool(name="w1_code_pool", bufs=W1_CODE_BUFS))
         token_code_pool = ctx.enter_context(tc.tile_pool(name="token_code_pool", bufs=TOKEN_CODE_BUFS))
         hidden_code_pool = ctx.enter_context(tc.tile_pool(name="hidden_code_pool", bufs=HIDDEN_CODE_BUFS))
         w2_code_pool = ctx.enter_context(tc.tile_pool(name="w2_code_pool", bufs=W2_CODE_BUFS))
-        scale_pool = ctx.enter_context(tc.tile_pool(name="scale_pool", bufs=SCALE_BUFS))
         combine_pool = ctx.enter_context(tc.tile_pool(name="combine_pool", bufs=COMBINE_BUFS))
         sums_pool = ctx.enter_context(tc.psum_pool(name="sums_pool", bufs=SUMS_BANKS))
 
@@ -93,10 +90,12 @@ def tile_routed_moe_kernel(tc, xT, w1, w2, gate, offs, pos1, pos2, out):
         for e in range(E):
             if e == 0:
                 stream.append(("w1", 0))
-            if e % W2_GROUP == 0:
+            if e % W2_GROUP == 0 and e // W2_GROUP < LAST_GROUPS_FROM:
                 stream.append(("w2", e // W2_GROUP))
             if e > 0:
                 stream.append(("w1", e))
+        for q in range(LAST_GROUPS_FROM, E // W2_GROUP):
+            stream.append(("w2", q))
         stream.append(("lists", 0))
         stream.append(("gate", 0))
         loaded = {}
@@ -128,7 +127,7 @@ def tile_routed_moe_kernel(tc, xT, w1, w2, gate, offs, pos1, pos2, out):
 
         def quantize_tokens(e):
             token_codes[e] = token_code_pool.tile([P, C], U32, name="token_codes", align_bytes=64)
-            token_scales[e] = scale_pool.tile([P, C], U8, name="scales", align_bytes=64)
+            token_scales[e] = by_vector_pool.tile([P, C], U8, name="by_vector", align_bytes=64)
             nc.vector.quantize_mx(
                 out=token_codes[e][:].bitcast(FP8X4),
                 scales=token_scales[e][:],
@@ -136,35 +135,36 @@ def tile_routed_moe_kernel(tc, xT, w1, w2, gate, offs, pos1, pos2, out):
             )
 
         def interleave_w1(e):
-            w1_bf16[e] = by_copy_pool.tile([P, PACK * H], BF16, name="by_copy", align_bytes=64)
+            w1_bf16[e] = by_vector_pool.tile([P, PACK * H], BF16, name="by_vector", align_bytes=64)
             dst = w1_bf16[e][:].rearrange("p (t m j) -> p m j t", t=4, j=PACK)
             src = loaded[("w1", e)][:].rearrange("p j (m t) -> p m j t", t=4)
             split = EARLY_GROUPS if e < LATE_FROM else LATE_GROUPS
+            nc.vector.tensor_copy(out=dst[:, 0:split, :, :], in_=src[:, 0:split, :, :])
             if split < P:
                 nc.scalar.copy(out=dst[:, split:P, :, :], in_=src[:, split:P, :, :])
-            nc.vector.tensor_copy(out=dst[:, 0:split, :, :], in_=src[:, 0:split, :, :])
 
         def quantize_w1(e):
             w1_codes[e] = w1_code_pool.tile([P, H], U32, name="w1_codes", align_bytes=64)
-            w1_scales[e] = scale_pool.tile([P, H], U8, name="scales", align_bytes=64)
+            w1_scales[e] = by_vector_pool.tile([P, H], U8, name="by_vector", align_bytes=64)
             nc.vector.quantize_mx(out=w1_codes[e][:].bitcast(FP8X4), scales=w1_scales[e][:], in_=w1_bf16[e][:])
 
         def interleave_w2(q):
-            w2_bf16[q] = by_copy_pool.tile([P, W2_GROUP, N, PACK], BF16, name="by_copy", align_bytes=64)
-            for a in range(W2_ON_SCALAR):
+            w2_bf16[q] = by_vector_pool.tile([P, W2_GROUP, N, PACK], BF16, name="by_vector", align_bytes=64)
+            on_scalar = W2_ON_SCALAR if q < LAST_GROUPS_FROM else 0
+            if on_scalar < W2_GROUP:
+                nc.vector.tensor_copy(
+                    out=w2_bf16[q][:, on_scalar:W2_GROUP, :, :].rearrange("p a (n i) j -> p a n j i", i=4),
+                    in_=loaded[("w2", q)][:, on_scalar:W2_GROUP, :].rearrange("p a (j n i) -> p a n j i", j=PACK, i=4),
+                )
+            for a in range(on_scalar):
                 nc.scalar.copy(
                     out=w2_bf16[q][:, a, :, :].rearrange("p (n i) j -> p n j i", i=4),
                     in_=loaded[("w2", q)][:, a, :].rearrange("p (j n i) -> p n j i", j=PACK, i=4),
                 )
-            if W2_ON_SCALAR < W2_GROUP:
-                nc.vector.tensor_copy(
-                    out=w2_bf16[q][:, W2_ON_SCALAR:W2_GROUP, :, :].rearrange("p a (n i) j -> p a n j i", i=4),
-                    in_=loaded[("w2", q)][:, W2_ON_SCALAR:W2_GROUP, :].rearrange("p a (j n i) -> p a n j i", j=PACK, i=4),
-                )
 
         def quantize_w2(q):
             w2_codes[q] = w2_code_pool.tile([P, W2_GROUP * N], U32, name="w2_codes", align_bytes=64)
-            w2_scales[q] = scale_pool.tile([P, W2_GROUP * N], U8, name="scales", align_bytes=64)
+            w2_scales[q] = by_vector_pool.tile([P, W2_GROUP * N], U8, name="by_vector", align_bytes=64)
             nc.vector.quantize_mx(
                 out=w2_codes[q][:].bitcast(FP8X4),
                 scales=w2_scales[q][:],
@@ -185,60 +185,68 @@ def tile_routed_moe_kernel(tc, xT, w1, w2, gate, offs, pos1, pos2, out):
                 )
 
         def gelu(e):
-            k, b = e // PAIR, e % PAIR
-            if b == 0:
-                hidden_bf16[k] = by_scalar_pool.tile([P, PAIR, C, PACK], BF16, name="by_scalar", align_bytes=64)
-            nc.scalar.activation(
-                out=hidden_bf16[k][:, b, :, :], in_=first_sums[e][:].rearrange("p t s -> p s t"), func=GELU
+            hidden_bf16[e] = by_scalar_pool.tile([P, C, PACK], BF16, name="by_scalar", align_bytes=64)
+            nc.scalar.activation(out=hidden_bf16[e][:], in_=first_sums[e][:].rearrange("p t s -> p s t"), func=GELU)
+
+        def quantize_hidden(e):
+            hidden_codes[e] = hidden_code_pool.tile([P, C], U32, name="hidden_codes", align_bytes=64)
+            hidden_scales[e] = by_vector_pool.tile([P, C], U8, name="by_vector", align_bytes=64)
+            nc.vector.quantize_mx(
+                out=hidden_codes[e][:].bitcast(FP8X4),
+                scales=hidden_scales[e][:],
+                in_=hidden_bf16[e][:].rearrange("p s t -> p (s t)"),
             )
 
-        def second_layer(k):
-            hidden_codes[k] = hidden_code_pool.tile([P, PAIR * C], U32, name="hidden_codes", align_bytes=64)
-            hidden_scales[k] = scale_pool.tile([P, PAIR * C], U8, name="scales", align_bytes=64)
-            nc.vector.quantize_mx(
-                out=hidden_codes[k][:].bitcast(FP8X4),
-                scales=hidden_scales[k][:],
-                in_=hidden_bf16[k][:].rearrange("p b s t -> p (b s t)"),
+        def second_layer(e):
+            second_sums = sums_pool.tile([P, C], F32, name="sums")
+            q, a = e // W2_GROUP, e % W2_GROUP
+            nc.tensor.matmul_mx(
+                out=second_sums[:],
+                lhsT=w2_codes[q][:, a * N : (a + 1) * N].bitcast(FP8X4),
+                lhsT_scale=w2_scales[q][:, a * N : (a + 1) * N],
+                rhs=hidden_codes[e][:].bitcast(FP8X4),
+                rhs_scale=hidden_scales[e][:],
+                start=True,
+                stop=True,
             )
-            second_sums = sums_pool.tile([P, PAIR * C], F32, name="sums")
-            for b in range(PAIR):
-                e = PAIR * k + b
-                q, a = e // W2_GROUP, e % W2_GROUP
-                nc.tensor.matmul_mx(
-                    out=second_sums[:, b * C : (b + 1) * C],
-                    lhsT=w2_codes[q][:, a * N : (a + 1) * N].bitcast(FP8X4),
-                    lhsT_scale=w2_scales[q][:, a * N : (a + 1) * N],
-                    rhs=hidden_codes[k][:, b * C : (b + 1) * C].bitcast(FP8X4),
-                    rhs_scale=hidden_scales[k][:, b * C : (b + 1) * C],
-                    start=True,
-                    stop=True,
-                )
-            y_slots = y_all[:, PAIR * k * C : PAIR * (k + 1) * C]
-            if k == E // PAIR - 1:
+            y_slots = y_all[:, e * C : (e + 1) * C]
+            if e == E - 1:
                 nc.vector.tensor_copy(out=y_slots, in_=second_sums[:])
             else:
                 nc.scalar.copy(out=y_slots, in_=second_sums[:])
 
+        due = []
+        w2_copied_at = {}
         for tick in range(FIRST_TICK, LAST_TICK + 1):
+            if 0 <= tick < E:
+                before = stream[stream.index(("w1", tick)) - 1]
+                if before[0] == "w2":
+                    interleave_w2(before[1])
+                    w2_copied_at[before[1]] = tick
+                interleave_w1(tick)
+            if tick == E:
+                for q in range(LAST_GROUPS_FROM, E // W2_GROUP):
+                    interleave_w2(q)
+                    w2_copied_at[q] = tick
             if 0 <= tick + TOKEN_AHEAD < E:
                 quantize_tokens(tick + TOKEN_AHEAD)
+            if 0 <= tick - SECOND_LAG < E:
+                quantize_hidden(tick - SECOND_LAG)
+                due.append(tick - SECOND_LAG)
+            for q in range(E // W2_GROUP):
+                if q in w2_copied_at and tick == w2_copied_at[q] + W2_QUANT_LAG:
+                    quantize_w2(q)
             if 0 <= tick < E:
                 quantize_w1(tick)
                 first_layer(tick)
-            if tick >= SECOND_LAG and (tick - SECOND_LAG) % PAIR == 0:
-                second_layer((tick - SECOND_LAG) // PAIR)
+            for e in list(due):
+                if e // W2_GROUP in w2_codes:
+                    second_layer(e)
+                    due.remove(e)
             if 0 <= tick - GELU_LAG < E:
                 gelu(tick - GELU_LAG)
             if 0 <= tick + GATHER_AHEAD < E:
                 gather_tokens(tick + GATHER_AHEAD)
-            for q in range(E // W2_GROUP):
-                if tick == W2_GROUP * q + W2_QUANT_LAG:
-                    quantize_w2(q)
-            if 0 <= tick + COPY_AHEAD < E:
-                before = stream[stream.index(("w1", tick + COPY_AHEAD)) - 1]
-                if before[0] == "w2":
-                    interleave_w2(before[1])
-                interleave_w1(tick + COPY_AHEAD)
 
         gate_sb = loaded[("gate", 0)]
         products = []

@@ -19,7 +19,11 @@ K, T, E, C, H, N = 512, 1024, 16, 128, 512, 128
 SLOTS = E * C
 FLOPS = 2 * SLOTS * K * H + 2 * SLOTS * H * N
 
-W2_GROUP = 4
+W2_UNITS = [(0, 4), (4, 4), (8, 4), (12, 2), (14, 2)]
+TRAILING = 2
+LEADING = len(W2_UNITS) - TRAILING
+TRAILING_ON_SCALAR = [2, 0, 0, 0]
+W1_LAST_PIECES = 2
 
 GATHER_AHEAD = 4
 TOKEN_AHEAD = 1
@@ -31,16 +35,15 @@ LATE_GROUPS = 128
 LATE_FROM = 12
 W2_QUANT_LAG = 1
 FIRST_TICK = -GATHER_AHEAD
-LAST_TICK = E - 1 + SECOND_LAG
+LAST_TICK = E - 1 + max(SECOND_LAG, TRAILING)
 
 LOAD_BUFS = 9
 BY_SCALAR_BUFS = 12
 BY_VECTOR_BUFS = 16
-LAST_GROUPS_FROM = 3
 W1_CODE_BUFS = 4
 TOKEN_CODE_BUFS = 4
 HIDDEN_CODE_BUFS = 6
-W2_CODE_BUFS = 2
+W2_CODE_BUFS = 3
 SUMS_BANKS = 8
 COMBINE_BUFS = 3
 
@@ -86,18 +89,24 @@ def tile_routed_moe_kernel(tc, xT, w1, w2, gate, offs, pos1, pos2, out):
 
         y_all = held.tile([P, SLOTS], F32, name="y_all")
 
+        unit_of = {}
+        for u in range(len(W2_UNITS)):
+            for a in range(W2_UNITS[u][1]):
+                unit_of[W2_UNITS[u][0] + a] = u
         stream = []
         for e in range(E):
             if e == 0:
                 stream.append(("w1", 0))
-            if e % W2_GROUP == 0 and e // W2_GROUP < LAST_GROUPS_FROM:
-                stream.append(("w2", e // W2_GROUP))
+            for u in range(LEADING):
+                if W2_UNITS[u][0] == e:
+                    stream.append(("w2", u))
             if e > 0:
                 stream.append(("w1", e))
-        for q in range(LAST_GROUPS_FROM, E // W2_GROUP):
-            stream.append(("w2", q))
+        for u in range(LEADING, len(W2_UNITS)):
+            stream.append(("w2", u))
         stream.append(("lists", 0))
-        stream.append(("gate", 0))
+        for step in range(len(COMBINE_TOKENS)):
+            stream.append(("gate", step))
         loaded = {}
         for what, index in stream:
             if what == "lists":
@@ -107,12 +116,15 @@ def tile_routed_moe_kernel(tc, xT, w1, w2, gate, offs, pos1, pos2, out):
                 loaded[(what, index)] = load_pool.tile([P, PACK, H], F32, name="load")
                 nc.sync.dma_start(loaded[(what, index)][:], w1[index].rearrange("(p j) i -> p j i", j=PACK))
             elif what == "w2":
-                loaded[(what, index)] = load_pool.tile([P, W2_GROUP, PACK * N], F32, name="load")
-                group = w2[index * W2_GROUP : (index + 1) * W2_GROUP]
-                nc.sync.dma_start(loaded[(what, index)][:], group.rearrange("e (p j) n -> p e (j n)", j=PACK))
+                first, count = W2_UNITS[index]
+                loaded[(what, index)] = load_pool.tile([P, count, PACK * N], F32, name="load")
+                nc.sync.dma_start(
+                    loaded[(what, index)][:], w2[first : first + count].rearrange("e (p j) n -> p e (j n)", j=PACK)
+                )
             else:
-                loaded[(what, index)] = load_pool.tile([P, 2, T], F32, name="load")
-                nc.sync.dma_start(loaded[(what, index)][:], gate.rearrange("r n t -> n r t"))
+                tokens = slice(sum(COMBINE_TOKENS[:index]), sum(COMBINE_TOKENS[: index + 1]))
+                loaded[(what, index)] = load_pool.tile([P, 2, COMBINE_TOKENS[index]], F32, name="load")
+                nc.sync.dma_start(loaded[(what, index)][:], gate[:, :, tokens].rearrange("r n t -> n r t"))
 
         token_bf16, token_codes, token_scales = {}, {}, {}
         w1_bf16, w1_codes, w1_scales = {}, {}, {}
@@ -146,29 +158,39 @@ def tile_routed_moe_kernel(tc, xT, w1, w2, gate, offs, pos1, pos2, out):
         def quantize_w1(e):
             w1_codes[e] = w1_code_pool.tile([P, H], U32, name="w1_codes", align_bytes=64)
             w1_scales[e] = by_vector_pool.tile([P, H], U8, name="by_vector", align_bytes=64)
-            nc.vector.quantize_mx(out=w1_codes[e][:].bitcast(FP8X4), scales=w1_scales[e][:], in_=w1_bf16[e][:])
+            pieces = W1_LAST_PIECES if e == E - 1 else 1
+            width = H // pieces
+            for piece in range(pieces):
+                columns = slice(piece * width, (piece + 1) * width)
+                nc.vector.quantize_mx(
+                    out=w1_codes[e][:, columns].bitcast(FP8X4),
+                    scales=w1_scales[e][:, columns],
+                    in_=w1_bf16[e][:, PACK * columns.start : PACK * columns.stop],
+                )
 
-        def interleave_w2(q):
-            w2_bf16[q] = by_vector_pool.tile([P, W2_GROUP, N, PACK], BF16, name="by_vector", align_bytes=64)
-            on_scalar = W2_ON_SCALAR if q < LAST_GROUPS_FROM else 0
-            if on_scalar < W2_GROUP:
+        def interleave_w2(u):
+            count = W2_UNITS[u][1]
+            w2_bf16[u] = by_vector_pool.tile([P, count, N, PACK], BF16, name="by_vector", align_bytes=64)
+            on_scalar = min(W2_ON_SCALAR if u < LEADING else TRAILING_ON_SCALAR[u - LEADING], count)
+            if on_scalar < count:
                 nc.vector.tensor_copy(
-                    out=w2_bf16[q][:, on_scalar:W2_GROUP, :, :].rearrange("p a (n i) j -> p a n j i", i=4),
-                    in_=loaded[("w2", q)][:, on_scalar:W2_GROUP, :].rearrange("p a (j n i) -> p a n j i", j=PACK, i=4),
+                    out=w2_bf16[u][:, on_scalar:count, :, :].rearrange("p a (n i) j -> p a n j i", i=4),
+                    in_=loaded[("w2", u)][:, on_scalar:count, :].rearrange("p a (j n i) -> p a n j i", j=PACK, i=4),
                 )
             for a in range(on_scalar):
                 nc.scalar.copy(
-                    out=w2_bf16[q][:, a, :, :].rearrange("p (n i) j -> p n j i", i=4),
-                    in_=loaded[("w2", q)][:, a, :].rearrange("p (j n i) -> p n j i", j=PACK, i=4),
+                    out=w2_bf16[u][:, a, :, :].rearrange("p (n i) j -> p n j i", i=4),
+                    in_=loaded[("w2", u)][:, a, :].rearrange("p (j n i) -> p n j i", j=PACK, i=4),
                 )
 
-        def quantize_w2(q):
-            w2_codes[q] = w2_code_pool.tile([P, W2_GROUP * N], U32, name="w2_codes", align_bytes=64)
-            w2_scales[q] = by_vector_pool.tile([P, W2_GROUP * N], U8, name="by_vector", align_bytes=64)
+        def quantize_w2(u):
+            count = W2_UNITS[u][1]
+            w2_codes[u] = w2_code_pool.tile([P, count * N], U32, name="w2_codes", align_bytes=64)
+            w2_scales[u] = by_vector_pool.tile([P, count * N], U8, name="by_vector", align_bytes=64)
             nc.vector.quantize_mx(
-                out=w2_codes[q][:].bitcast(FP8X4),
-                scales=w2_scales[q][:],
-                in_=w2_bf16[q][:].rearrange("p a n j -> p (a n j)"),
+                out=w2_codes[u][:].bitcast(FP8X4),
+                scales=w2_scales[u][:],
+                in_=w2_bf16[u][:].rearrange("p a n j -> p (a n j)"),
             )
 
         def first_layer(e):
@@ -199,48 +221,45 @@ def tile_routed_moe_kernel(tc, xT, w1, w2, gate, offs, pos1, pos2, out):
 
         def second_layer(e):
             second_sums = sums_pool.tile([P, C], F32, name="sums")
-            q, a = e // W2_GROUP, e % W2_GROUP
+            u = unit_of[e]
+            a = e - W2_UNITS[u][0]
             nc.tensor.matmul_mx(
                 out=second_sums[:],
-                lhsT=w2_codes[q][:, a * N : (a + 1) * N].bitcast(FP8X4),
-                lhsT_scale=w2_scales[q][:, a * N : (a + 1) * N],
+                lhsT=w2_codes[u][:, a * N : (a + 1) * N].bitcast(FP8X4),
+                lhsT_scale=w2_scales[u][:, a * N : (a + 1) * N],
                 rhs=hidden_codes[e][:].bitcast(FP8X4),
                 rhs_scale=hidden_scales[e][:],
                 start=True,
                 stop=True,
             )
-            y_slots = y_all[:, e * C : (e + 1) * C]
-            if e == E - 1:
-                nc.vector.tensor_copy(out=y_slots, in_=second_sums[:])
-            else:
-                nc.scalar.copy(out=y_slots, in_=second_sums[:])
+            nc.scalar.copy(out=y_all[:, e * C : (e + 1) * C], in_=second_sums[:])
 
         due = []
-        w2_copied_at = {}
+        w2_quantize_at = {}
         for tick in range(FIRST_TICK, LAST_TICK + 1):
             if 0 <= tick < E:
                 before = stream[stream.index(("w1", tick)) - 1]
                 if before[0] == "w2":
                     interleave_w2(before[1])
-                    w2_copied_at[before[1]] = tick
+                    w2_quantize_at[before[1]] = tick + W2_QUANT_LAG
                 interleave_w1(tick)
             if tick == E:
-                for q in range(LAST_GROUPS_FROM, E // W2_GROUP):
-                    interleave_w2(q)
-                    w2_copied_at[q] = tick
+                for u in range(LEADING, len(W2_UNITS)):
+                    interleave_w2(u)
+                    w2_quantize_at[u] = tick + u - LEADING
             if 0 <= tick + TOKEN_AHEAD < E:
                 quantize_tokens(tick + TOKEN_AHEAD)
             if 0 <= tick - SECOND_LAG < E:
                 quantize_hidden(tick - SECOND_LAG)
                 due.append(tick - SECOND_LAG)
-            for q in range(E // W2_GROUP):
-                if q in w2_copied_at and tick == w2_copied_at[q] + W2_QUANT_LAG:
-                    quantize_w2(q)
+            for u in range(len(W2_UNITS)):
+                if w2_quantize_at.get(u) == tick:
+                    quantize_w2(u)
             if 0 <= tick < E:
                 quantize_w1(tick)
                 first_layer(tick)
             for e in list(due):
-                if e // W2_GROUP in w2_codes:
+                if unit_of[e] in w2_codes:
                     second_layer(e)
                     due.remove(e)
             if 0 <= tick - GELU_LAG < E:
@@ -248,7 +267,6 @@ def tile_routed_moe_kernel(tc, xT, w1, w2, gate, offs, pos1, pos2, out):
             if 0 <= tick + GATHER_AHEAD < E:
                 gather_tokens(tick + GATHER_AHEAD)
 
-        gate_sb = loaded[("gate", 0)]
         products = []
         first_token = 0
         for step in range(len(COMBINE_TOKENS) + 1):
@@ -257,9 +275,9 @@ def tile_routed_moe_kernel(tc, xT, w1, w2, gate, offs, pos1, pos2, out):
                 entries = slice(tokens.start // 16, tokens.stop // 16)
                 first_token = tokens.stop
                 one = combine_pool.tile([P, COMBINE_TOKENS[step]], F32, name="one")
-                nc.vector.tensor_tensor(one[:], y_all[:].indirect(pos1_sb[:, entries]), gate_sb[:, 0, tokens], MULT)
+                nc.vector.tensor_tensor(one[:], y_all[:].indirect(pos1_sb[:, entries]), loaded[("gate", step)][:, 0, :], MULT)
                 two = combine_pool.tile([P, COMBINE_TOKENS[step]], F32, name="two")
-                nc.vector.tensor_tensor(two[:], y_all[:].indirect(pos2_sb[:, entries]), gate_sb[:, 1, tokens], MULT)
+                nc.vector.tensor_tensor(two[:], y_all[:].indirect(pos2_sb[:, entries]), loaded[("gate", step)][:, 1, :], MULT)
                 products.append((one, two, tokens))
             if step >= 1:
                 one, two, tokens = products[step - 1]

@@ -19,31 +19,34 @@ K, T, E, C, H, N = 512, 1024, 16, 128, 512, 128
 SLOTS = E * C
 FLOPS = 2 * SLOTS * K * H + 2 * SLOTS * H * N
 
-W2_UNITS = [(0, 4), (4, 4), (8, 4), (12, 2), (14, 2)]
-TRAILING = 2
+W2_UNITS = [(0, 4), (4, 4), (8, 2), (10, 2), (12, 2), (14, 1), (15, 1)]
+TRAILING = 5
 LEADING = len(W2_UNITS) - TRAILING
-TRAILING_ON_SCALAR = [2, 0, 0, 0]
+TRAILING_ON_SCALAR = [0, 0, 0, 0, 0]
 W1_LAST_PIECES = 2
+LAST_SHARED = True
+TAIL_BY_UNITS = True
+TAIL_QUANT_LAG = 1
 
 GATHER_AHEAD = 4
 TOKEN_AHEAD = 1
 GELU_LAG = 0
-SECOND_LAG = 2
+SECOND_LAG = 3
 W2_ON_SCALAR = 2
 EARLY_GROUPS = 128
 LATE_GROUPS = 128
 LATE_FROM = 12
 W2_QUANT_LAG = 1
 FIRST_TICK = -GATHER_AHEAD
-LAST_TICK = E - 1 + max(SECOND_LAG, TRAILING)
+LAST_TICK = E - 1 + max(SECOND_LAG, TRAILING + 1)
 
 LOAD_BUFS = 9
 BY_SCALAR_BUFS = 12
-BY_VECTOR_BUFS = 16
+BY_VECTOR_BUFS = 20
 W1_CODE_BUFS = 4
 TOKEN_CODE_BUFS = 4
-HIDDEN_CODE_BUFS = 6
-W2_CODE_BUFS = 3
+HIDDEN_CODE_BUFS = 10
+W2_CODE_BUFS = 7
 SUMS_BANKS = 8
 COMBINE_BUFS = 3
 
@@ -79,7 +82,7 @@ def tile_routed_moe_kernel(tc, xT, w1, w2, gate, offs, pos1, pos2, out):
         planes = []
         planes_bf16 = []
         for j in range(PACK):
-            plane = held.tile([P, T], F32, name="plane%d" % j)
+            plane = load_pool.tile([P, T], F32, name="load")
             nc.sync.dma_start(plane[:], rows_of_plane[:, j, :])
             planes.append(plane)
         for j in range(PACK):
@@ -127,7 +130,7 @@ def tile_routed_moe_kernel(tc, xT, w1, w2, gate, offs, pos1, pos2, out):
                 nc.sync.dma_start(loaded[(what, index)][:], gate[:, :, tokens].rearrange("r n t -> n r t"))
 
         token_bf16, token_codes, token_scales = {}, {}, {}
-        w1_bf16, w1_codes, w1_scales = {}, {}, {}
+        w1_bf16, w1_codes, w1_scales, w1_halves = {}, {}, {}, {}
         w2_bf16, w2_codes, w2_scales = {}, {}, {}
         first_sums, hidden_bf16, hidden_codes, hidden_scales = {}, {}, {}, {}
 
@@ -147,13 +150,24 @@ def tile_routed_moe_kernel(tc, xT, w1, w2, gate, offs, pos1, pos2, out):
             )
 
         def interleave_w1(e):
+            src = loaded[("w1", e)][:].rearrange("p j (m t) -> p m j t", t=4)
+            if e == E - 1 and LAST_SHARED:
+                w1_halves[0] = by_vector_pool.tile([P, PACK * H // 2], BF16, name="by_vector", align_bytes=64)
+                nc.vector.tensor_copy(
+                    out=w1_halves[0][:].rearrange("p (t m j) -> p m j t", t=2, j=PACK), in_=src[:, :, :, 0:2]
+                )
+                return
             w1_bf16[e] = by_vector_pool.tile([P, PACK * H], BF16, name="by_vector", align_bytes=64)
             dst = w1_bf16[e][:].rearrange("p (t m j) -> p m j t", t=4, j=PACK)
-            src = loaded[("w1", e)][:].rearrange("p j (m t) -> p m j t", t=4)
             split = EARLY_GROUPS if e < LATE_FROM else LATE_GROUPS
             nc.vector.tensor_copy(out=dst[:, 0:split, :, :], in_=src[:, 0:split, :, :])
             if split < P:
                 nc.scalar.copy(out=dst[:, split:P, :, :], in_=src[:, split:P, :, :])
+
+        def interleave_last_on_scalar():
+            src = loaded[("w1", E - 1)][:].rearrange("p j (m t) -> p m j t", t=4)
+            w1_halves[1] = by_scalar_pool.tile([P, PACK * H // 2], BF16, name="by_scalar", align_bytes=64)
+            nc.scalar.copy(out=w1_halves[1][:].rearrange("p (t m j) -> p m j t", t=2, j=PACK), in_=src[:, :, :, 2:4])
 
         def quantize_w1(e):
             w1_codes[e] = w1_code_pool.tile([P, H], U32, name="w1_codes", align_bytes=64)
@@ -165,7 +179,7 @@ def tile_routed_moe_kernel(tc, xT, w1, w2, gate, offs, pos1, pos2, out):
                 nc.vector.quantize_mx(
                     out=w1_codes[e][:, columns].bitcast(FP8X4),
                     scales=w1_scales[e][:, columns],
-                    in_=w1_bf16[e][:, PACK * columns.start : PACK * columns.stop],
+                    in_=w1_halves[piece][:] if e == E - 1 and LAST_SHARED else w1_bf16[e][:, PACK * columns.start : PACK * columns.stop],
                 )
 
         def interleave_w2(u):
@@ -243,7 +257,11 @@ def tile_routed_moe_kernel(tc, xT, w1, w2, gate, offs, pos1, pos2, out):
                     interleave_w2(before[1])
                     w2_quantize_at[before[1]] = tick + W2_QUANT_LAG
                 interleave_w1(tick)
-            if tick == E:
+            if TAIL_BY_UNITS:
+                if 0 <= tick - E < TRAILING:
+                    interleave_w2(LEADING + tick - E)
+                    w2_quantize_at[LEADING + tick - E] = tick + TAIL_QUANT_LAG
+            elif tick == E:
                 for u in range(LEADING, len(W2_UNITS)):
                     interleave_w2(u)
                     w2_quantize_at[u] = tick + u - LEADING
@@ -262,6 +280,8 @@ def tile_routed_moe_kernel(tc, xT, w1, w2, gate, offs, pos1, pos2, out):
                 if unit_of[e] in w2_codes:
                     second_layer(e)
                     due.remove(e)
+            if tick == E - 2 and LAST_SHARED:
+                interleave_last_on_scalar()
             if 0 <= tick - GELU_LAG < E:
                 gelu(tick - GELU_LAG)
             if 0 <= tick + GATHER_AHEAD < E:

@@ -22,7 +22,7 @@ FLOPS = 2 * SLOTS * K * H + 2 * SLOTS * H * N
 W2_UNITS = [(0, 4), (4, 4), (8, 2), (10, 2), (12, 2), (14, 1), (15, 1)]
 TRAILING = 5
 LEADING = len(W2_UNITS) - TRAILING
-TRAILING_ON_SCALAR = [0, 0, 0, 0, 0]
+TRAILING_ON_SCALAR = [0, 0, 1, 0, 0]
 W1_LAST_PIECES = 2
 LAST_SHARED = True
 TAIL_BY_UNITS = True
@@ -40,9 +40,10 @@ W2_QUANT_LAG = 1
 FIRST_TICK = -GATHER_AHEAD
 LAST_TICK = E - 1 + max(SECOND_LAG, TRAILING + 1)
 
+X_LOADS = 2
 LOAD_BUFS = 9
 BY_SCALAR_BUFS = 12
-BY_VECTOR_BUFS = 20
+BY_VECTOR_BUFS = 18
 W1_CODE_BUFS = 4
 TOKEN_CODE_BUFS = 4
 HIDDEN_CODE_BUFS = 10
@@ -81,13 +82,15 @@ def tile_routed_moe_kernel(tc, xT, w1, w2, gate, offs, pos1, pos2, out):
         rows_of_plane = xT.rearrange("(p j) n -> p j n", j=PACK)
         planes = []
         planes_bf16 = []
-        for j in range(PACK):
-            plane = load_pool.tile([P, T], F32, name="load")
-            nc.sync.dma_start(plane[:], rows_of_plane[:, j, :])
-            planes.append(plane)
+        for part in range(X_LOADS):
+            rows = PACK // X_LOADS
+            some_planes = load_pool.tile([P, rows, T], F32, name="load")
+            nc.sync.dma_start(some_planes[:], rows_of_plane[:, part * rows : (part + 1) * rows, :])
+            for j in range(rows):
+                planes.append(some_planes[:, j, :])
         for j in range(PACK):
             plane_bf16 = held.tile([P, T], BF16, name="plane_bf16_%d" % j)
-            nc.vector.tensor_copy(out=plane_bf16[:], in_=planes[j][:])
+            nc.vector.tensor_copy(out=plane_bf16[:], in_=planes[j])
             planes_bf16.append(plane_bf16)
 
         y_all = held.tile([P, SLOTS], F32, name="y_all")
@@ -108,8 +111,8 @@ def tile_routed_moe_kernel(tc, xT, w1, w2, gate, offs, pos1, pos2, out):
         for u in range(LEADING, len(W2_UNITS)):
             stream.append(("w2", u))
         stream.append(("lists", 0))
-        for step in range(len(COMBINE_TOKENS)):
-            stream.append(("gate", step))
+        for piece in range(len(COMBINE_TOKENS) + 1):
+            stream.append(("gate", piece))
         loaded = {}
         for what, index in stream:
             if what == "lists":
@@ -125,9 +128,13 @@ def tile_routed_moe_kernel(tc, xT, w1, w2, gate, offs, pos1, pos2, out):
                     loaded[(what, index)][:], w2[first : first + count].rearrange("e (p j) n -> p e (j n)", j=PACK)
                 )
             else:
-                tokens = slice(sum(COMBINE_TOKENS[:index]), sum(COMBINE_TOKENS[: index + 1]))
-                loaded[(what, index)] = load_pool.tile([P, 2, COMBINE_TOKENS[index]], F32, name="load")
-                nc.sync.dma_start(loaded[(what, index)][:], gate[:, :, tokens].rearrange("r n t -> n r t"))
+                if index == 0:
+                    loaded[(what, index)] = load_pool.tile([P, T], F32, name="load")
+                    nc.sync.dma_start(loaded[(what, index)][:], gate[0])
+                else:
+                    tokens = slice(sum(COMBINE_TOKENS[: index - 1]), sum(COMBINE_TOKENS[:index]))
+                    loaded[(what, index)] = load_pool.tile([P, COMBINE_TOKENS[index - 1]], F32, name="load")
+                    nc.sync.dma_start(loaded[(what, index)][:], gate[1][:, tokens])
 
         token_bf16, token_codes, token_scales = {}, {}, {}
         w1_bf16, w1_codes, w1_scales, w1_halves = {}, {}, {}, {}
@@ -287,6 +294,8 @@ def tile_routed_moe_kernel(tc, xT, w1, w2, gate, offs, pos1, pos2, out):
             if 0 <= tick + GATHER_AHEAD < E:
                 gather_tokens(tick + GATHER_AHEAD)
 
+        one = held.tile([P, T], F32, name="one")
+        nc.vector.tensor_tensor(one[:], y_all[:].indirect(pos1_sb[:]), loaded[("gate", 0)][:], MULT)
         products = []
         first_token = 0
         for step in range(len(COMBINE_TOKENS) + 1):
@@ -294,13 +303,11 @@ def tile_routed_moe_kernel(tc, xT, w1, w2, gate, offs, pos1, pos2, out):
                 tokens = slice(first_token, first_token + COMBINE_TOKENS[step])
                 entries = slice(tokens.start // 16, tokens.stop // 16)
                 first_token = tokens.stop
-                one = combine_pool.tile([P, COMBINE_TOKENS[step]], F32, name="one")
-                nc.vector.tensor_tensor(one[:], y_all[:].indirect(pos1_sb[:, entries]), loaded[("gate", step)][:, 0, :], MULT)
                 two = combine_pool.tile([P, COMBINE_TOKENS[step]], F32, name="two")
-                nc.vector.tensor_tensor(two[:], y_all[:].indirect(pos2_sb[:, entries]), loaded[("gate", step)][:, 1, :], MULT)
-                products.append((one, two, tokens))
+                nc.vector.tensor_tensor(two[:], y_all[:].indirect(pos2_sb[:, entries]), loaded[("gate", step + 1)][:], MULT)
+                products.append((two, tokens))
             if step >= 1:
-                one, two, tokens = products[step - 1]
+                two, tokens = products[step - 1]
                 total = combine_pool.tile([P, tokens.stop - tokens.start], F32, name="total")
-                nc.vector.tensor_tensor(total[:], one[:], two[:], ADD)
+                nc.vector.tensor_tensor(total[:], one[:, tokens], two[:], ADD)
                 nc.sync.dma_start(out[:, tokens], total[:])

@@ -19,39 +19,28 @@ K, T, E, C, H, N = 512, 1024, 16, 128, 512, 128
 SLOTS = E * C
 FLOPS = 2 * SLOTS * K * H + 2 * SLOTS * H * N
 
-W2_UNITS = [(0, 4), (4, 4), (8, 2), (10, 2), (12, 2), (14, 1), (15, 1)]
-TRAILING = 5
-LEADING = len(W2_UNITS) - TRAILING
-TRAILING_ON_SCALAR = [0, 0, 1, 0, 0]
-W1_LAST_PIECES = 2
-LAST_SHARED = True
-TAIL_BY_UNITS = True
-TAIL_QUANT_LAG = 1
 
-GATHER_AHEAD = 4
-TOKEN_AHEAD = 1
-GELU_LAG = 0
-SECOND_LAG = 3
-W2_ON_SCALAR = 2
-EARLY_GROUPS = 128
-LATE_GROUPS = 128
-LATE_FROM = 12
-W2_QUANT_LAG = 1
-FIRST_TICK = -GATHER_AHEAD
-LAST_TICK = E - 1 + max(SECOND_LAG, TRAILING + 1)
+W2_UNITS = [(0, 4), (4, 4), (8, 2), (10, 2), (12, 2), (14, 1), (15, 1)]
+W2_BEHIND = [2, 6]
+LEADING = len(W2_BEHIND)
+TRAILING = len(W2_UNITS) - LEADING
+W2_ON_SCALAR = [2, 2, 0, 0, 1, 0, 0]
+Y_GROUPS = [(0, 2), (2, 2), (4, 2), (6, 2), (8, 2), (10, 2), (12, 2), (14, 1), (15, 1)]
+
+AHEAD = 4
+LAG = 3
+HEAD_TILES = [(0,), (1,), (2, 3)]
 
 X_LOADS = 2
 LOAD_BUFS = 9
-BY_SCALAR_BUFS = 12
+BY_SCALAR_BUFS = 8
 BY_VECTOR_BUFS = 18
 W1_CODE_BUFS = 4
-TOKEN_CODE_BUFS = 4
-HIDDEN_CODE_BUFS = 10
+CODE_BUFS = 12
 W2_CODE_BUFS = 7
 SUMS_BANKS = 8
 COMBINE_BUFS = 3
-
-COMBINE_TOKENS = [512,256,256]
+COMBINE_TOKENS = [512, 256, 256]
 
 
 def tile_routed_moe_kernel(tc, xT, w1, w2, gate, offs, pos1, pos2, out):
@@ -63,8 +52,7 @@ def tile_routed_moe_kernel(tc, xT, w1, w2, gate, offs, pos1, pos2, out):
         by_scalar_pool = ctx.enter_context(tc.tile_pool(name="by_scalar_pool", bufs=BY_SCALAR_BUFS))
         by_vector_pool = ctx.enter_context(tc.tile_pool(name="by_vector_pool", bufs=BY_VECTOR_BUFS))
         w1_code_pool = ctx.enter_context(tc.tile_pool(name="w1_code_pool", bufs=W1_CODE_BUFS))
-        token_code_pool = ctx.enter_context(tc.tile_pool(name="token_code_pool", bufs=TOKEN_CODE_BUFS))
-        hidden_code_pool = ctx.enter_context(tc.tile_pool(name="hidden_code_pool", bufs=HIDDEN_CODE_BUFS))
+        code_pool = ctx.enter_context(tc.tile_pool(name="code_pool", bufs=CODE_BUFS))
         w2_code_pool = ctx.enter_context(tc.tile_pool(name="w2_code_pool", bufs=W2_CODE_BUFS))
         combine_pool = ctx.enter_context(tc.tile_pool(name="combine_pool", bufs=COMBINE_BUFS))
         sums_pool = ctx.enter_context(tc.psum_pool(name="sums_pool", bufs=SUMS_BANKS))
@@ -101,13 +89,10 @@ def tile_routed_moe_kernel(tc, xT, w1, w2, gate, offs, pos1, pos2, out):
                 unit_of[W2_UNITS[u][0] + a] = u
         stream = []
         for e in range(E):
-            if e == 0:
-                stream.append(("w1", 0))
+            stream.append(("w1", e))
             for u in range(LEADING):
-                if W2_UNITS[u][0] == e:
+                if W2_BEHIND[u] == e:
                     stream.append(("w2", u))
-            if e > 0:
-                stream.append(("w1", e))
         for u in range(LEADING, len(W2_UNITS)):
             stream.append(("w2", u))
         stream.append(("lists", 0))
@@ -127,49 +112,67 @@ def tile_routed_moe_kernel(tc, xT, w1, w2, gate, offs, pos1, pos2, out):
                 nc.sync.dma_start(
                     loaded[(what, index)][:], w2[first : first + count].rearrange("e (p j) n -> p e (j n)", j=PACK)
                 )
+            elif index == 0:
+                loaded[(what, index)] = load_pool.tile([P, T], F32, name="load")
+                nc.sync.dma_start(loaded[(what, index)][:], gate[0])
             else:
-                if index == 0:
-                    loaded[(what, index)] = load_pool.tile([P, T], F32, name="load")
-                    nc.sync.dma_start(loaded[(what, index)][:], gate[0])
-                else:
-                    tokens = slice(sum(COMBINE_TOKENS[: index - 1]), sum(COMBINE_TOKENS[:index]))
-                    loaded[(what, index)] = load_pool.tile([P, COMBINE_TOKENS[index - 1]], F32, name="load")
-                    nc.sync.dma_start(loaded[(what, index)][:], gate[1][:, tokens])
+                tokens = slice(sum(COMBINE_TOKENS[: index - 1]), sum(COMBINE_TOKENS[:index]))
+                loaded[(what, index)] = load_pool.tile([P, COMBINE_TOKENS[index - 1]], F32, name="load")
+                nc.sync.dma_start(loaded[(what, index)][:], gate[1][:, tokens])
 
-        token_bf16, token_codes, token_scales = {}, {}, {}
+        shared_bf16 = {}
+        token_codes, token_scales = {}, {}
         w1_bf16, w1_codes, w1_scales, w1_halves = {}, {}, {}, {}
         w2_bf16, w2_codes, w2_scales = {}, {}, {}
-        first_sums, hidden_bf16, hidden_codes, hidden_scales = {}, {}, {}, {}
+        first_sums, hidden_codes, hidden_scales = {}, {}, {}
+        group_of, group_sums = {}, {}
+        for first, count in Y_GROUPS:
+            for a in range(count):
+                group_of[first + a] = (first, count)
 
-        def gather_tokens(e):
-            token_bf16[e] = by_scalar_pool.tile([P, C, PACK], BF16, name="by_scalar", align_bytes=64)
+        def gather_plane(dst, e, j):
             entries = offs_sb[:, e * (C // 16) : (e + 1) * (C // 16)]
-            for j in range(PACK):
-                nc.scalar.activation(out=token_bf16[e][:, :, j], in_=planes_bf16[j][:].indirect(entries), func=COPY)
+            nc.scalar.activation(out=dst[:, :, j], in_=planes_bf16[j][:].indirect(entries), func=COPY)
 
-        def quantize_tokens(e):
-            token_codes[e] = token_code_pool.tile([P, C], U32, name="token_codes", align_bytes=64)
-            token_scales[e] = by_vector_pool.tile([P, C], U8, name="by_vector", align_bytes=64)
-            nc.vector.quantize_mx(
-                out=token_codes[e][:].bitcast(FP8X4),
-                scales=token_scales[e][:],
-                in_=token_bf16[e][:].rearrange("p s j -> p (s j)"),
-            )
+        def quantize(source, width):
+            codes = code_pool.tile([P, width], U32, name="codes", align_bytes=64)
+            scales = by_vector_pool.tile([P, width], U8, name="by_vector", align_bytes=64)
+            nc.vector.quantize_mx(out=codes[:].bitcast(FP8X4), scales=scales[:], in_=source)
+            return codes, scales
+
+        def quantize_head(i):
+            experts = HEAD_TILES[i]
+            codes, scales = quantize(shared_bf16[("head", i)][:].rearrange("p e s j -> p (e s j)"), C * len(experts))
+            for a in range(len(experts)):
+                token_codes[experts[a]] = codes[:, a * C : (a + 1) * C]
+                token_scales[experts[a]] = scales[:, a * C : (a + 1) * C]
+
+        def gelu_and_gather(e):
+            count = 2 if e + AHEAD < E else 1
+            tile = by_scalar_pool.tile([P, count, C, PACK], BF16, name="by_scalar", align_bytes=64)
+            nc.scalar.activation(out=tile[:, 0, :, :], in_=first_sums[e][:].rearrange("p t s -> p s t"), func=GELU)
+            if count == 2:
+                for j in range(PACK):
+                    gather_plane(tile[:, 1, :, :], e + AHEAD, j)
+            shared_bf16[e] = tile
+
+        def quantize_shared(e):
+            count = 2 if e + AHEAD < E else 1
+            codes, scales = quantize(shared_bf16[e][:].rearrange("p e s j -> p (e s j)"), C * count)
+            hidden_codes[e], hidden_scales[e] = codes[:, 0:C], scales[:, 0:C]
+            if count == 2:
+                token_codes[e + AHEAD], token_scales[e + AHEAD] = codes[:, C : 2 * C], scales[:, C : 2 * C]
 
         def interleave_w1(e):
             src = loaded[("w1", e)][:].rearrange("p j (m t) -> p m j t", t=4)
-            if e == E - 1 and LAST_SHARED:
+            if e == E - 1:
                 w1_halves[0] = by_vector_pool.tile([P, PACK * H // 2], BF16, name="by_vector", align_bytes=64)
                 nc.vector.tensor_copy(
                     out=w1_halves[0][:].rearrange("p (t m j) -> p m j t", t=2, j=PACK), in_=src[:, :, :, 0:2]
                 )
                 return
             w1_bf16[e] = by_vector_pool.tile([P, PACK * H], BF16, name="by_vector", align_bytes=64)
-            dst = w1_bf16[e][:].rearrange("p (t m j) -> p m j t", t=4, j=PACK)
-            split = EARLY_GROUPS if e < LATE_FROM else LATE_GROUPS
-            nc.vector.tensor_copy(out=dst[:, 0:split, :, :], in_=src[:, 0:split, :, :])
-            if split < P:
-                nc.scalar.copy(out=dst[:, split:P, :, :], in_=src[:, split:P, :, :])
+            nc.vector.tensor_copy(out=w1_bf16[e][:].rearrange("p (t m j) -> p m j t", t=4, j=PACK), in_=src)
 
         def interleave_last_on_scalar():
             src = loaded[("w1", E - 1)][:].rearrange("p j (m t) -> p m j t", t=4)
@@ -179,20 +182,20 @@ def tile_routed_moe_kernel(tc, xT, w1, w2, gate, offs, pos1, pos2, out):
         def quantize_w1(e):
             w1_codes[e] = w1_code_pool.tile([P, H], U32, name="w1_codes", align_bytes=64)
             w1_scales[e] = by_vector_pool.tile([P, H], U8, name="by_vector", align_bytes=64)
-            pieces = W1_LAST_PIECES if e == E - 1 else 1
+            pieces = 2 if e == E - 1 else 1
             width = H // pieces
             for piece in range(pieces):
                 columns = slice(piece * width, (piece + 1) * width)
                 nc.vector.quantize_mx(
                     out=w1_codes[e][:, columns].bitcast(FP8X4),
                     scales=w1_scales[e][:, columns],
-                    in_=w1_halves[piece][:] if e == E - 1 and LAST_SHARED else w1_bf16[e][:, PACK * columns.start : PACK * columns.stop],
+                    in_=w1_halves[piece][:] if e == E - 1 else w1_bf16[e][:],
                 )
 
         def interleave_w2(u):
             count = W2_UNITS[u][1]
             w2_bf16[u] = by_vector_pool.tile([P, count, N, PACK], BF16, name="by_vector", align_bytes=64)
-            on_scalar = min(W2_ON_SCALAR if u < LEADING else TRAILING_ON_SCALAR[u - LEADING], count)
+            on_scalar = W2_ON_SCALAR[u]
             if on_scalar < count:
                 nc.vector.tensor_copy(
                     out=w2_bf16[u][:, on_scalar:count, :, :].rearrange("p a (n i) j -> p a n j i", i=4),
@@ -221,78 +224,76 @@ def tile_routed_moe_kernel(tc, xT, w1, w2, gate, offs, pos1, pos2, out):
                     out=first_sums[e][:, t, :],
                     lhsT=w1_codes[e][:, t * P : (t + 1) * P].bitcast(FP8X4),
                     lhsT_scale=w1_scales[e][:, t * P : (t + 1) * P],
-                    rhs=token_codes[e][:].bitcast(FP8X4),
-                    rhs_scale=token_scales[e][:],
+                    rhs=token_codes[e].bitcast(FP8X4),
+                    rhs_scale=token_scales[e],
                     start=True,
                     stop=True,
                 )
 
-        def gelu(e):
-            hidden_bf16[e] = by_scalar_pool.tile([P, C, PACK], BF16, name="by_scalar", align_bytes=64)
-            nc.scalar.activation(out=hidden_bf16[e][:], in_=first_sums[e][:].rearrange("p t s -> p s t"), func=GELU)
-
-        def quantize_hidden(e):
-            hidden_codes[e] = hidden_code_pool.tile([P, C], U32, name="hidden_codes", align_bytes=64)
-            hidden_scales[e] = by_vector_pool.tile([P, C], U8, name="by_vector", align_bytes=64)
-            nc.vector.quantize_mx(
-                out=hidden_codes[e][:].bitcast(FP8X4),
-                scales=hidden_scales[e][:],
-                in_=hidden_bf16[e][:].rearrange("p s t -> p (s t)"),
-            )
-
         def second_layer(e):
-            second_sums = sums_pool.tile([P, C], F32, name="sums")
+            first, count = group_of[e]
+            if e == first:
+                group_sums[first] = sums_pool.tile([P, count, C], F32, name="sums")
             u = unit_of[e]
             a = e - W2_UNITS[u][0]
             nc.tensor.matmul_mx(
-                out=second_sums[:],
+                out=group_sums[first][:, e - first, :],
                 lhsT=w2_codes[u][:, a * N : (a + 1) * N].bitcast(FP8X4),
                 lhsT_scale=w2_scales[u][:, a * N : (a + 1) * N],
-                rhs=hidden_codes[e][:].bitcast(FP8X4),
-                rhs_scale=hidden_scales[e][:],
+                rhs=hidden_codes[e].bitcast(FP8X4),
+                rhs_scale=hidden_scales[e],
                 start=True,
                 stop=True,
             )
-            nc.scalar.copy(out=y_all[:, e * C : (e + 1) * C], in_=second_sums[:])
+            if e == first + count - 1:
+                nc.scalar.copy(
+                    out=y_all[:, first * C : (first + count) * C], in_=group_sums[first][:].rearrange("p a s -> p (a s)")
+                )
+
+        for i in range(len(HEAD_TILES)):
+            shared_bf16[("head", i)] = by_scalar_pool.tile(
+                [P, len(HEAD_TILES[i]), C, PACK], BF16, name="by_scalar", align_bytes=64
+            )
+        for part in range(2):
+            for i in range(len(HEAD_TILES)):
+                for a in range(len(HEAD_TILES[i])):
+                    for j in (2 * part, 2 * part + 1):
+                        gather_plane(shared_bf16[("head", i)][:, a, :, :], HEAD_TILES[i][a], j)
 
         due = []
         w2_quantize_at = {}
-        for tick in range(FIRST_TICK, LAST_TICK + 1):
-            if 0 <= tick < E:
-                before = stream[stream.index(("w1", tick)) - 1]
-                if before[0] == "w2":
-                    interleave_w2(before[1])
-                    w2_quantize_at[before[1]] = tick + W2_QUANT_LAG
+        for tick in range(E + max(LAG, TRAILING + 1)):
+            if tick < E:
                 interleave_w1(tick)
-            if TAIL_BY_UNITS:
-                if 0 <= tick - E < TRAILING:
-                    interleave_w2(LEADING + tick - E)
-                    w2_quantize_at[LEADING + tick - E] = tick + TAIL_QUANT_LAG
-            elif tick == E:
-                for u in range(LEADING, len(W2_UNITS)):
-                    interleave_w2(u)
-                    w2_quantize_at[u] = tick + u - LEADING
-            if 0 <= tick + TOKEN_AHEAD < E:
-                quantize_tokens(tick + TOKEN_AHEAD)
-            if 0 <= tick - SECOND_LAG < E:
-                quantize_hidden(tick - SECOND_LAG)
-                due.append(tick - SECOND_LAG)
+                behind = stream[stream.index(("w1", tick)) + 1]
+                if behind[0] == "w2" and tick < E - 1:
+                    interleave_w2(behind[1])
+                    w2_quantize_at[behind[1]] = tick + 1
+            elif tick - E < TRAILING:
+                interleave_w2(LEADING + tick - E)
+                w2_quantize_at[LEADING + tick - E] = tick + 1
+            if tick == 0:
+                quantize_head(0)
+                quantize_head(1)
+            if tick == 1:
+                quantize_head(2)
+            if 0 <= tick - LAG < E:
+                quantize_shared(tick - LAG)
+                due.append(tick - LAG)
             for u in range(len(W2_UNITS)):
                 if w2_quantize_at.get(u) == tick:
                     quantize_w2(u)
-            if 0 <= tick < E:
+            if tick < E:
                 quantize_w1(tick)
                 first_layer(tick)
             for e in list(due):
                 if unit_of[e] in w2_codes:
                     second_layer(e)
                     due.remove(e)
-            if tick == E - 2 and LAST_SHARED:
+            if tick == E - 2:
                 interleave_last_on_scalar()
-            if 0 <= tick - GELU_LAG < E:
-                gelu(tick - GELU_LAG)
-            if 0 <= tick + GATHER_AHEAD < E:
-                gather_tokens(tick + GATHER_AHEAD)
+            if tick < E:
+                gelu_and_gather(tick)
 
         one = held.tile([P, T], F32, name="one")
         nc.vector.tensor_tensor(one[:], y_all[:].indirect(pos1_sb[:]), loaded[("gate", 0)][:], MULT)

@@ -24,8 +24,8 @@ W2_UNITS = [(0, 4), (4, 4), (8, 2), (10, 2), (12, 2), (14, 1), (15, 1)]
 W2_BEHIND = [2, 6]
 LEADING = len(W2_BEHIND)
 TRAILING = len(W2_UNITS) - LEADING
-W2_ON_SCALAR = [2, 2, 0, 0, 1, 0, 0]
-Y_GROUPS = [(0, 2), (2, 2), (4, 2), (6, 2), (8, 2), (10, 2), (12, 2), (14, 1), (15, 1)]
+W2_ON_SCALAR = [2, 2, 0, 1, 1, 1, 0]
+Y_GROUPS = [(0, 2), (2, 2), (4, 2), (6, 2), (8, 4), (12, 2), (14, 1), (15, 1)]
 
 AHEAD = 4
 LAG = 3
@@ -246,9 +246,15 @@ def tile_routed_moe_kernel(tc, xT, w1, w2, gate, offs, pos1, pos2, out):
                 stop=True,
             )
             if e == first + count - 1:
+                y_due.append(first)
+
+        def copy_y():
+            for first in y_due:
+                count = group_of[first][1]
                 nc.scalar.copy(
                     out=y_all[:, first * C : (first + count) * C], in_=group_sums[first][:].rearrange("p a s -> p (a s)")
                 )
+            y_due.clear()
 
         for i in range(len(HEAD_TILES)):
             shared_bf16[("head", i)] = by_scalar_pool.tile(
@@ -261,6 +267,7 @@ def tile_routed_moe_kernel(tc, xT, w1, w2, gate, offs, pos1, pos2, out):
                         gather_plane(shared_bf16[("head", i)][:, a, :, :], HEAD_TILES[i][a], j)
 
         due = []
+        y_due = []
         w2_quantize_at = {}
         for tick in range(E + max(LAG, TRAILING + 1)):
             if tick < E:
@@ -272,6 +279,7 @@ def tile_routed_moe_kernel(tc, xT, w1, w2, gate, offs, pos1, pos2, out):
             elif tick - E < TRAILING:
                 interleave_w2(LEADING + tick - E)
                 w2_quantize_at[LEADING + tick - E] = tick + 1
+            copy_y()
             if tick == 0:
                 quantize_head(0)
                 quantize_head(1)
@@ -294,6 +302,8 @@ def tile_routed_moe_kernel(tc, xT, w1, w2, gate, offs, pos1, pos2, out):
                 interleave_last_on_scalar()
             if tick < E:
                 gelu_and_gather(tick)
+
+        copy_y()
 
         one = held.tile([P, T], F32, name="one")
         nc.vector.tensor_tensor(one[:], y_all[:].indirect(pos1_sb[:]), loaded[("gate", 0)][:], MULT)

@@ -1,6 +1,7 @@
 from contextlib import ExitStack
 
 import concourse.mybir as mybir
+from concourse.masks import make_identity
 
 F32 = mybir.dt.float32
 BF16 = mybir.dt.bfloat16
@@ -21,26 +22,29 @@ FLOPS = 2 * SLOTS * K * H + 2 * SLOTS * H * N
 
 
 W2_UNITS = [(0, 4), (4, 4), (8, 2), (10, 2), (12, 2), (14, 1), (15, 1)]
-W2_BEHIND = [2, 6]
+W2_BEHIND = [3, 6]
 LEADING = len(W2_BEHIND)
 TRAILING = len(W2_UNITS) - LEADING
-W2_ON_SCALAR = [2, 2, 0, 1, 1, 1, 0]
-Y_GROUPS = [(0, 2), (2, 2), (4, 2), (6, 2), (8, 4), (12, 2), (14, 1), (15, 1)]
+W2_PIECES = [(0, 2, True), (2, 2, False), (4, 2, True), (6, 2, False), (8, 2, False), (10, 1, True), (11, 1, False),
+             (12, 1, True), (13, 1, False), (14, 1, True), (15, 1, False)]
+Y_GROUPS = [(0, 4), (4, 4), (8, 4), (12, 2), (14, 1), (15, 1)]
 
 AHEAD = 4
 LAG = 3
 HEAD_TILES = [(0,), (1,), (2, 3)]
 
 X_LOADS = 2
-LOAD_BUFS = 9
+W1_IN_PAIRS = [0, 2]
+LOAD_BUFS = 5
 BY_SCALAR_BUFS = 8
-BY_VECTOR_BUFS = 18
+BY_VECTOR_BUFS = 20
 W1_CODE_BUFS = 4
 CODE_BUFS = 12
-W2_CODE_BUFS = 7
+W2_CODE_BUFS = 11
 SUMS_BANKS = 8
-COMBINE_BUFS = 3
-COMBINE_TOKENS = [512, 256, 256]
+GATE_PIECES = [(0, 0, 320), (1, 0, 320), (0, 320, 704), (1, 320, 384), (1, 704, 192), (1, 896, 128)]
+ON_TENSOR = 320
+STEPS = [(320, 384), (704, 192), (896, 128)]
 
 
 def tile_routed_moe_kernel(tc, xT, w1, w2, gate, offs, pos1, pos2, out):
@@ -48,19 +52,22 @@ def tile_routed_moe_kernel(tc, xT, w1, w2, gate, offs, pos1, pos2, out):
     with ExitStack() as ctx:
         lists = ctx.enter_context(tc.tile_pool(name="lists", bufs=1))
         held = ctx.enter_context(tc.tile_pool(name="held", bufs=1))
+        wide_pool = ctx.enter_context(tc.tile_pool(name="wide_pool", bufs=3))
         load_pool = ctx.enter_context(tc.tile_pool(name="load_pool", bufs=LOAD_BUFS))
         by_scalar_pool = ctx.enter_context(tc.tile_pool(name="by_scalar_pool", bufs=BY_SCALAR_BUFS))
         by_vector_pool = ctx.enter_context(tc.tile_pool(name="by_vector_pool", bufs=BY_VECTOR_BUFS))
         w1_code_pool = ctx.enter_context(tc.tile_pool(name="w1_code_pool", bufs=W1_CODE_BUFS))
         code_pool = ctx.enter_context(tc.tile_pool(name="code_pool", bufs=CODE_BUFS))
         w2_code_pool = ctx.enter_context(tc.tile_pool(name="w2_code_pool", bufs=W2_CODE_BUFS))
-        combine_pool = ctx.enter_context(tc.tile_pool(name="combine_pool", bufs=COMBINE_BUFS))
         sums_pool = ctx.enter_context(tc.psum_pool(name="sums_pool", bufs=SUMS_BANKS))
 
         zero = held.tile([P, 1], F32, name="zero")
         unused = held.tile([P, 1], F32, name="unused")
         nc.vector.memset(zero[:], 0.0)
         nc.scalar.activation(out=unused[:], in_=zero[:], func=GELU)
+
+        identity = held.tile([P, P], F32, name="identity")
+        make_identity(nc, identity[:])
 
         offs_sb = lists.tile([P, SLOTS // 16], U16, name="offs_sb")
         nc.sync.dma_start(offs_sb[:], offs)
@@ -70,12 +77,12 @@ def tile_routed_moe_kernel(tc, xT, w1, w2, gate, offs, pos1, pos2, out):
         rows_of_plane = xT.rearrange("(p j) n -> p j n", j=PACK)
         planes = []
         planes_bf16 = []
+        all_planes = wide_pool.tile([P, PACK, T], F32, name="wide")
         for part in range(X_LOADS):
-            rows = PACK // X_LOADS
-            some_planes = load_pool.tile([P, rows, T], F32, name="load")
-            nc.sync.dma_start(some_planes[:], rows_of_plane[:, part * rows : (part + 1) * rows, :])
-            for j in range(rows):
-                planes.append(some_planes[:, j, :])
+            rows = slice(part * PACK // X_LOADS, (part + 1) * PACK // X_LOADS)
+            nc.sync.dma_start(all_planes[:, rows, :], rows_of_plane[:, rows, :])
+        for j in range(PACK):
+            planes.append(all_planes[:, j, :])
         for j in range(PACK):
             plane_bf16 = held.tile([P, T], BF16, name="plane_bf16_%d" % j)
             nc.vector.tensor_copy(out=plane_bf16[:], in_=planes[j])
@@ -96,7 +103,7 @@ def tile_routed_moe_kernel(tc, xT, w1, w2, gate, offs, pos1, pos2, out):
         for u in range(LEADING, len(W2_UNITS)):
             stream.append(("w2", u))
         stream.append(("lists", 0))
-        for piece in range(len(COMBINE_TOKENS) + 1):
+        for piece in GATE_PIECES:
             stream.append(("gate", piece))
         loaded = {}
         for what, index in stream:
@@ -104,28 +111,36 @@ def tile_routed_moe_kernel(tc, xT, w1, w2, gate, offs, pos1, pos2, out):
                 nc.sync.dma_start(pos1_sb[:], pos1)
                 nc.sync.dma_start(pos2_sb[:], pos2)
             elif what == "w1":
-                loaded[(what, index)] = load_pool.tile([P, PACK, H], F32, name="load")
-                nc.sync.dma_start(loaded[(what, index)][:], w1[index].rearrange("(p j) i -> p j i", j=PACK))
+                if index in W1_IN_PAIRS:
+                    two = wide_pool.tile([P, 2, PACK * H], F32, name="wide")
+                    nc.sync.dma_start(two[:], w1[index : index + 2].rearrange("e (p j) i -> p e (j i)", j=PACK))
+                    for a in range(2):
+                        loaded[(what, index + a)] = two[:, a, :].rearrange("p (j i) -> p j i", j=PACK)
+                elif index - 1 not in W1_IN_PAIRS:
+                    one = load_pool.tile([P, PACK, H], F32, name="load")
+                    nc.sync.dma_start(one[:], w1[index].rearrange("(p j) i -> p j i", j=PACK))
+                    loaded[(what, index)] = one[:]
             elif what == "w2":
                 first, count = W2_UNITS[index]
                 loaded[(what, index)] = load_pool.tile([P, count, PACK * N], F32, name="load")
                 nc.sync.dma_start(
                     loaded[(what, index)][:], w2[first : first + count].rearrange("e (p j) n -> p e (j n)", j=PACK)
                 )
-            elif index == 0:
-                loaded[(what, index)] = load_pool.tile([P, T], F32, name="load")
-                nc.sync.dma_start(loaded[(what, index)][:], gate[0])
             else:
-                tokens = slice(sum(COMBINE_TOKENS[: index - 1]), sum(COMBINE_TOKENS[:index]))
-                loaded[(what, index)] = load_pool.tile([P, COMBINE_TOKENS[index - 1]], F32, name="load")
-                nc.sync.dma_start(loaded[(what, index)][:], gate[1][:, tokens])
+                row, first, count = index
+                if index == GATE_PIECES[0]:
+                    gates = load_pool.tile([P, 2, T], F32, name="load")
+                loaded[(what, index)] = gates[:, row, first : first + count]
+                nc.sync.dma_start(loaded[(what, index)], gate[row][:, first : first + count])
 
         shared_bf16 = {}
         token_codes, token_scales = {}, {}
         w1_bf16, w1_codes, w1_scales, w1_halves = {}, {}, {}, {}
         w2_bf16, w2_codes, w2_scales = {}, {}, {}
         first_sums, hidden_codes, hidden_scales = {}, {}, {}
-        group_of, group_sums = {}, {}
+        group_of, group_sums, piece_of = {}, {}, {}
+        for first, count, on_scalar in W2_PIECES:
+            piece_of[first] = (count, on_scalar)
         for first, count in Y_GROUPS:
             for a in range(count):
                 group_of[first + a] = (first, count)
@@ -164,7 +179,7 @@ def tile_routed_moe_kernel(tc, xT, w1, w2, gate, offs, pos1, pos2, out):
                 token_codes[e + AHEAD], token_scales[e + AHEAD] = codes[:, C : 2 * C], scales[:, C : 2 * C]
 
         def interleave_w1(e):
-            src = loaded[("w1", e)][:].rearrange("p j (m t) -> p m j t", t=4)
+            src = loaded[("w1", e)].rearrange("p j (m t) -> p m j t", t=4)
             if e == E - 1:
                 w1_halves[0] = by_vector_pool.tile([P, PACK * H // 2], BF16, name="by_vector", align_bytes=64)
                 nc.vector.tensor_copy(
@@ -175,7 +190,7 @@ def tile_routed_moe_kernel(tc, xT, w1, w2, gate, offs, pos1, pos2, out):
             nc.vector.tensor_copy(out=w1_bf16[e][:].rearrange("p (t m j) -> p m j t", t=4, j=PACK), in_=src)
 
         def interleave_last_on_scalar():
-            src = loaded[("w1", E - 1)][:].rearrange("p j (m t) -> p m j t", t=4)
+            src = loaded[("w1", E - 1)].rearrange("p j (m t) -> p m j t", t=4)
             w1_halves[1] = by_scalar_pool.tile([P, PACK * H // 2], BF16, name="by_scalar", align_bytes=64)
             nc.scalar.copy(out=w1_halves[1][:].rearrange("p (t m j) -> p m j t", t=2, j=PACK), in_=src[:, :, :, 2:4])
 
@@ -192,30 +207,29 @@ def tile_routed_moe_kernel(tc, xT, w1, w2, gate, offs, pos1, pos2, out):
                     in_=w1_halves[piece][:] if e == E - 1 else w1_bf16[e][:],
                 )
 
-        def interleave_w2(u):
-            count = W2_UNITS[u][1]
-            w2_bf16[u] = by_vector_pool.tile([P, count, N, PACK], BF16, name="by_vector", align_bytes=64)
-            on_scalar = W2_ON_SCALAR[u]
-            if on_scalar < count:
-                nc.vector.tensor_copy(
-                    out=w2_bf16[u][:, on_scalar:count, :, :].rearrange("p a (n i) j -> p a n j i", i=4),
-                    in_=loaded[("w2", u)][:, on_scalar:count, :].rearrange("p a (j n i) -> p a n j i", j=PACK, i=4),
-                )
-            for a in range(on_scalar):
-                nc.scalar.copy(
-                    out=w2_bf16[u][:, a, :, :].rearrange("p (n i) j -> p n j i", i=4),
-                    in_=loaded[("w2", u)][:, a, :].rearrange("p (j n i) -> p n j i", j=PACK, i=4),
-                )
-
-        def quantize_w2(u):
-            count = W2_UNITS[u][1]
-            w2_codes[u] = w2_code_pool.tile([P, count * N], U32, name="w2_codes", align_bytes=64)
-            w2_scales[u] = by_vector_pool.tile([P, count * N], U8, name="by_vector", align_bytes=64)
-            nc.vector.quantize_mx(
-                out=w2_codes[u][:].bitcast(FP8X4),
-                scales=w2_scales[u][:],
-                in_=w2_bf16[u][:].rearrange("p a n j -> p (a n j)"),
+        def interleave_w2(first):
+            count, on_scalar = piece_of[first]
+            u = unit_of[first]
+            a = first - W2_UNITS[u][0]
+            pool, name, copy = (
+                (by_scalar_pool, "by_scalar", nc.scalar.copy) if on_scalar else (by_vector_pool, "by_vector", nc.vector.tensor_copy)
             )
+            w2_bf16[first] = pool.tile([P, count, N, PACK], BF16, name=name, align_bytes=64)
+            copy(
+                out=w2_bf16[first][:].rearrange("p a (n i) j -> p a n j i", i=4),
+                in_=loaded[("w2", u)][:, a : a + count, :].rearrange("p a (j n i) -> p a n j i", j=PACK, i=4),
+            )
+
+        def quantize_w2(first):
+            count = piece_of[first][0]
+            codes = w2_code_pool.tile([P, count * N], U32, name="w2_codes", align_bytes=64)
+            scales = by_vector_pool.tile([P, count * N], U8, name="by_vector", align_bytes=64)
+            nc.vector.quantize_mx(
+                out=codes[:].bitcast(FP8X4), scales=scales[:], in_=w2_bf16[first][:].rearrange("p a n j -> p (a n j)")
+            )
+            for a in range(count):
+                w2_codes[first + a] = codes[:, a * N : (a + 1) * N]
+                w2_scales[first + a] = scales[:, a * N : (a + 1) * N]
 
         def first_layer(e):
             first_sums[e] = sums_pool.tile([P, 4, C], F32, name="sums")
@@ -234,27 +248,22 @@ def tile_routed_moe_kernel(tc, xT, w1, w2, gate, offs, pos1, pos2, out):
             first, count = group_of[e]
             if e == first:
                 group_sums[first] = sums_pool.tile([P, count, C], F32, name="sums")
-            u = unit_of[e]
-            a = e - W2_UNITS[u][0]
             nc.tensor.matmul_mx(
                 out=group_sums[first][:, e - first, :],
-                lhsT=w2_codes[u][:, a * N : (a + 1) * N].bitcast(FP8X4),
-                lhsT_scale=w2_scales[u][:, a * N : (a + 1) * N],
+                lhsT=w2_codes[e].bitcast(FP8X4),
+                lhsT_scale=w2_scales[e],
                 rhs=hidden_codes[e].bitcast(FP8X4),
                 rhs_scale=hidden_scales[e],
                 start=True,
                 stop=True,
             )
-            if e == first + count - 1:
-                y_due.append(first)
 
-        def copy_y():
-            for first in y_due:
-                count = group_of[first][1]
-                nc.scalar.copy(
-                    out=y_all[:, first * C : (first + count) * C], in_=group_sums[first][:].rearrange("p a s -> p (a s)")
-                )
-            y_due.clear()
+        def copy_y(first):
+            count = group_of[first][1]
+            copy = nc.scalar.copy
+            copy(
+                out=y_all[:, first * C : (first + count) * C], in_=group_sums[first][:].rearrange("p a s -> p (a s)")
+            )
 
         for i in range(len(HEAD_TILES)):
             shared_bf16[("head", i)] = by_scalar_pool.tile(
@@ -266,59 +275,89 @@ def tile_routed_moe_kernel(tc, xT, w1, w2, gate, offs, pos1, pos2, out):
                     for j in (2 * part, 2 * part + 1):
                         gather_plane(shared_bf16[("head", i)][:, a, :, :], HEAD_TILES[i][a], j)
 
-        due = []
-        y_due = []
-        w2_quantize_at = {}
-        for tick in range(E + max(LAG, TRAILING + 1)):
-            if tick < E:
-                interleave_w1(tick)
-                behind = stream[stream.index(("w1", tick)) + 1]
-                if behind[0] == "w2" and tick < E - 1:
-                    interleave_w2(behind[1])
-                    w2_quantize_at[behind[1]] = tick + 1
-            elif tick - E < TRAILING:
-                interleave_w2(LEADING + tick - E)
-                w2_quantize_at[LEADING + tick - E] = tick + 1
-            copy_y()
+        for tick in range(E):
+            interleave_w1(tick)
+            for u in range(LEADING):
+                if W2_BEHIND[u] == tick:
+                    interleave_w2(W2_UNITS[u][0])
+                    interleave_w2(W2_UNITS[u][0] + 2)
             if tick == 0:
                 quantize_head(0)
                 quantize_head(1)
             if tick == 1:
                 quantize_head(2)
-            if 0 <= tick - LAG < E:
+            if tick >= LAG:
                 quantize_shared(tick - LAG)
-                due.append(tick - LAG)
-            for u in range(len(W2_UNITS)):
-                if w2_quantize_at.get(u) == tick:
-                    quantize_w2(u)
-            if tick < E:
-                quantize_w1(tick)
-                first_layer(tick)
-            for e in list(due):
-                if unit_of[e] in w2_codes:
-                    second_layer(e)
-                    due.remove(e)
+            for u in range(LEADING):
+                if W2_BEHIND[u] + 1 == tick:
+                    quantize_w2(W2_UNITS[u][0])
+                    quantize_w2(W2_UNITS[u][0] + 2)
+            quantize_w1(tick)
+            first_layer(tick)
+            for u in range(LEADING):
+                first = W2_UNITS[u][0]
+                if tick == max(first + 3 + LAG, W2_BEHIND[u] + 1):
+                    for e in range(first, first + 4):
+                        second_layer(e)
+                    copy_y(first)
             if tick == E - 2:
                 interleave_last_on_scalar()
-            if tick < E:
-                gelu_and_gather(tick)
+            if tick == E - 1:
+                interleave_w2(10)
+            gelu_and_gather(tick)
 
-        copy_y()
+        interleave_w2(8)
+        quantize_shared(13)
+        interleave_w2(11)
+        quantize_w2(8)
+        for e in (8, 9):
+            second_layer(e)
+        quantize_shared(14)
+        interleave_w2(12)
+        interleave_w2(13)
+        interleave_w2(14)
+        quantize_w2(10)
+        quantize_w2(11)
+        for e in (10, 11):
+            second_layer(e)
+        copy_y(8)
+        quantize_shared(15)
+        quantize_w2(12)
+        quantize_w2(13)
+        for e in (12, 13):
+            second_layer(e)
+        copy_y(12)
+        interleave_w2(15)
+        quantize_w2(14)
+        second_layer(14)
+        copy_y(14)
+        quantize_w2(15)
+        second_layer(15)
+        copy_y(15)
 
-        one = held.tile([P, T], F32, name="one")
-        nc.vector.tensor_tensor(one[:], y_all[:].indirect(pos1_sb[:]), loaded[("gate", 0)][:], MULT)
-        products = []
-        first_token = 0
-        for step in range(len(COMBINE_TOKENS) + 1):
-            if step < len(COMBINE_TOKENS):
-                tokens = slice(first_token, first_token + COMBINE_TOKENS[step])
-                entries = slice(tokens.start // 16, tokens.stop // 16)
-                first_token = tokens.stop
-                two = combine_pool.tile([P, COMBINE_TOKENS[step]], F32, name="two")
-                nc.vector.tensor_tensor(two[:], y_all[:].indirect(pos2_sb[:, entries]), loaded[("gate", step + 1)][:], MULT)
-                products.append((two, tokens))
-            if step >= 1:
-                two, tokens = products[step - 1]
-                total = combine_pool.tile([P, tokens.stop - tokens.start], F32, name="total")
-                nc.vector.tensor_tensor(total[:], one[:, tokens], two[:], ADD)
-                nc.sync.dma_start(out[:, tokens], total[:])
+        products = load_pool.tile([P, 2, T], F32, name="load")
+        totals = load_pool.tile([P, T], F32, name="load")
+
+        def product(pos_sb, piece):
+            row, first, count = piece
+            entries = slice(first // 16, (first + count) // 16)
+            part = products[:, row, first : first + count]
+            nc.vector.tensor_tensor(part, y_all[:].indirect(pos_sb[:, entries]), loaded[("gate", piece)], MULT)
+            return part
+
+        tensor_sum = sums_pool.tile([P, ON_TENSOR], F32, name="sums")
+        for row in range(2):
+            part = product((pos1_sb, pos2_sb)[row], GATE_PIECES[row])
+            nc.tensor.matmul(tensor_sum[:], lhsT=identity[:], rhs=part, start=row == 0, stop=row == 1)
+        nc.scalar.copy(out=totals[:, 0:ON_TENSOR], in_=tensor_sum[:])
+        nc.sync.dma_start(out[:, 0:ON_TENSOR], totals[:, 0:ON_TENSOR])
+
+        product(pos1_sb, GATE_PIECES[2])
+        for i in range(len(STEPS) + 1):
+            if i < len(STEPS):
+                product(pos2_sb, GATE_PIECES[3 + i])
+            if i >= 1:
+                first, count = STEPS[i - 1]
+                tokens = slice(first, first + count)
+                nc.vector.tensor_tensor(totals[:, tokens], products[:, 0, tokens], products[:, 1, tokens], ADD)
+                nc.sync.dma_start(out[:, tokens], totals[:, tokens])

@@ -26,8 +26,8 @@ W2_BEHIND = [3, 6]
 LEADING = len(W2_BEHIND)
 TRAILING = len(W2_UNITS) - LEADING
 W2_PIECES = [(0, 2, True), (2, 2, False), (4, 2, True), (6, 2, False), (8, 2, False), (10, 1, True), (11, 1, False),
-             (12, 1, True), (13, 1, False), (14, 1, True), (15, 1, False)]
-Y_GROUPS = [(0, 4), (4, 4), (8, 4), (12, 2), (14, 1), (15, 1)]
+             (12, 1, True), (13, 1, True), (14, 1, False), (15, 1, False)]
+Y_GROUPS = [(0, 4), (4, 4), (8, 4), (12, 1), (13, 1), (14, 1), (15, 1)]
 
 AHEAD = 4
 LAG = 3
@@ -37,10 +37,10 @@ X_LOADS = 2
 W1_IN_PAIRS = [0, 2]
 LOAD_BUFS = 5
 BY_SCALAR_BUFS = 8
-BY_VECTOR_BUFS = 20
+BY_VECTOR_BUFS = 22
 W1_CODE_BUFS = 4
-CODE_BUFS = 12
-W2_CODE_BUFS = 11
+CODE_BUFS = 10
+W2_CODE_BUFS = 8
 SUMS_BANKS = 8
 GATE_PIECES = [(0, 0, 320), (1, 0, 320), (0, 320, 704), (1, 320, 384), (1, 704, 192), (1, 896, 128)]
 ON_TENSOR = 320
@@ -315,22 +315,23 @@ def tile_routed_moe_kernel(tc, xT, w1, w2, gate, offs, pos1, pos2, out):
         quantize_shared(14)
         interleave_w2(12)
         interleave_w2(13)
-        interleave_w2(14)
         quantize_w2(10)
         quantize_w2(11)
         for e in (10, 11):
             second_layer(e)
         copy_y(8)
         quantize_shared(15)
+        interleave_w2(14)
         quantize_w2(12)
-        quantize_w2(13)
-        for e in (12, 13):
-            second_layer(e)
+        second_layer(12)
         copy_y(12)
         interleave_w2(15)
         quantize_w2(14)
         second_layer(14)
         copy_y(14)
+        quantize_w2(13)
+        second_layer(13)
+        copy_y(13)
         quantize_w2(15)
         second_layer(15)
         copy_y(15)

@@ -22,7 +22,7 @@ FLOPS = 2 * SLOTS * K * H + 2 * SLOTS * H * N
 
 
 W2_UNITS = [(0, 4), (4, 4), (8, 2), (10, 2), (12, 2), (14, 1), (15, 1)]
-W2_BEHIND = [3, 6]
+W2_BEHIND = [6, 7]
 LEADING = len(W2_BEHIND)
 TRAILING = len(W2_UNITS) - LEADING
 W2_PIECES = [(0, 2, True), (2, 2, False), (4, 2, True), (6, 2, False), (8, 2, False), (10, 1, True), (11, 1, False),

@@ -42,9 +42,9 @@ W1_CODE_BUFS = 4
 CODE_BUFS = 10
 W2_CODE_BUFS = 8
 SUMS_BANKS = 8
-GATE_PIECES = [(0, 0, 320), (1, 0, 320), (0, 320, 704), (1, 320, 384), (1, 704, 192), (1, 896, 128)]
-ON_TENSOR = 320
-STEPS = [(320, 384), (704, 192), (896, 128)]
+GATE_PIECES = [(0, 0, 256), (1, 0, 256), (0, 256, 768), (1, 256, 448), (1, 704, 192), (1, 896, 128)]
+ON_TENSOR = 256
+STEPS = [(256, 448), (704, 192), (896, 128)]
 
 
 def tile_routed_moe_kernel(tc, xT, w1, w2, gate, offs, pos1, pos2, out):

from contextlib import ExitStack

import concourse.mybir as mybir
from concourse.masks import make_identity

F32 = mybir.dt.float32
BF16 = mybir.dt.bfloat16
U32 = mybir.dt.uint32
U16 = mybir.dt.uint16
U8 = mybir.dt.uint8
FP8X4 = mybir.dt.float8_e4m3fn_x4
GELU = mybir.ActivationFunctionType.Gelu_apprx_tanh
COPY = mybir.ActivationFunctionType.Copy
MULT = mybir.AluOpType.mult
ADD = mybir.AluOpType.add

P = 128
PACK = 4
K, T, E, C, H, N = 512, 1024, 16, 128, 512, 128
SLOTS = E * C
FLOPS = 2 * SLOTS * K * H + 2 * SLOTS * H * N


W2_UNITS = [(0, 4), (4, 4), (8, 2), (10, 2), (12, 2), (14, 1), (15, 1)]
W2_BEHIND = [6, 7]
LEADING = len(W2_BEHIND)
TRAILING = len(W2_UNITS) - LEADING
W2_PIECES = [(0, 2, True), (2, 2, False), (4, 2, True), (6, 2, False), (8, 2, False), (10, 1, True), (11, 1, False),
             (12, 1, True), (13, 1, True), (14, 1, False), (15, 1, False)]
Y_GROUPS = [(0, 4), (4, 4), (8, 4), (12, 1), (13, 1), (14, 1), (15, 1)]

AHEAD = 4
LAG = 3
HEAD_TILES = [(0,), (1,), (2, 3)]

X_LOADS = 2
W1_IN_PAIRS = [0, 2]
LOAD_BUFS = 5
BY_SCALAR_BUFS = 8
BY_VECTOR_BUFS = 22
W1_CODE_BUFS = 4
CODE_BUFS = 10
W2_CODE_BUFS = 8
SUMS_BANKS = 8
GATE_PIECES = [(0, 0, 256), (1, 0, 256), (0, 256, 768), (1, 256, 448), (1, 704, 192), (1, 896, 128)]
ON_TENSOR = 256
STEPS = [(256, 448), (704, 192), (896, 128)]


def tile_routed_moe_kernel(tc, xT, w1, w2, gate, offs, pos1, pos2, out):
    nc = tc.nc
    with ExitStack() as ctx:
        lists = ctx.enter_context(tc.tile_pool(name="lists", bufs=1))
        held = ctx.enter_context(tc.tile_pool(name="held", bufs=1))
        wide_pool = ctx.enter_context(tc.tile_pool(name="wide_pool", bufs=3))
        load_pool = ctx.enter_context(tc.tile_pool(name="load_pool", bufs=LOAD_BUFS))
        by_scalar_pool = ctx.enter_context(tc.tile_pool(name="by_scalar_pool", bufs=BY_SCALAR_BUFS))
        by_vector_pool = ctx.enter_context(tc.tile_pool(name="by_vector_pool", bufs=BY_VECTOR_BUFS))
        w1_code_pool = ctx.enter_context(tc.tile_pool(name="w1_code_pool", bufs=W1_CODE_BUFS))
        code_pool = ctx.enter_context(tc.tile_pool(name="code_pool", bufs=CODE_BUFS))
        w2_code_pool = ctx.enter_context(tc.tile_pool(name="w2_code_pool", bufs=W2_CODE_BUFS))
        sums_pool = ctx.enter_context(tc.psum_pool(name="sums_pool", bufs=SUMS_BANKS))

        zero = held.tile([P, 1], F32, name="zero")
        unused = held.tile([P, 1], F32, name="unused")
        nc.vector.memset(zero[:], 0.0)
        nc.scalar.activation(out=unused[:], in_=zero[:], func=GELU)

        identity = held.tile([P, P], F32, name="identity")
        make_identity(nc, identity[:])

        offs_sb = lists.tile([P, SLOTS // 16], U16, name="offs_sb")
        nc.sync.dma_start(offs_sb[:], offs)
        pos1_sb = lists.tile([P, T // 16], U16, name="pos1_sb")
        pos2_sb = lists.tile([P, T // 16], U16, name="pos2_sb")

        rows_of_plane = xT.rearrange("(p j) n -> p j n", j=PACK)
        planes = []
        planes_bf16 = []
        all_planes = wide_pool.tile([P, PACK, T], F32, name="wide")
        for part in range(X_LOADS):
            rows = slice(part * PACK // X_LOADS, (part + 1) * PACK // X_LOADS)
            nc.sync.dma_start(all_planes[:, rows, :], rows_of_plane[:, rows, :])
        for j in range(PACK):
            planes.append(all_planes[:, j, :])
        for j in range(PACK):
            plane_bf16 = held.tile([P, T], BF16, name="plane_bf16_%d" % j)
            nc.vector.tensor_copy(out=plane_bf16[:], in_=planes[j])
            planes_bf16.append(plane_bf16)

        y_all = held.tile([P, SLOTS], F32, name="y_all")

        unit_of = {}
        for u in range(len(W2_UNITS)):
            for a in range(W2_UNITS[u][1]):
                unit_of[W2_UNITS[u][0] + a] = u
        stream = []
        for e in range(E):
            stream.append(("w1", e))
            for u in range(LEADING):
                if W2_BEHIND[u] == e:
                    stream.append(("w2", u))
        for u in range(LEADING, len(W2_UNITS)):
            stream.append(("w2", u))
        stream.append(("lists", 0))
        for piece in GATE_PIECES:
            stream.append(("gate", piece))
        loaded = {}
        for what, index in stream:
            if what == "lists":
                nc.sync.dma_start(pos1_sb[:], pos1)
                nc.sync.dma_start(pos2_sb[:], pos2)
            elif what == "w1":
                if index in W1_IN_PAIRS:
                    two = wide_pool.tile([P, 2, PACK * H], F32, name="wide")
                    nc.sync.dma_start(two[:], w1[index : index + 2].rearrange("e (p j) i -> p e (j i)", j=PACK))
                    for a in range(2):
                        loaded[(what, index + a)] = two[:, a, :].rearrange("p (j i) -> p j i", j=PACK)
                elif index - 1 not in W1_IN_PAIRS:
                    one = load_pool.tile([P, PACK, H], F32, name="load")
                    nc.sync.dma_start(one[:], w1[index].rearrange("(p j) i -> p j i", j=PACK))
                    loaded[(what, index)] = one[:]
            elif what == "w2":
                first, count = W2_UNITS[index]
                loaded[(what, index)] = load_pool.tile([P, count, PACK * N], F32, name="load")
                nc.sync.dma_start(
                    loaded[(what, index)][:], w2[first : first + count].rearrange("e (p j) n -> p e (j n)", j=PACK)
                )
            else:
                row, first, count = index
                if index == GATE_PIECES[0]:
                    gates = load_pool.tile([P, 2, T], F32, name="load")
                loaded[(what, index)] = gates[:, row, first : first + count]
                nc.sync.dma_start(loaded[(what, index)], gate[row][:, first : first + count])

        shared_bf16 = {}
        token_codes, token_scales = {}, {}
        w1_bf16, w1_codes, w1_scales, w1_halves = {}, {}, {}, {}
        w2_bf16, w2_codes, w2_scales = {}, {}, {}
        first_sums, hidden_codes, hidden_scales = {}, {}, {}
        group_of, group_sums, piece_of = {}, {}, {}
        for first, count, on_scalar in W2_PIECES:
            piece_of[first] = (count, on_scalar)
        for first, count in Y_GROUPS:
            for a in range(count):
                group_of[first + a] = (first, count)

        def gather_plane(dst, e, j):
            entries = offs_sb[:, e * (C // 16) : (e + 1) * (C // 16)]
            nc.scalar.activation(out=dst[:, :, j], in_=planes_bf16[j][:].indirect(entries), func=COPY)

        def quantize(source, width):
            codes = code_pool.tile([P, width], U32, name="codes", align_bytes=64)
            scales = by_vector_pool.tile([P, width], U8, name="by_vector", align_bytes=64)
            nc.vector.quantize_mx(out=codes[:].bitcast(FP8X4), scales=scales[:], in_=source)
            return codes, scales

        def quantize_head(i):
            experts = HEAD_TILES[i]
            codes, scales = quantize(shared_bf16[("head", i)][:].rearrange("p e s j -> p (e s j)"), C * len(experts))
            for a in range(len(experts)):
                token_codes[experts[a]] = codes[:, a * C : (a + 1) * C]
                token_scales[experts[a]] = scales[:, a * C : (a + 1) * C]

        def gelu_and_gather(e):
            count = 2 if e + AHEAD < E else 1
            tile = by_scalar_pool.tile([P, count, C, PACK], BF16, name="by_scalar", align_bytes=64)
            nc.scalar.activation(out=tile[:, 0, :, :], in_=first_sums[e][:].rearrange("p t s -> p s t"), func=GELU)
            if count == 2:
                for j in range(PACK):
                    gather_plane(tile[:, 1, :, :], e + AHEAD, j)
            shared_bf16[e] = tile

        def quantize_shared(e):
            count = 2 if e + AHEAD < E else 1
            codes, scales = quantize(shared_bf16[e][:].rearrange("p e s j -> p (e s j)"), C * count)
            hidden_codes[e], hidden_scales[e] = codes[:, 0:C], scales[:, 0:C]
            if count == 2:
                token_codes[e + AHEAD], token_scales[e + AHEAD] = codes[:, C : 2 * C], scales[:, C : 2 * C]

        def interleave_w1(e):
            src = loaded[("w1", e)].rearrange("p j (m t) -> p m j t", t=4)
            if e == E - 1:
                w1_halves[0] = by_vector_pool.tile([P, PACK * H // 2], BF16, name="by_vector", align_bytes=64)
                nc.vector.tensor_copy(
                    out=w1_halves[0][:].rearrange("p (t m j) -> p m j t", t=2, j=PACK), in_=src[:, :, :, 0:2]
                )
                return
            w1_bf16[e] = by_vector_pool.tile([P, PACK * H], BF16, name="by_vector", align_bytes=64)
            nc.vector.tensor_copy(out=w1_bf16[e][:].rearrange("p (t m j) -> p m j t", t=4, j=PACK), in_=src)

        def interleave_last_on_scalar():
            src = loaded[("w1", E - 1)].rearrange("p j (m t) -> p m j t", t=4)
            w1_halves[1] = by_scalar_pool.tile([P, PACK * H // 2], BF16, name="by_scalar", align_bytes=64)
            nc.scalar.copy(out=w1_halves[1][:].rearrange("p (t m j) -> p m j t", t=2, j=PACK), in_=src[:, :, :, 2:4])

        def quantize_w1(e):
            w1_codes[e] = w1_code_pool.tile([P, H], U32, name="w1_codes", align_bytes=64)
            w1_scales[e] = by_vector_pool.tile([P, H], U8, name="by_vector", align_bytes=64)
            pieces = 2 if e == E - 1 else 1
            width = H // pieces
            for piece in range(pieces):
                columns = slice(piece * width, (piece + 1) * width)
                nc.vector.quantize_mx(
                    out=w1_codes[e][:, columns].bitcast(FP8X4),
                    scales=w1_scales[e][:, columns],
                    in_=w1_halves[piece][:] if e == E - 1 else w1_bf16[e][:],
                )

        def interleave_w2(first):
            count, on_scalar = piece_of[first]
            u = unit_of[first]
            a = first - W2_UNITS[u][0]
            pool, name, copy = (
                (by_scalar_pool, "by_scalar", nc.scalar.copy) if on_scalar else (by_vector_pool, "by_vector", nc.vector.tensor_copy)
            )
            w2_bf16[first] = pool.tile([P, count, N, PACK], BF16, name=name, align_bytes=64)
            copy(
                out=w2_bf16[first][:].rearrange("p a (n i) j -> p a n j i", i=4),
                in_=loaded[("w2", u)][:, a : a + count, :].rearrange("p a (j n i) -> p a n j i", j=PACK, i=4),
            )

        def quantize_w2(first):
            count = piece_of[first][0]
            codes = w2_code_pool.tile([P, count * N], U32, name="w2_codes", align_bytes=64)
            scales = by_vector_pool.tile([P, count * N], U8, name="by_vector", align_bytes=64)
            nc.vector.quantize_mx(
                out=codes[:].bitcast(FP8X4), scales=scales[:], in_=w2_bf16[first][:].rearrange("p a n j -> p (a n j)")
            )
            for a in range(count):
                w2_codes[first + a] = codes[:, a * N : (a + 1) * N]
                w2_scales[first + a] = scales[:, a * N : (a + 1) * N]

        def first_layer(e):
            first_sums[e] = sums_pool.tile([P, 4, C], F32, name="sums")
            for t in range(4):
                nc.tensor.matmul_mx(
                    out=first_sums[e][:, t, :],
                    lhsT=w1_codes[e][:, t * P : (t + 1) * P].bitcast(FP8X4),
                    lhsT_scale=w1_scales[e][:, t * P : (t + 1) * P],
                    rhs=token_codes[e].bitcast(FP8X4),
                    rhs_scale=token_scales[e],
                    start=True,
                    stop=True,
                )

        def second_layer(e):
            first, count = group_of[e]
            if e == first:
                group_sums[first] = sums_pool.tile([P, count, C], F32, name="sums")
            nc.tensor.matmul_mx(
                out=group_sums[first][:, e - first, :],
                lhsT=w2_codes[e].bitcast(FP8X4),
                lhsT_scale=w2_scales[e],
                rhs=hidden_codes[e].bitcast(FP8X4),
                rhs_scale=hidden_scales[e],
                start=True,
                stop=True,
            )

        def copy_y(first):
            count = group_of[first][1]
            copy = nc.scalar.copy
            copy(
                out=y_all[:, first * C : (first + count) * C], in_=group_sums[first][:].rearrange("p a s -> p (a s)")
            )

        for i in range(len(HEAD_TILES)):
            shared_bf16[("head", i)] = by_scalar_pool.tile(
                [P, len(HEAD_TILES[i]), C, PACK], BF16, name="by_scalar", align_bytes=64
            )
        for part in range(2):
            for i in range(len(HEAD_TILES)):
                for a in range(len(HEAD_TILES[i])):
                    for j in (2 * part, 2 * part + 1):
                        gather_plane(shared_bf16[("head", i)][:, a, :, :], HEAD_TILES[i][a], j)

        for tick in range(E):
            interleave_w1(tick)
            for u in range(LEADING):
                if W2_BEHIND[u] == tick:
                    interleave_w2(W2_UNITS[u][0])
                    interleave_w2(W2_UNITS[u][0] + 2)
            if tick == 0:
                quantize_head(0)
                quantize_head(1)
            if tick == 1:
                quantize_head(2)
            if tick >= LAG:
                quantize_shared(tick - LAG)
            for u in range(LEADING):
                if W2_BEHIND[u] + 1 == tick:
                    quantize_w2(W2_UNITS[u][0])
                    quantize_w2(W2_UNITS[u][0] + 2)
            quantize_w1(tick)
            first_layer(tick)
            for u in range(LEADING):
                first = W2_UNITS[u][0]
                if tick == max(first + 3 + LAG, W2_BEHIND[u] + 1):
                    for e in range(first, first + 4):
                        second_layer(e)
                    copy_y(first)
            if tick == E - 2:
                interleave_last_on_scalar()
            if tick == E - 1:
                interleave_w2(10)
            gelu_and_gather(tick)

        interleave_w2(8)
        quantize_shared(13)
        interleave_w2(11)
        quantize_w2(8)
        for e in (8, 9):
            second_layer(e)
        quantize_shared(14)
        interleave_w2(12)
        interleave_w2(13)
        quantize_w2(10)
        quantize_w2(11)
        for e in (10, 11):
            second_layer(e)
        copy_y(8)
        quantize_shared(15)
        interleave_w2(14)
        quantize_w2(12)
        second_layer(12)
        copy_y(12)
        interleave_w2(15)
        quantize_w2(14)
        second_layer(14)
        copy_y(14)
        quantize_w2(13)
        second_layer(13)
        copy_y(13)
        quantize_w2(15)
        second_layer(15)
        copy_y(15)

        products = load_pool.tile([P, 2, T], F32, name="load")
        totals = load_pool.tile([P, T], F32, name="load")

        def product(pos_sb, piece):
            row, first, count = piece
            entries = slice(first // 16, (first + count) // 16)
            part = products[:, row, first : first + count]
            nc.vector.tensor_tensor(part, y_all[:].indirect(pos_sb[:, entries]), loaded[("gate", piece)], MULT)
            return part

        tensor_sum = sums_pool.tile([P, ON_TENSOR], F32, name="sums")
        for row in range(2):
            part = product((pos1_sb, pos2_sb)[row], GATE_PIECES[row])
            nc.tensor.matmul(tensor_sum[:], lhsT=identity[:], rhs=part, start=row == 0, stop=row == 1)
        nc.scalar.copy(out=totals[:, 0:ON_TENSOR], in_=tensor_sum[:])
        nc.sync.dma_start(out[:, 0:ON_TENSOR], totals[:, 0:ON_TENSOR])

        product(pos1_sb, GATE_PIECES[2])
        for i in range(len(STEPS) + 1):
            if i < len(STEPS):
                product(pos2_sb, GATE_PIECES[3 + i])
            if i >= 1:
                first, count = STEPS[i - 1]
                tokens = slice(first, first + count)
                nc.vector.tensor_tensor(totals[:, tokens], products[:, 0, tokens], products[:, 1, tokens], ADD)
                nc.sync.dma_start(out[:, tokens], totals[:, tokens])
